import numpy as np, ml_dtypes
CORES = [23,119,17,113]
N = 4
BF = ml_dtypes.bfloat16
def gentries(a):
    return np.ascontiguousarray(a.reshape(8, 16, -1).transpose(0, 2, 1)).reshape(8, -1)
def gtable(e):
    e = np.asarray(e); return np.ascontiguousarray(e.reshape(8, -1, 16).transpose(0, 2, 1)).reshape(128, -1).astype(np.int32)
W, C, PB, R, INC, RO = 4096, 3, 256, 16, 64, 8
V = C * PB
TOP = 4080
def procs():
    return np.ascontiguousarray(np.broadcast_to(np.arange(V).reshape(C, 1, PB), (C, R, PB))).reshape(-1)
def rows():
    return np.ascontiguousarray(np.broadcast_to(np.arange(R).reshape(1, R, 1), (C, R, PB))).reshape(-1)
def owners(rng, E, share, rich):
    P = procs(); O = rng.integers(0, V, (N, 2, 8, W))
    for q in range(N):
        for g in range(8):
            e = E[q, g].reshape(-1); w = rng.random(V) < rich
            for s in range(2):
                p = rng.permutation(R * V); o = O[q, s, g].copy(); o[e[p]] = P[p]
                o = np.where(rng.random(W) < share[q, g], o, O[q, s, g])
                i = np.nonzero(w[P] & (P % 2 == s))[0]; o[e[i]] = P[i]
                O[q, s, g] = o
    return O
def parts(rng):
    M = rng.integers(0, 256, (N, 8, 16, W)); Z = rng.integers(0, 256, (N, 8, 16, V)); K = rng.integers(0, W, (N, 8, W)); E = rng.integers(0, W, (N, 8, C, R, PB))
    O = owners(rng, E, rng.choice(np.array([0.25, 0.5, 0.75, 0.95]), (N, 8)), 0.06); T = rng.integers(500, 1500, (N, 8, V))
    return M, K, O, E, Z, T
def least(M, O, E, Z):
    P = procs(); out = np.zeros((N, 8, V), np.int64)
    for q in range(N):
        for g in range(8):
            e = E[q, g].reshape(-1); y = M[q, g][:, e].reshape(16, C, R, PB)
            d = np.add.reduce(np.abs(y - Z[q, g].reshape(16, C, 1, PB)), axis=0)
            live = ((O[q, 0, g][e] == P) | (O[q, 1, g][e] == P)).reshape(C, R, PB)
            out[q, g] = np.min(np.where(live, d, TOP), axis=1).reshape(V)
    return out
def pack(M, K, O, E, Z, T):
    return {"msg": np.ascontiguousarray(M.reshape(N, 128, W)).astype(np.float32).astype(BF), "enc": K.astype(np.int32), "own": np.ascontiguousarray(O.reshape(N, 16, W)).astype(np.int32),
            "ends": np.stack([gtable(a.reshape(8, -1)) for a in E]), "st": np.ascontiguousarray(Z.reshape(N, 128, V)).astype(np.float32).astype(BF), "th": T.astype(np.int32)}
def setup_inputs(rng):
    return pack(*parts(rng))
def setup_inputs_corners(rng):
    M, K, O, E, Z, T = parts(rng); P = procs(); k = rows(); ee = np.arange(W); c = W // V
    x = rng.random(K.shape); K = np.where(x < 0.2, ee, np.where(x < 0.35, 0, np.where(x < 0.5, W - 1, np.where(x < 0.8, (ee + 1) % W, K))))
    for q in range(N):
        for g in range(8):
            w = (q + g) % 4
            if w == 0:
                x = rng.random(W); O[q, 0, g] = np.where(x < 0.1, 0, np.where(x < 0.2, V - 1, O[q, 0, g])); O[q, 1, g] = np.where(x > 0.85, O[q, 0, g], O[q, 1, g])
                continue
            O[q, :, g, :c * V] = np.tile(np.arange(V), c)
            mine = P + V * rng.integers(0, c, P.shape); other = (P + rng.integers(1, V, P.shape)) % V + V * rng.integers(0, c, P.shape)
            pos = rng.choice(np.array([0, R - 1, int(rng.integers(0, R))]), V)[P]; full = (rng.random(V) < 0.5)[P]
            hit = full if w == 1 else (k == pos if w == 2 else k != pos)
            E[q, g] = np.where(hit, mine, other).reshape(C, R, PB)
            if w == 1 and g >= 4:
                M[q, g] = 160 + ((M[q, g] * 3) >> 3); Z[q, g] = Z[q, g] >> 3
    low = least(M, O, E, Z); x = rng.integers(0, 5, T.shape)
    T = np.where(x == 0, low, np.where(x == 1, np.minimum(low + 1, TOP), np.where(x == 2, 0, np.where(x == 3, TOP, T))))
    for q in range(N):
        g = 4 + (1 - q) % 4; T[q, g] = low[q, g] + rng.integers(0, 2, V) - INC
    return pack(M, K, O, E, Z, T)
def setup_inputs_crowd(rng):
    M, K, O, E, Z, T = parts(rng); P = procs(); k = rows(); O = rng.integers(0, V, O.shape); a = np.arange(V); u = a - a % 2
    for q in range(N):
        for g in range(8):
            w = g % 4; e = E[q, g].reshape(-1).copy(); pos = rng.integers(0, R, V); hit = k == pos[P]; one = (0, W - 1, int(rng.integers(0, W)))[(q + g // 4) % 3]
            T[q, g] = TOP
            if w == 2:
                e[hit] = u[P[hit]]; O[q, 0, g, :V] = u; O[q, 1, g, :V] = u + 1; K[q, g] = rng.choice(np.array([0, W - 1, W // 2]), W)
            elif w == 3:
                m = rng.random(e.shape) < 0.5; e = np.where(m, rng.choice(np.array([V, V + 1, W - 1]), e.shape), e)
                e[hit] = P[hit]; O[q, 0, g] = (0, V - 1)[(q + g // 4) % 2]; O[q, 1, g, :V] = a; T[q, g] = TOP * rng.integers(0, 2, V)
            else:
                e[hit] = P[hit]; O[q, 0, g, :V] = a; K[q, g] = one
                if w == 1:
                    for b in range(C): T[q, g, b * PB + (0 if g == 1 else int(rng.integers(0, PB)))] = 0
            E[q, g] = e.reshape(C, R, PB)
    return pack(M, K, O, E, Z, T)
def setup_inputs_ends(rng):
    x = rng.random((N, 8, 1, W)); M = np.where(x < 0.4, 255, np.where(x < 0.8, 0, 255 * rng.integers(0, 2, (N, 8, 16, W))))
    x = rng.random((N, 8, 1, V)); Z = np.where(x < 0.35, 255, np.where(x < 0.7, 0, 255 * rng.integers(0, 2, (N, 8, 16, V))))
    E = rng.integers(0, W, (N, 8, C, R, PB)); E = np.where(rng.random(E.shape) < 0.68, (W - 1) * rng.integers(0, 2, E.shape), E)
    O = owners(rng, E, np.ones((N, 8)), 0.0); O = np.where(rng.random(O.shape) < 0.65, (V - 1) * rng.integers(0, 2, O.shape), O)
    K = rng.integers(0, W, (N, 8, W)); K = np.where(rng.random(K.shape) < 0.7, (W - 1) * rng.integers(0, 2, K.shape), K)
    T = TOP * rng.integers(0, 2, (N, 8, V))
    T[:, 7, :V - PB] = 0; T[:, 7, V - 1] = TOP
    M[:, 7, :, W - 1] = 255; M[:, 7, :, 0] = 0; Z[:, 7, :, V - 1] = 0
    O[:, 0, 7, W - 1] = 0; O[:, 1, 7, W - 1] = V - 1; O[:, 0, 7, 0] = V - 1; O[:, 1, 7, 0] = 0
    k = np.arange(R); both = np.where((k % 2 == 1) | (k == R - 2), W - 1, 0)
    for q in range(N): E[q, 7, C - 1, :, PB - 1] = both if (N - 1 - q) % 2 == 0 else W - 1
    T[:, 6] = 0; T[:, 6, 0] = TOP
    M[:, 6, :, W - 1] = 255; M[:, 6, :, 0] = 0; Z[:, 6, :, 0] = 0; Z[:, 6, :, 1] = 0
    O[:, 0, 6, W - 1] = V - 1; O[:, 1, 6, W - 1] = 0; E[:, 6, 0, :, 0] = W - 1
    O[:, 0, 6, 0] = 1; E[:, 6, 0, :, 1] = 0; E[:, 6, 0, R - 1, 1] = W - 1
    return pack(M, K, O, E, Z, T)
def setup_inputs_spread(rng):
    M, K, O, E, Z, T = parts(rng)
    M = np.minimum((np.exp2(8.5 * rng.random((N, 8, 1, W))) * rng.random(M.shape)).astype(np.int64), 255)
    Z = np.minimum((np.exp2(8.5 * rng.random((N, 8, 1, V))) * rng.random(Z.shape)).astype(np.int64), 255)
    K = np.minimum((W * rng.random(K.shape) ** 3).astype(np.int64), W - 1); E = np.minimum((W * rng.random(E.shape) ** 2).astype(np.int64), W - 1)
    O = owners(rng, E, rng.choice(np.array([0.5, 0.8, 1.0]), (N, 8)), 0.03)
    O = np.where(rng.random(O.shape) < 0.15, np.minimum((V * rng.random(O.shape) ** 3).astype(np.int64), V - 1), O)
    T = np.minimum(np.exp2(12 * rng.random(T.shape)).astype(np.int64) - 1, TOP)
    return pack(M, K, O, E, Z, T)
def setup_inputs_ties(rng):
    M, K, O, E, Z, T = parts(rng); base = rng.integers(0, 3, (N, 8, 16, W)); top = (np.arange(8) % 2).reshape(1, 8, 1, 1)
    for q in range(N):
        for g in range(8):
            M[q, g] = base[q, g][:, rng.integers(0, 24, W)]
            z = M[q, g][:, rng.integers(0, W, V)]; Z[q, g] = np.where(rng.random(V) < 0.5, z, rng.integers(0, 3, (16, V)))
    E[:, ::3, :, 1::2] = E[:, ::3, :, 0::2]
    O = owners(rng, E, rng.choice(np.array([0.6, 0.9]), (N, 8)), 0.05)
    M = np.where(top == 1, 255 - M, M); Z = np.where(top == 1, 255 - Z, Z); T = rng.integers(0, 24, T.shape)
    T = np.where(rng.random(T.shape) < 0.2, rng.integers(0, 2, T.shape), T)
    return pack(M, K, O, E, Z, T)
def check_inputs(d):
    bad = []
    for k, hi in (("msg", 255), ("enc", W - 1), ("own", V - 1), ("ends", W - 1), ("st", 255), ("th", TOP)):
        a = np.asarray(d[k]).astype(np.float64)
        if not (np.min(a) >= 0 and np.max(a) <= hi): bad.append("range of " + k)
        elif np.any(a != np.floor(a)): bad.append("whole numbers of " + k)
    return bad
def first(name, ok):
    qi = np.arange(N)[:, None, None]; gi = np.arange(8)[None, :, None]; lane = np.arange(PB)
    low = np.full((N, 8, W), PB, np.int64); np.minimum.at(low, (qi, gi, name), np.where(ok, lane, PB))
    return ok & (low[qi, gi, name] == lane)
def pick(a, k):
    return np.take_along_axis(a, k[:, :, None, :], 2)[:, :, 0]
def reference(msg, enc, own, ends, st, th):
    M = msg.astype(np.float32).astype(np.int64).reshape(N, 8, 16, W); K = enc.astype(np.int64); O = own.astype(np.int64).reshape(N, 2, 8, W)
    E = np.stack([gentries(a) for a in ends]).astype(np.int64).reshape(N, 8, C, R, PB)
    Z = st.astype(np.float32).astype(np.int64).reshape(N, 8, 16, V); T = th.astype(np.int64)
    qi = np.arange(N)[:, None, None]; gi = np.arange(8)[None, :, None]; lane = np.arange(PB); far = 2 ** 20
    for t in range(RO):
        b = t % C; lo = b * PB; v = lo + lane
        e = E[:, :, b].copy(); z = Z[..., lo:lo + PB].copy(); flat = e.reshape(N, 8, R * PB)
        y = np.take_along_axis(M, flat[:, :, None, :], 3).reshape(N, 8, 16, R, PB)
        d = np.add.reduce(np.abs(y - z[:, :, :, None, :]), axis=2)
        o0 = np.take_along_axis(O[:, 0], flat, 2).reshape(e.shape); o1 = np.take_along_axis(O[:, 1], flat, 2).reshape(e.shape)
        live = (o0 == v) | (o1 == v); stale = np.logical_not(live); has = np.any(stale, axis=2)
        dl = np.where(live, d, far); f = np.argmin(dl, axis=2); fire = np.min(dl, axis=2) < T[..., lo:lo + PB]
        m = np.argmax(np.where(live, d, -1), axis=2); s = np.argmin(np.where(stale, d, far), axis=2); j = np.where(has, np.argmax(stale, axis=2), f)
        ef = pick(e, f); em = pick(e, m); es = pick(e, s)
        yf = np.take_along_axis(M, ef[:, :, None, :], 3); ys = np.take_along_axis(M, es[:, :, None, :], 3)
        c = np.take_along_axis(K, ef, 2); hop = np.take_along_axis(O[:, 0], es, 2); hint = E[qi, gi, hop // PB, s, hop % PB]
        fb = fire[:, :, None, :]; hb = has[:, :, None, :]
        zn = np.where(fb, np.abs(z - yf), np.where(hb, (z + ys) >> 1, z))
        E[qi, gi, b, np.where(fire, j, s), lane] = np.where(fire, c, np.where(has, hint, es))
        Z[..., lo:lo + PB] = zn; T[..., lo:lo + PB] += np.where(fire, 0, INC)
        q, g, i = np.nonzero(first(c, fire)); O[q, t & 1, g, c[q, g, i]] = lo + i
        q, g, i = np.nonzero(first(ef, fire)); to = (q + 1 + t % (N - 1)) % N; a = ef[q, g, i]
        M[to, g, :, a] = zn[q, g, :, i]; K[to, g, a] = em[q, g, i]
    return {"ym": M.reshape(N, 128, W).astype(np.float32).astype(BF), "yk": K.astype(np.float32), "yo": O.reshape(N, 16, W).astype(np.float32),
            "ye": np.stack([gtable(a.reshape(8, -1)) for a in E]).astype(np.float32), "yz": Z.reshape(N, 128, V).astype(np.float32).astype(BF), "yt": T.astype(np.float32)}

@@ -1,0 +1,685 @@
+import math
+from concourse.mybir import AluOpType as A, ActivationFunctionType as F
+
+W, V, PB, RO, N = 4096, 768, 256, 8, 4
+CH = [(0, 5), (5, 10), (10, 14), (14, 16)]
+RELU = 1
+OC = [(0, 4), (4, 8), (8, 12), (12, 16)]
+REP = 5
+BIG = float(2 ** 29)
+CYC, PEC, GATH, SCAT, HOP, FAR = 1.04, 0.52, 1.56, 3.8, 60.0, 2200.0
+ROUNDS = 3
+
+
+def _sb(n, d):
+    return ("sbuf", [128, n], d)
+
+
+bf, f32, i32, u16 = "bfloat16", "float32", "int32", "uint16"
+SCRATCH = {
+    "Mw": _sb(8704, bf), "Kw": _sb(8704, bf), "Xw": _sb(4608, bf),
+    "G0": _sb(4608, bf), "G1": _sb(4608, bf), "D0": _sb(4608, bf), "D1": _sb(4608, bf), "AB": _sb(4096, bf),
+    "Z0": _sb(REP * 256, bf), "Z1": _sb(REP * 256, bf), "Z2": _sb(REP * 256, bf),
+    "ELi": _sb(V, i32), "ELf": _sb(V, f32), "ELu": _sb(V, u16), "Et": _sb(256, f32),
+    "cin": _sb(768, i32), "cpi": _sb(1792, i32), "cpb": _sb(2304, bf), "thi": _sb(128, i32), "thf": _sb(128, f32),
+    "PS": _sb(304, f32), "PP": _sb(272, f32), "PK": _sb(816, f32), "SF": _sb(272, f32), "SK": _sb(816, f32),
+    "d0f": _sb(272, f32), "d0k": _sb(816, f32), "prm": _sb(54, u16), "prR": _sb(864, f32),
+    "pr": _sb(512, bf), "lv": _sb(256, bf), "JP": _sb(256, bf), "BY": _sb(144, bf), "NQR": _sb(16, bf),
+    "FW": _sb(1280, bf), "F2": _sb(256, bf), "EQ": _sb(256, bf), "KG": _sb(384, bf), "CR": _sb(384, f32), "E2": _sb(384, bf),
+    "XG": _sb(256, bf), "GS": _sb(256, bf), "DS": _sb(256, f32), "DR": _sb(256, bf), "MK": _sb(256, f32), "HG": _sb(256, f32),
+    "AR": _sb(256, bf),
+    "sz": _sb(RO * 256, bf), "se": _sb(RO * 256, bf), "so": _sb(RO * 16, u16),
+    "lz": _sb(RO * 256, bf), "le": _sb(RO * 256, bf), "lo": _sb(RO * 16, u16),
+    "si": _sb(RO * 192, i32), "sf": _sb(RO * 256, f32), "sb": _sb(RO * 64, bf), "su": _sb(RO * 128, u16),
+    "col": _sb(32, f32), "coli": _sb(8, i32), "n143": _sb(144, f32), "one": _sb(144, f32), "nd16": _sb(128, f32),
+    "OH": _sb(32, f32), "BA": _sb(9 * 144, bf), "BF": _sb(144, f32), "RP": _sb(256, bf),
+    "ID": _sb(7 * 128, bf), "IF": _sb(128, f32),
+    "rr": _sb(256, bf), "cc": _sb(256, bf), "kc": _sb(256, bf), "NB": _sb(3 * 512, bf), "NR": _sb(512, bf),
+    "TM": _sb(384, bf), "VP": _sb(768, bf), "stt": _sb(256, f32), "cxi": _sb(24, i32), "cx": _sb(24, u16), "c92": _sb(16, bf),
+    "cs": _sb(16, u16), "oK": _sb(256, f32), "oO": _sb(512, f32), "oT": _sb(128, f32), "TL": _sb(48, f32),
+}
+for _b in range(8):
+    SCRATCH["P%d" % _b] = ("psum", [128, 512], f32)
+SEMAPHORES = ["v", "s", "p", "c", "sent"] + ["az%d" % t for t in range(RO)] + ["ae%d" % t for t in range(RO)] + ["d%d" % t for t in range(40)]
+
+
+def rank_program(g, core, T, topo):
+    rank = T.rank_of(core)
+    if rank is None:
+        return
+    Q = {"v": g.vector, "s": g.scalar, "p": g.tensor, "c": g, "y": g.sync}
+    ops, lastw, readers = [], {}, {}
+    BANKS = ["b%d" % b for b in range(8)]
+    KL, NC = 16 * CH[-1][0], len(CH)
+
+    def add(q, kind, fn, r, w, busy, lat):
+        r, w, me, dep = r.split(), w.split(), len(ops), {}
+        for k in r:
+            for j in lastw.get(k, []):
+                dep[j] = True
+        for k in w:
+            for j in lastw.get(k, []) + readers.get(k, []):
+                same = ops[j]["q"] == q and ops[j]["kind"] == "op" and (q == "p" or k in BANKS or k[0] == "#")
+                dep[j] = dep.get(j, False) or (not same and k[0] != "#")
+        ops.append(dict(q=q, kind=kind, fn=fn, dep=dep, busy=busy, lat=lat))
+        for k in r:
+            readers.setdefault(k, []).append(me)
+        for k in w:
+            lastw[k] = [me]
+            readers[k] = []
+        return me
+
+    def op(q, fn, r, w, busy): add(q, "op", fn, r, w, busy, busy)
+
+    def dma(q, pairs, r, w, behind=0):
+        size = behind + sum(int(math.prod(o.shape)) * (2 if "16" in str(o.dtype) else 4) for o, i in pairs)
+        add(q, "dma", pairs, r, w + " #" + q, 60.0 * len(pairs), 2000.0 + size / 150.0)
+
+    def emit():
+        n = len(ops)
+        gap = lambda j, wait: ops[j]["lat"] + HOP if wait else ops[j]["busy"]
+        rank_, succ = [0.0] * n, [[] for _ in range(n)]
+        for i in range(n):
+            for j, wait in ops[i]["dep"].items():
+                succ[j].append((i, wait))
+        for j in range(n - 1, -1, -1):
+            rank_[j] = max([ops[j]["lat"]] + [gap(j, wait) + rank_[i] for i, wait in succ[j]])
+
+        def place(order, links):
+            at0, lanes = [0.0] * n, {q: [] for q in Q}
+            for i in order:
+                at = max([0.0] + links(i, at0))
+                lane_, pos, busy = lanes[ops[i]["q"]], 0, ops[i]["busy"]
+                for a, b in lane_:
+                    if at + busy <= a:
+                        break
+                    at = max(at, b)
+                    pos += 1
+                lane_.insert(pos, (at, at + busy))
+                at0[i] = at
+            return at0
+
+        def ahead(i, at0): return [at0[j] + gap(j, wait) for j, wait in ops[i]["dep"].items()]
+
+        def behind(j, at0):
+            return [ops[j]["lat"] - ops[j]["busy"]] + [at0[i] + ops[i]["busy"] + gap(j, wait) - ops[j]["busy"] for i, wait in succ[j]]
+
+        order, best = list(range(n)), None
+        for _ in range(ROUNDS):
+            fw = place(order, ahead)
+            span = max(fw[i] + ops[i]["lat"] for i in range(n))
+            if best is None or span < best:
+                best, start = span, fw
+            bw = place(sorted(range(n), key=lambda i: (-fw[i] - ops[i]["busy"], -i)), behind)
+            order = sorted(range(n), key=lambda i: (-bw[i] - ops[i]["busy"], i))
+        cnt, seen, final, tok, nd = {q: 0 for q in Q}, {q: {} for q in Q}, {}, {}, 0
+        for i in sorted(range(n), key=lambda i: (start[i], i)):
+            o = ops[i]
+            q, want = o["q"], {}
+            for j, wait in o["dep"].items():
+                if wait:
+                    want[tok[j][0]] = max(want.get(tok[j][0], 0), tok[j][1])
+            for s, m in want.items():
+                if seen[q].get(s, 0) < m:
+                    Q[q].wait_ge(T.sem[s], m)
+                    seen[q][s] = m
+            if o["kind"] == "op":
+                cnt[q] += 1
+                o["fn"]().then_inc(T.sem[q], 1)
+                tok[i] = (q, cnt[q])
+            elif o["kind"] == "dma":
+                for a, b in o["fn"]:
+                    Q[q].dma_start(a, b).then_inc(T.sem["d%d" % nd], 16)
+                tok[i] = ("d%d" % nd, 16 * len(o["fn"]))
+                nd += 1
+            else:
+                tok[i] = o["fn"]()
+                continue
+            final[tok[i][0]] = tok[i][1]
+        for s, m in final.items():
+            g.wait_ge(T.sem[s], m)
+
+    v, sc, pe = g.vector, g.scalar, g.tensor
+    GATHERS = ("G0_", "G1_", "D0_", "D1_", "se", "GS", "DS", "HG", "PP", "FW", "sz", "KG", "EQ", "E2", "XG")
+
+    def cost(o, a, w, per):
+        if w in ("M", "K Kd", "X Xb"):
+            return 50.0 + a.shape[1] * SCAT * CYC
+        if w.startswith(GATHERS):
+            return 60.0 + o.shape[1] * GATH * CYC
+        if per is None:
+            per = 0.5 if "16" in str(o.dtype) and "16" in str(a.dtype) else 1.0
+        return max(64.0, o.shape[1] * per) * CYC
+
+    def tt(o, a, b, x, r, w):
+        op("v", lambda: v.tensor_tensor(o, a, b, x), r, w, cost(o, b, w, 1.0 if w[:2] in BANKS and w[2] == " " else 2.0))
+
+    def ts(o, a, s1, x, r, w): op("v", lambda: v.tensor_scalar(o, a, s1, None, x), r, w, cost(o, a, w, None))
+    def t2(o, a, s1, s2, x, y, r, w): op("v", lambda: v.tensor_scalar(o, a, s1, s2, x, y), r, w, cost(o, a, w, None))
+    def cp(o, a, r, w): op("v", lambda: v.tensor_copy(o, a), r, w, cost(o, a, w, None))
+    def ms(o, x, w): op("v", lambda: v.memset(o, x), "", w, cost(o, o, "", None))
+    def scan(o, a, b, r, w): op("v", lambda: v.tensor_tensor_scan(o, a, b, 0.0, A.add, A.min), r, w, cost(o, a, w, 1.0))
+
+    def act(o, a, f, r, w, bias=0.0, scale=1.0):
+        op("s", lambda: sc.activation(o, a, f, bias=bias, scale=scale), r, w, cost(o, a, w, 1.0))
+
+    def lin(o, a, r, w, bias=0.0, scale=1.0): act(o, a, F.Identity, r, w, bias, scale)
+
+    def iota(o, pat, base, cm, w, flag=True):
+        busy = 130.0 + 2 * o.shape[1] * CYC
+        if flag:
+            op("c", lambda: g.iota(o, pat, base, cm, allow_small_or_imprecise_dtypes=True), "", w, busy)
+        else:
+            op("c", lambda: g.iota(o, pat, base, cm), "", w, busy)
+
+    def mm(lst, r, w, start=True, stop=True):
+        def fn():
+            ins = None
+            for j, (o, l, x) in enumerate(lst):
+                ins = pe.matmul(o, l, x, start and j == 0, stop and j == len(lst) - 1)
+            return ins
+        op("p", fn, r, w, sum(max(min(64, l.shape[1]), x.shape[1]) * (1 if "16" in str(x.dtype) else 4) * PEC for o, l, x in lst))
+
+    def r2l(o, B, off, X, a, b):
+        return [(o, B[:, off + 15 - r:off + 143 - r], X[:, a + r:b:16]) for r in range(16)]
+
+    P = [T["P%d" % b] for b in range(8)]
+    Gb, Db, Zb = [T.G0, T.G1], [T.D0, T.D1], [T.Z0, T.Z1, T.Z2]
+    def cl(j): return T.col[:, j:j + 1]
+    def oh(q, big=0): return T.OH[:, 16 * big + q:16 * big + q + 1]
+    def st(a, n=16): return T.stt[:, a:a + n]
+    QF, G15, GF, WX, WY, WN, WU, WE, WH, H16, SC0, SC1, TW6, TW3, NQ, G23, N8, N16, JA, JB = range(20)
+    bABS, bREL, bDEL, bX, bY, bN, bU, bE, bH = [144 * j for j in range(9)]
+    I1, I46, ILV, IM, IP, I16, I256 = [T.ID[:, 128 * j:128 * j + 128] for j in range(7)]
+    SDUM, SADD, SZ1, SZ2, SV, STT = 0, 16, 64, 80, 96, 144
+    lane = T.cpb[:, 2048:2304]
+
+    dma("y", [(T.cin[:, 0:256], T.own[0:8, :]), (T.cin[:, 256:512], T.own[8:16, :])], "", "cin")
+    dma("s", [(T.ELi[:, 0:256], T.ends[:, 0:256])], "", "ELi0")
+    dma("s", [(Zb[0][:, 0:256], T.st[:, 0:256])], "", "Z0")
+    dma("y", [(T.Mw[:, 0:W], T.msg[:, :])], "", "M", 2 ** 19)
+    dma("s", [(T.cin[:, 512:768], T.enc[:, :])] + [(T.thi[0:48, 16 * q:16 * q + 16], T.th[q, :]) for q in range(8)], "", "thi cin2")
+    iota(T.coli[:, 0:1], [[0, 1]], 0, 1, "coli", False)
+    iota(lane, [[1, 256]], 0, 0, "cpl")
+    iota(T.n143[:, :], [[1, 144]], 0, 0, "n143")
+    iota(T.one[:, :], [[0, 144]], 1, 0, "one")
+    op("c", lambda: g.affine_select(T.IF[:, :], T.one[:, 0:128], [[-1, 128]], A.is_equal, 0.0, 0, 1), "one", "IF", 440.0)
+    for b in range(3):
+        iota(T.prR[:, 288 * b:288 * b + 272], [[1, 16], [16, 17]], -16, 0, "prR%d" % b)
+        iota(T.prR[:, 288 * b + 272:288 * b + 288], [[0, 16]], 0, 0, "prQ%d" % b)
+    for b in range(3):
+        iota(T.prR[:, 288 * b:288 * b + 272:17], [[1, 16]], 256 + 16 * b, 0, "prR%d" % b)
+    PRR = "prR0 prR1 prR2 prQ0 prQ1 prQ2"
+    iota(T.NB[:, 0:512], [[0, 32], [-16, 16]], 0, 0, "NB0")
+    iota(T.kc[:, :], [[256, 16], [16, 16]], 0, 0, "kc")
+    iota(st(STT, 48), [[0, 3], [16, 16]], -4096, 0, "st4")
+    iota(T.nd16[:, :], [[1, 8], [0, 16]], 0, 0, "nd16")
+    iota(T.rr[:, :], [[0, 16], [1, 16]], 0, 0, "rr")
+    iota(T.cc[:, :], [[1, 16], [0, 16]], 0, 0, "cc")
+    iota(st(SDUM), [[16, 16]], 4352, 0, "st0")
+    iota(st(SADD), [[0, 16]], 0, 0, "st1a")
+    iota(st(SADD + 16), [[32, 16]], 7680, 0, "st1b")
+    iota(st(SADD + 32), [[16, 16]], 3840, 0, "st1c")
+    iota(st(SZ1), [[16, 16]], 4096, 0, "st2a")
+    iota(st(SZ2), [[16, 16]], 4352 - 8192, 0, "st2b")
+    iota(st(SV, 48), [[16, 48]], 0, 0, "st3")
+    iota(T.cxi[:, 0:16], [[1, 16]], 0, 0, "cxi", False)
+    iota(T.cxi[:, 16:24], [[2, 8]], 0, 0, "cxj", False)
+    for b in (1, 2):
+        iota(T.NB[:, 512 * b:512 * b + 512], [[0, 32], [-16, 16]], -256 * b, 0, "NB%d" % b)
+
+    ms(T.Xw[:, :], 0.0, "X Xb")
+    ts(T.coli[:, 1:2], T.coli[:, 0:1], 15, A.bitwise_and, "coli", "coli1")
+    ts(T.coli[:, 2:3], T.coli[:, 0:1], 4, A.arith_shift_right, "coli", "coli2")
+    cp(cl(QF), T.coli[:, 1:2], "coli1", "qf")
+    t2(cl(G15), T.coli[:, 2:3], 16.0, 15.0, A.mult, A.add, "coli2", "g15")
+    lin(T.cpb[:, 1792:2048], lane, "cpl qf", "cph", cl(QF), 0.0)
+    ts(T.cpi[:, 0:256], T.cin[:, 0:256], 15, A.bitwise_and, "cin", "cpi0")
+    t2(T.cpi[:, 256:512], T.cin[:, 0:256], 4, 15, A.arith_shift_right, A.bitwise_and, "cin", "cpi1")
+    ts(T.cpi[:, 512:1024], T.cin[:, 0:512], 8, A.arith_shift_right, "cin", "cpi2")
+    ts(T.cpi[:, 1024:1280], T.cin[:, 256:512], 255, A.bitwise_and, "cin", "cpi3")
+    cp(T.cpb[:, 0:1280], T.cpi[:, 0:1280], "cpi0 cpi1 cpi2 cpi3", "cpb")
+    rows = [(0, 0), (1, 256), (6, 512), (3, 768), (2, 1024), (4, 1792), (5, 2048)]
+    dma("s", [(T.Xw[q::16, 0:W], T.cpb[:, a:a + 256]) for q, a in rows[5:]], "cph cpl", "Xb")
+    dma("y", [(T.Xw[q::16, 0:W], T.cpb[:, a:a + 256]) for q, a in rows[:5]], "cpb", "X", 2 ** 19)
+    dma("y", [(T.Kw[:, 0:W], T.msg[:, :])], "X Xb", "K")
+    dma("y", [(T.ELi[:, 256:V], T.ends[:, 256:V])], "", "ELi1", 2 ** 20)
+    for b in (1, 2):
+        dma("y", [(Zb[b][:, 256 * j:256 * j + 256], T.st[:, 256 * b:256 * b + 256]) for j in range(REP)], "", "Z%d Zr%d" % (b, b), 2 ** 21)
+    cp(T.ELu[:, 0:256], T.ELi[:, 0:256], "ELi0", "ELu0")
+    ts(T.BF[:, :], T.n143[:, :], cl(G15), A.is_equal, "n143 g15", "BF")
+    mm(r2l(P[7][:, 0:54], T.BF, 0, T.prR, 0, 864), "BF " + PRR, "b7")
+    ts(T.OH[:, 0:16], T.n143[:, 0:16], cl(QF), A.is_equal, "n143 qf", "oh")
+    t2(T.OH[:, 16:32], T.n143[:, 0:16], cl(QF), 256.0, A.is_equal, A.mult, "n143 qf", "oi")
+    ts(cl(NQ), cl(QF), -1.0, A.mult, "qf", "nq")
+    cp(cl(GF), T.coli[:, 2:3], "coli2", "gf")
+    t2(cl(WX), oh(1), 16.0, oh(0), A.mult, A.add, "oh", "wx")
+    tt(cl(WY), oh(2), oh(3, 1), A.add, "oh oi", "wy")
+    tt(cl(WN), oh(5), oh(4, 1), A.add, "oh oi", "wn")
+    tt(cl(WX), cl(WX), oh(6, 1), A.add, "wx oi", "wx")
+    tt(cl(WH), oh(1), oh(6, 1), A.add, "oh oi", "wh")
+    t2(cl(WE), oh(4), oh(5), 4608.0, A.add, A.mult, "oh", "we")
+    tt(cl(WU), cl(WX), cl(WY), A.add, "wx wy", "wu")
+    ts(cl(H16), oh(4), 16.0, A.mult, "oh", "h16")
+    ts(cl(TW6), oh(6), 2.0, A.mult, "oh", "tw6")
+    ts(cl(TW3), oh(3), 2.0, A.mult, "oh", "tw3")
+    ts(cl(SC0), cl(WX), 0.0, A.is_equal, "wx", "sc0")
+    ts(cl(SC1), cl(WY), 0.0, A.is_equal, "wy", "sc1")
+    for j, x in enumerate((1.0, 4608.0, -float(2 ** 27), -32.0, 32.0, 16.0, 256.0)):
+        lin(T.ID[:, 128 * j:128 * j + 128], T.IF[:, :], "IF", "ID%d" % j, 0.0, x)
+    ts(T.coli[:, 3:4], T.coli[:, 0:1], 7, A.bitwise_and, "coli", "coli3")
+    ts(cl(G23), cl(G15), 8.0, A.add, "g15", "g23")
+    ts(cl(N8), T.coli[:, 3:4], -1.0, A.mult, "coli3", "n8")
+    t2(T.BY[:, :], T.n143[:, :], cl(G23), cl(WY), A.is_equal, A.mult, "n143 g23 wy", "BY")
+    ts(cl(N16), cl(N8), -8.0, A.add, "n8", "n16")
+    t2(cl(JA), cl(G15), -15.0, cl(N8), A.add, A.subtract, "g15 n8", "ja")
+    t2(cl(JB), cl(G15), -15.0, cl(N16), A.add, A.subtract, "g15 n16", "jb")
+    lin(T.BA[:, bY:bY + 144], T.BF[:, :], "BF wx", "BX", 0.0, cl(WX))
+    ts(T.JP[:, 0:128], T.n143[:, 0:128], cl(JA), A.is_equal, "n143 ja", "JA")
+    ts(T.JP[:, 128:256], T.n143[:, 0:128], cl(JB), A.is_equal, "n143 jb", "JB")
+    tt(T.BA[:, bX:bX + 144], T.BA[:, bY:bY + 144], T.BY[:, :], A.add, "BX BY", "BA%d" % bX)
+    lin(T.NR[:, 0:256], lane, "cpl n8", "NR", cl(N8), 0.0)
+    lin(T.NR[:, 256:512], lane, "cpl n16", "NS", cl(N16), 0.0)
+    lin(T.NQR[:, :], lane[:, 0:16], "cpl nq", "NQR", cl(NQ), 0.0)
+    for off, x, r in ((bREL, 16384.0, ""), (bDEL, -8192.0, ""), (bABS, 8192.0, ""),
+                      (bN, cl(WN), "wn"), (bU, cl(WU), "wu"), (bE, cl(WE), "we"), (bH, cl(WH), "wh")):
+        lin(T.BA[:, off:off + 144], T.BF[:, :], "BF " + r, "BA%d" % off, 0.0, x)
+    for j in range(1, REP):
+        cp(Zb[0][:, 256 * j:256 * j + 256], Zb[0][:, 0:256], "Z0", "Zr0")
+    ms(T.FW[:, :], -1.0, "FW")
+    ms(T.d0f[:, :], 0.0, "d0f")
+    for j, x in enumerate((0.0, -512.0, -256.0)):
+        ms(T.d0k[:, 272 * j:272 * j + 272], x, "d0k%d" % j)
+    ms(T.d0f[:, 0:272:17], BIG, "d0f")
+    ms(T.d0k[:, 0:816:17], BIG, "d0k0 d0k1 d0k2")
+    ms(T.c92[:, :], -9216.0, "c92")
+    ms(T.d0k[:, 1:816:17], BIG, "d0k0 d0k1 d0k2")
+    for j, X in enumerate((T.G0, T.G1)):
+        ms(X[:, W + 256:W + 512], 0.0, "Gz%d" % j)
+    for j, X in enumerate((T.D0, T.D1)):
+        ms(X[:, W:W + 256], 0.0, "Dz%d" % j)
+    ms(T.TM[:, 256:384], 0.0, "TMb")
+    for X, w in ((T.G0, "Gd0"), (T.G1, "Gd1"), (T.Kw, "Kd")):
+        lin(X[:, W:W + 256], lane, "cpl oh h16", w, cl(H16), oh(5))
+    ts(st(STT, 48), st(STT, 48), -float(2 ** 27), A.add, "st4", "st4")
+    ts(T.prm[:, :], P[7][:, 0:54], 1.0 / 16, A.mult, "", "b7 prm")
+
+    def mid_setup():
+        cp(T.thf[0:48, :], T.thi[0:48, :], "thi M", "thf")
+        mm([(P[6][:, 0:48], T.thf[0:48, :], T.IF[0:48, 0:48])], "IF thf", "b6")
+        ts(T.cpi[:, 1280:1536], T.cin[:, 512:768], 8, A.arith_shift_right, "cin2 M", "cpk0")
+        ts(T.cpi[:, 1536:1792], T.cin[:, 512:768], 255, A.bitwise_and, "cin2 M", "cpk1")
+        cp(T.cpb[:, 1280:1792], T.cpi[:, 1280:1792], "cpk0 cpk1", "cpk")
+        dma("y", [(T.Kw[4::16, 0:W], T.cpb[:, 1280:1536]), (T.Kw[5::16, 0:W], T.cpb[:, 1536:1792])], "cpk", "K")
+        ts(T.TL[:, :], P[6][:, 0:48], 8192.0, A.mult, "", "b6 TL")
+        tt(T.PS[:, 256:304], T.TL[:, :], st(STT, 48), A.add, "TL st4", "TT0 TT1 TT2")
+
+    def late_setup():
+        t2(T.RP[:, 0:128], T.nd16[:, :], cl(GF), cl(WN), A.is_equal, A.mult, "nd16 gf wn", "RP0")
+        t2(T.RP[:, 128:256], T.nd16[:, :], cl(GF), oh(0), A.is_equal, A.mult, "nd16 gf oh", "RP1")
+        ts(st(SV, 48), st(SV, 48), cl(QF), A.add, "st3 qf", "st3")
+        t2(T.TM[:, 0:256], T.rr[:, :], cl(QF), 8192.0, A.is_le, A.mult, "rr qf", "TM")
+        ts(st(SDUM), st(SDUM), cl(QF), A.add, "st0 qf", "st0")
+        cp(T.cx[:, :], T.cxi[:, :], "cxi cxj", "cx")
+        ts(T.VP[:, 512:768], T.cc[:, :], oh(1), A.mult, "cc oh", "VP2")
+        ts(T.VP[:, 0:256], T.rr[:, :], oh(0), A.mult, "rr oh", "VP")
+        ts(T.VP[:, 256:512], lane, oh(2), A.mult, "cpl oh", "VP1")
+        tt(T.VP[:, 0:256], T.VP[:, 0:256], T.VP[:, 512:768], A.add, "VP VP2", "VP")
+
+    def late_lists():
+        cp(T.ELu[:, 256:V], T.ELi[:, 256:V], "ELi1", "ELu1 ELu2")
+
+    def late_out():
+        cp(T.ELf[:, :], T.ELi[:, :], "ELi0 ELi1", "ELf")
+
+    peers = [c for c in T.cores if c != core]
+    mask = topo.mask(core, peers[0])
+    for c in peers:
+        mask &= topo.mask(core, c)
+    ne = bin(mask).count("1")
+    nsent = [0]
+
+    def send(t, dst, src, sem, r):
+        to = T.cores[(rank + 1 + t % (N - 1)) % N]
+        rid, pid, _ = topo.addr(to)
+
+        def fn():
+            g.remote_dma(dst, src, T.sem[sem], T.sem.sent, pid, rid, mask)
+            return sem, (2 * ne if sem[1] == "z" else ne)
+        lastw.setdefault("l" + sem[1:], []).append(add("c", "far", fn, r, "", 300.0, FAR + dst.shape[1] * 4.0))
+        nsent[0] += ne
+
+    def si(t, j, n=1): return T.si[:, 192 * t + 16 * j:192 * t + 16 * (j + n)]
+    def sf(t, j): return T.sf[:, 256 * t + 16 * j:256 * t + 16 * j + 16]
+    def sb(t, j): return T.sb[:, 64 * t + 16 * j:64 * t + 16 * j + 16]
+    def su(t, j): return T.su[:, 128 * t + 16 * j:128 * t + 16 * j + 16]
+    def blk(X, t): return X[:, 256 * t:256 * t + 256]
+    def allg(p): return " ".join("G%d_%d" % (p, j) for j in range(len(OC)))
+    def alld(p): return " ".join("D%d_%d" % (p, j) for j in range(NC))
+
+    def scat_m(t): cp(T.Mw[:, :].indirect(T.lo[:, 16 * t:16 * t + 16]), blk(T.lz, t), "lz%d" % t, "M")
+    def scat_k(t): cp(T.Kw[:, :].indirect(T.lo[:, 16 * t:16 * t + 16]), blk(T.le, t), "lz%d le%d" % (t, t), "K Kd")
+
+    def own_gather(t, j):
+        b, p, (k0, k1) = t % 3, t % 2, OC[j]
+        lin(Gb[p][:, 256 * k0:256 * k1], T.Xw[:, 0:W].indirect(T.ELu[:, 256 * b + 16 * k0:256 * b + 16 * k1]),
+            "X Xb ELu%d" % b, "G%d_%d #og" % (p, j))
+
+    def own_mm(t, j):
+        b, p, (k0, k1) = t % 3, t % 2, OC[j]
+        if j < 0:
+            mm([(P[1][:, :], I1, T.NB[:, 512 * b:512 * b + 512]), (P[1][:, :], I1, T.NR[:, :])], "ID0 NR NS NB%d" % b, "b1", True, False)
+            return
+        lst = [(P[1][:, 256 * (r // 8) + 16 * k0:256 * (r // 8) + 16 * k1], T.BA[:, bX + 15 - r % 8:bX + 143 - r % 8],
+                Gb[p][:, 256 * k0 + r:256 * k1:16]) for r in range(16)]
+        mm(lst, "G%d_%d BA%d" % (p, j, bX), "b1", False, j == len(OC) - 1)
+
+    def diff(t, j):
+        b, p, (k0, k1) = t % 3, t % 2, CH[j]
+        tt(Db[p][:, 256 * k0:256 * k1], T.Mw[:, 0:W].indirect(T.ELu[:, 256 * b + 16 * k0:256 * b + 16 * k1]),
+           Zb[b][:, 0:256 * (k1 - k0)], A.subtract, "M Z%d Zr%d ELu%d" % (b, b, b), "D%d_%d #df" % (p, j))
+
+    def fold(t, j):
+        p, (k0, k1) = t % 2, CH[j]
+        o, a, r, w = T.AB[:, 256 * k0:256 * k1], Db[p][:, 256 * k0:256 * k1], "D%d_%d" % (p, j), "AB%d" % j
+        if j < RELU:
+            ts(o, a, 0.0, A.max, r, w)
+        else:
+            act(o, a, F.Abs, r, w)
+
+    def dist_a(t, j):
+        p, (k0, k1) = t % 2, CH[j]
+        lst = [(P[0][:, 0:KL], I1, T.kc[:, 0:KL])] if j == 0 else []
+        if j < RELU:
+            lst += r2l(P[0][:, 16 * k0:16 * k1], T.BA, bDEL, Db[p], 256 * k0, 256 * k1)
+        if lst:
+            mm(lst, "D%d_%d ID0 kc BA%d" % (p, j, bDEL), "b0", j == 0, False)
+
+    def dist_b(t, j):
+        k0, k1 = CH[j]
+        off = bREL if j < RELU else bABS
+        bank = 4 if j == NC - 1 else 0
+        mm(r2l(P[bank][:, 16 * k0:16 * k1], T.BA, off, T.AB, 256 * k0, 256 * k1), "AB%d BA%d" % (j, off), "b%d" % bank, False, bank == 4)
+
+    def live(t):
+        ts(T.pr[:, :], P[1][:, :], 0.0, A.is_equal, "", "b1 pr")
+        mm([(P[2][:, 0:256], T.JP[:, 0:128], T.pr[:, 0:256]), (P[2][:, 0:256], T.JP[:, 128:256], T.pr[:, 256:512])], "pr JA JB", "b2")
+
+    def live_s(t): act(T.lv[:, :], P[2][:, 0:256], F.Sign, "", "b2 lv")
+
+    def live_mm(t):
+        mm([(P[0][:, 0:KL], ILV, T.lv[:, 0:KL])], "lv ID2", "b0", False, True)
+        mm([(P[4][:, KL:256], I1, T.kc[:, KL:256]), (P[4][:, KL:256], ILV, T.lv[:, KL:256])], "lv kc ID0 ID2", "b4", True, False)
+
+    def rows_of(t, part):
+        if part == 0:
+            tt(si(t, 2, 3), T.SK[:, 16:816:17], st(SADD, 48), A.add, "SK st1a st1b st1c", "raw%d" % t)
+            tt(sf(t, 6), sf(t, 1), st(SZ2), A.add, "fl%d st2b" % t, "b_%d" % t)
+        elif part == 1:
+            ts(si(t, 5, 2), si(t, 2, 2), 4095, A.bitwise_and, "raw%d" % t, "low%d" % t)
+            tt(sf(t, 5), si(t, 4), st(SZ1), A.min, "raw%d st2a" % t, "a%d" % t)
+            ts(su(t, 4), si(t, 6), cl(QF), A.add, "low%d qf" % t, "om%d" % t)
+            tt(sf(t, 6), sf(t, 6), si(t, 5), A.max, "b_%d low%d" % (t, t), "b_%d" % t)
+        else:
+            tt(sf(t, 5), sf(t, 5), sf(t, 6), A.max, "a%d b_%d" % (t, t), "a%d" % t)
+            ts(su(t, 5), sf(t, 5), cl(QF), A.add, "a%d qf" % t, "oz%d" % t)
+
+    def rows_late(t):
+        b = t % 3
+        tt(sf(t, 7), si(t, 5), sf(t, 1), A.subtract, "low%d fl%d" % (t, t), "c%d" % t)
+        t2(sf(t, 8), si(t, 4), float(2 ** 20), float(2 ** 22), A.is_lt, A.mult, "raw%d" % t, "d%d" % t)
+        t2(sf(t, 2), si(t, 1), 4096.0, 524288.0, A.is_ge, A.mult, "lf%d" % t, "fm%d" % t)
+        tt(sf(t, 7), sf(t, 7), si(t, 4), A.max, "c%d raw%d" % (t, t), "c%d" % t)
+        tt(sf(t, 8), sf(t, 8), si(t, 1), A.add, "d%d lf%d" % (t, t), "d%d" % t)
+        tt(T.PS[:, 256 + 16 * b:272 + 16 * b], T.PS[:, 256 + 16 * b:272 + 16 * b], sf(t, 2), A.add, "TT%d fm%d" % (b, t), "TT%d" % b)
+        tt(sb(t, 1), sf(t, 7), sf(t, 8), A.min, "c%d d%d" % (t, t), "row%d" % t)
+
+    def em_out(t):
+        p = t % 2
+        lin(blk(T.se, t), Gb[p][:, 0:W].indirect(su(t, 4)), allg(p) + " om%d" % t, "se%d" % t)
+        send(t, blk(T.le, t), blk(T.se, t), "ae%d" % t, "se%d" % t)
+
+    def stale_gather(t):
+        p = t % 2
+        lin(T.GS[:, :], Gb[p][:, :].indirect(su(t, 5)), allg(p) + " Gd%d Gz%d oz%d" % (p, p, t), "GS")
+        lin(T.DS[:, :], Db[p][:, :].indirect(su(t, 5)), alld(p) + " Dz%d Dn%d oz%d" % (p, p, t), "DS", -0.25, 0.5)
+
+    def hop_mm(t):
+        mm(r2l(P[6][:, 256:272], T.BA, bH, T.GS, 0, 256), "GS BA%d" % bH, "b6")
+        mm([(P[6][:, 0:256], T.RP[:, 128:256], T.GS[:, :])], "GS RP1", "b6")
+
+    def state_v(t):
+        t2(T.DR[:, :], T.DS[:, :], 12582912.0, 12582912.0, A.add, A.subtract, "DS", "DR")
+
+    def state_mm(t):
+        b = t % 3
+        mm([(P[7][:, 0:256], I1, Zb[b][:, 0:256]), (P[7][:, 0:256], I1, T.DR[:, :]), (P[7][:, 0:256], I1, blk(T.sz, t))],
+           "Z%d DR sz%d ID0" % (b, t), "b7")
+
+    def state_s(t):
+        b = t % 3
+        lin(Zb[b][:, 0:256], P[7][:, 0:256], "", "b7 Z%d" % b)
+        if t + 3 < RO:
+            dma("y", [(Zb[b][:, 256 * j:256 * j + 256], Zb[b][:, 0:256]) for j in range(1, REP)], "Z%d" % b, "Zr%d" % b)
+        else:
+            dma("y", [(blk(T.yz, b), Zb[b][:, 0:256])], "Z%d" % b, "")
+
+    def hint_a(t):
+        t2(si(t, 7), si(t, 5), 4, 240, A.arith_shift_right, A.bitwise_and, "low%d" % t, "s16_%d" % t)
+        ts(T.MK[:, :], P[6][:, 0:256], cl(QF), A.is_equal, "qf", "b6 MK")
+        tt(sf(t, 9), P[6][:, 256:272], si(t, 7), A.add, "s16_%d" % t, "b6 hc%d" % t)
+
+    def hint_b(t):
+        cp(su(t, 6), sf(t, 9), "hc%d" % t, "hu%d" % t)
+        tt(T.HG[:, :], T.ELf[:, :].indirect(su(t, 6)), T.MK[:, :], A.mult, "ELf MK hu%d" % t, "HG")
+
+    def hint_mm(t): mm(r2l(P[6][:, 272:288], T.BF, 0, T.HG, 0, 256), "HG BF", "b6")
+
+    def row_mm(t):
+        mm([(P[7][:, 256:512], IM, T.kc[:, :])] + [(P[7][:, 256 + 16 * k:272 + 16 * k], IP, sb(t, 1)) for k in range(16)],
+           "kc ID3 ID4 row%d" % t, "b7")
+
+    def row_s(t):
+        act(T.AR[:, :], P[7][:, 256:512], F.Abs, "", "b7 AR", scale=1.0 / 32)
+        act(P[5][:, 256:512], P[7][:, 256:512], F.Abs, "", "b7 b5")
+
+    def name_v(t):
+        tt(sf(t, 10), P[6][:, 272:288], sf(t, 1), A.add, "fl%d" % t, "b6 nm%d" % t)
+        tt(sf(t, 10), sf(t, 10), sf(t, 4), A.min, "nm%d C%d" % (t, t), "nm%d" % t)
+        cp(sb(t, 2), sf(t, 10), "nm%d" % t, "nh%d" % t)
+        tt(sb(t, 3), sf(t, 10), sb(t, 2), A.subtract, "nm%d nh%d" % (t, t), "nl%d" % t)
+
+    def bounds_mm(t):
+        lst = [(P[5][:, 0:256], IM, T.AR[:, :])]
+        for k in range(16):
+            lst += [(P[5][:, 16 * k:16 * k + 16], I1, sb(t, j)) for j in (2, 3)]
+        mm(lst, "AR ID0 ID3 nh%d nl%d" % (t, t), "b5")
+
+    def list_a(t): tt(T.Et[:, :], P[5][:, 256:512], blk(T.ELf, t % 3), A.min, "ELf", "b5 Et")
+
+    def list_b(t):
+        b = t % 3
+        tt(blk(T.ELf, b), P[5][:, 0:256], T.Et[:, :], A.max, "Et", "b5 ELf")
+        if t + 3 < RO:
+            cp(blk(T.ELu, b), blk(T.ELf, b), "ELf", "ELu%d" % b)
+        else:
+            dma("y", [(blk(T.ye, b), blk(T.ELf, b))], "ELf", "")
+
+    def choose(t):
+        b, p, s, u, w = t % 3, t % 2, t % 2, t - 1, t - 2
+        Fw = T.FW[:, 512:768]
+        lin(T.PS[:, 0:KL], P[0][:, 0:KL], "", "b0 PS")
+        lin(T.PS[:, KL:256], P[4][:, KL:256], "", "b4 PS2")
+        lin(T.PP[:, :], T.PS[:, :].indirect(T.prm[:, 18 * b:18 * b + 17]), "PS PS2 TT0 TT1 TT2 prm", "PP")
+        if w >= 0:
+            bounds_mm(w)
+        scan(T.SF[:, :], T.d0f[:, :], T.PP[:, :], "PP d0f", "SF")
+        act(T.PK[:, 0:272], T.PP[:, :], F.Abs, "PP", "PK0")
+        act(T.PK[:, 272:544], T.PP[:, :], F.Abs, "PP", "PK1", bias=float(2 ** 27 - 2 ** 25))
+        cp(si(t, 0), T.SF[:, 16:272:17], "SF", "f%d" % t)
+        ts(si(t, 1), si(t, 0), 8191, A.bitwise_and, "f%d" % t, "lf%d" % t)
+        ts(su(t, 0), si(t, 1), cl(QF), A.add, "lf%d qf" % t, "of%d" % t)
+        lin(Fw, Gb[p][:, 0:W + 256].indirect(su(t, 0)), allg(p) + " Gd%d of%d" % (p, t), "FW")
+        act(blk(T.sz, t), Db[p][:, 0:W + 256].indirect(su(t, 0)), F.Abs, alld(p) + " Dz%d of%d" % (p, t), "sz%d" % t)
+        send(t, blk(T.lz, t), blk(T.sz, t), "az%d" % t, "sz%d" % t)
+        lin(T.F2[:, :], Fw, "FW", "F2")
+        t2(sf(t, 0), si(t, 1), 4096.0, 256.0, A.is_ge, A.mult, "lf%d" % t, "nf%d" % t)
+        t2(sf(t, 1), si(t, 1), 4096.0, 8192.0, A.is_lt, A.mult, "lf%d" % t, "fl%d" % t)
+        if w >= 0:
+            list_b(w)
+        if u >= 0:
+            hint_a(u)
+            state_v(u)
+        if t == 0:
+            late_lists()
+        mm(r2l(P[3][:, 0:16], T.BA, bN, T.FW, 512, 768), "FW BA%d" % bN, "b3")
+        mm([(P[2][:, 0:16], I1, T.NB[:, 512 * b:512 * b + 16]), (P[2][:, 0:16], I1, T.NQR[:, :])]
+           + r2l(P[2][:, 0:16], T.BA, bU, T.FW, 512, 768), "FW ID0 NQR NB%d BA%d" % (b, bU), "b2")
+        ef = T.su[:, 128 * t + 32:128 * t + 56]
+        cp(ef[:, 0:16], P[3][:, 0:16], "", "b3 ef%d" % t)
+        cp(ef[:, 16:24], P[3][:, 1:16:2], "", "b3 eg%d" % t)
+        lin(T.KG[:, :], T.Kw[:, 0:W + 256].indirect(ef), "K Kd ef%d eg%d" % (t, t), "KG")
+        tt(sf(t, 3), P[3][:, 0:16], sf(t, 0), A.add, "nf%d" % t, "b3 es%d" % t)
+        act(T.PK[:, 544:816], T.PP[:, :], F.Relu, "PP", "PK2", scale=-1.0)
+        mm([(P[3][:, 0:384], I1, T.TM[:, :])], "TM TMb ID0", "b3", True, False)
+        if u >= 0:
+            rows_late(u)
+        cp(su(t, 1), P[2][:, 0:16], "", "b2 u%d" % t)
+        tt(sb(t, 0), P[2][:, 0:16], st(SV + 16 * b), A.is_lt, "st3", "b2 lt%d" % t)
+        tt(T.EQ[:, :], T.FW[:, 512 - 256 * b:1280 - 256 * b].indirect(su(t, 1)), T.F2[:, :], A.is_equal, "FW F2 u%d" % t, "EQ")
+        mm([(P[3][:, 0:384], T.RP[:, 0:128], T.KG[:, :])], "KG RP0", "b3", False, True)
+        mm(r2l(P[2][:, 0:16], T.BA, bN, T.KG, 0, 256), "KG BA%d" % bN, "b2")
+        lin(T.CR[:, :], P[3][:, 0:384], "", "b3 CR")
+        mm([(P[4][:, 0:16], I1, T.c92[:, :]), (P[4][:, 0:16], I46, sb(t, 0))] + r2l(P[4][:, 0:16], T.BA, bE, T.EQ, 0, 256),
+           "EQ c92 ID0 ID1 lt%d BA%d" % (t, bE), "b4")
+        if u >= 0:
+            hint_b(u)
+        else:
+            late_out()
+        cp(sf(t, 4), P[2][:, 0:16], "", "b2 C%d" % t)
+        cp(su(t, 7), P[2][:, 0:16], "", "b2 cu%d" % t)
+        tt(T.E2[:, :], sf(t, 4).indirect(T.cx[:, :]), T.CR[:, :], A.is_equal, "C%d cx CR" % t, "E2")
+        bias = 0.0 if b == 0 else (oh((6, 3)[s]) if b == 1 else cl((TW6, TW3)[s]))
+        lin(T.XG[:, :], T.Xw[:, :].indirect(su(t, 7)), "X Xb cu%d sc0 sc1 oh tw6 tw3" % t, "XG", bias, cl((SC0, SC1)[s]))
+        act(sf(t, 12), P[4][:, 0:16], F.Relu, "", "b4 y%d" % t)
+        mm(r2l(P[2][:, 0:16], T.BA, bABS, T.E2, 0, 256) + r2l(P[2][:, 1:16:2], T.BA, bABS, T.E2, 256, 384), "E2 BA%d" % bABS, "b2")
+        tt(sf(t, 3), sf(t, 12), sf(t, 3), A.add, "es%d y%d" % (t, t), "es%d" % t)
+        cp(T.so[:, 16 * t:16 * t + 16], sf(t, 3), "es%d" % t, "so%d" % t)
+        send(t, T.lo[:, 16 * t:16 * t + 16], T.so[:, 16 * t:16 * t + 16], "az%d" % t, "so%d" % t)
+        scan(T.SK[:, :], T.d0k[:, :], T.PK[:, :], "PK0 PK1 PK2 d0k0 d0k1 d0k2", "SK")
+        lin(Db[p][:, W + 256:W + 512], Zb[b][:, 0:256], "Z%d of%d" % (b, t), "Dn%d" % p, 0.0, -2.0)
+        if u >= 0:
+            state_mm(u)
+            state_s(u)
+            row_mm(u)
+            hint_mm(u)
+        tt(sf(t, 11), P[2][:, 0:16], st(SDUM), A.min, "st0", "b2 cd%d" % t)
+        rows_of(t, 0)
+        tt(sf(t, 11), sf(t, 11), sf(t, 4), A.max, "cd%d C%d" % (t, t), "cd%d" % t)
+        rows_of(t, 1)
+        em_out(t)
+        if u >= 0:
+            row_s(u)
+        cp(T.cs[:, :], sf(t, 11), "cd%d" % t, "cs")
+        rows_of(t, 2)
+        stale_gather(t)
+
+    def claims(t, hi, lo):
+        s = t % 2
+        for c in range(hi, lo, -1):
+            tt(T.Xw[:, :].indirect(T.cs[:, 2 * c:2 * c + 2]), T.XG[:, 32 * c:32 * c + 32],
+               T.VP[:, 256 * s + 32 * c:256 * s + 32 * c + 32], A.add, "cs XG VP VP1", "X Xb")
+
+    for t in range(RO):
+        u, w = t - 1, t - 2
+        own_mm(t, -1)
+        own_gather(t, 0)
+        if u >= 0:
+            hop_mm(u)
+            scat_m(u)
+        own_mm(t, 0)
+        diff(t, 0)
+        own_gather(t, 1)
+        fold(t, 0)
+        own_mm(t, 1)
+        dist_a(t, 0)
+        dist_b(t, 0)
+        if t == 0:
+            mid_setup()
+        diff(t, 1)
+        own_gather(t, 2)
+        own_mm(t, 2)
+        own_gather(t, 3)
+        if RELU > 1:
+            fold(t, 1)
+            dist_a(t, 1)
+            dist_b(t, 1)
+        own_mm(t, 3)
+        if RELU < 2:
+            fold(t, 1)
+            dist_b(t, 1)
+        diff(t, 2)
+        for j in range(2, NC - 1):
+            fold(t, j)
+            if j == NC - 2:
+                live(t)
+            diff(t, j + 1)
+            if j < RELU:
+                dist_a(t, j)
+            dist_b(t, j)
+        live_s(t)
+        fold(t, NC - 1)
+        live_mm(t)
+        dist_b(t, NC - 1)
+        if t == 0:
+            late_setup()
+        if w >= 0:
+            name_v(w)
+            list_a(w)
+        if u >= 0:
+            scat_k(u)
+        choose(t)
+        if t < RO - 1:
+            claims(t, 7, -1)
+
+    t = RO - 1
+    rows_late(t)
+    scat_m(t)
+    dma("y", [(T.ym[:, 0:W // 2], T.Mw[:, 0:W // 2])], "M", "")
+    name_v(t - 1)
+    bounds_mm(t - 1)
+    hop_mm(t)
+    list_a(t - 1)
+    claims(t, 7, 3)
+    hint_a(t)
+    list_b(t - 1)
+    row_mm(t)
+    hint_b(t)
+    row_s(t)
+    hint_mm(t)
+    claims(t, 3, -1)
+    dma("s", [(T.cpb[:, a:a + 256], T.Xw[q::16, 0:W]) for q, a in rows[:5]], "X Xb", "cpb")
+    scat_k(t)
+    dma("s", [(T.cpb[:, 1280:1536], T.Kw[4::16, 0:W]), (T.cpb[:, 1536:1792], T.Kw[5::16, 0:W])], "K", "cpk")
+    dma("s", [(T.ym[:, W // 2:W], T.Mw[:, W // 2:W])], "M", "")
+    state_v(t)
+    tt(T.TL[:, :], T.PS[:, 256:304], st(STT, 48), A.subtract, "TT0 TT1 TT2 st4", "TL")
+    list_a(t)
+    ts(T.TL[:, :], T.TL[:, :], 1.0 / 8192, A.mult, "TL", "TL")
+    name_v(t)
+    state_mm(t)
+    bounds_mm(t)
+    state_s(t)
+    mm([(P[2][0:48, 0:128], T.TL[:, :], T.IF[:, :])], "IF TL", "b2")
+    list_b(t)
+    lin(T.oT[0:48, :], P[2][0:48, 0:128], "", "b2 oT")
+    dma("s", [(T.yt[q, :], T.oT[0:48, 16 * q:16 * q + 16]) for q in range(8)], "oT", "")
+    mm([(P[1][:, 0:256], I, T.cpb[:, a:a + 256]) for I, a in ((I1, 0), (I16, 256), (I256, 512))], "cpb ID0 ID5 ID6", "b1")
+    mm([(P[1][:, 256:512], I, T.cpb[:, a:a + 256]) for I, a in ((I256, 768), (I1, 1024))], "cpb", "b1")
+    mm([(P[0][:, 0:256], I, T.cpb[:, a:a + 256]) for I, a in ((I256, 1280), (I1, 1536))], "cpk", "b0")
+    cp(T.oO[:, :], P[1][:, :], "", "b1 oO")
+    lin(T.oK[:, :], P[0][:, 0:256], "", "b0 oK")
+    dma("y", [(T.yo[0:8, :], T.oO[:, 0:256]), (T.yo[8:16, :], T.oO[:, 256:512])], "oO", "")
+    dma("s", [(T.yk[:, :], T.oK[:, :])], "oK", "")
+    emit()
+    g.wait_ge(T.sem.sent, nsent[0])

@@ -2,45 +2,57 @@ import math
 from concourse.mybir import AluOpType as A, ActivationFunctionType as F
 
 W, V, PB, RO, N = 4096, 768, 256, 8, 4
-CH = [(0, 5), (5, 10), (10, 14), (14, 16)]
-RELU = 1
+STREAM = [("diff", 0, 5), ("diff", 5, 10), ("relu", 0, 5), ("diff", 10, 14), ("abs", 5, 10), ("live", 0, 0), ("diff", 14, 16), ("abs", 10, 14),
+          ("sign", 0, 0), ("abs", 14, 16), ("least", 0, 0)]
 OC = [(0, 4), (4, 8), (8, 12), (12, 16)]
+KL = 16 * 14
 REP = 5
+ROUND_S, MASK_S = True, True
 BIG = float(2 ** 29)
-CYC, PEC, GATH, SCAT, HOP, FAR = 1.04, 0.52, 1.56, 3.8, 60.0, 2200.0
-ROUNDS = 3
+MAGIC = 12582912.0
+CYC, PEC, GATH, SCAT, HOP, FAR, DMA, RATE = 0.83, 0.42, 1.56, 3.8, 175.0, 2300.0, 2000.0, 300.0
+CYCLE = {
+    "v": "putM' diff0 diff5 relu0 diff10 live diff14 put'' putK' late least min row others first name other same hint' "
+         "enclosed twice drop cut' offsets'' claim",
+    "s": "own0 own4 own8 own12 abs5 abs10 sign abs14 least keys chosen minus enclosed twice send merge stale mask round cutoff state",
+    "p": "own0 own4 diff0 own8 relu0 own12 live abs5 abs10 sign abs14 cutoff' open name other smaller twice enclosed same both hint' bounds'",
+}
+LAST = 2
+SIZE = {"bfloat16": 2, "float16": 2, "uint16": 2, "float32": 4, "int32": 4}
 
 
 def _sb(n, d):
     return ("sbuf", [128, n], d)
 
 
-bf, f32, i32, u16 = "bfloat16", "float32", "int32", "uint16"
+bf, f16, f32, i32, u16 = "bfloat16", "float16", "float32", "int32", "uint16"
+TW = 8960
 SCRATCH = {
-    "Mw": _sb(8704, bf), "Kw": _sb(8704, bf), "Xw": _sb(4608, bf),
-    "G0": _sb(4608, bf), "G1": _sb(4608, bf), "D0": _sb(4608, bf), "D1": _sb(4608, bf), "AB": _sb(4096, bf),
+    "Mw": _sb(TW, bf), "Kw": _sb(TW, bf), "Xw": _sb(4128, bf),
+    "G0": _sb(4352, bf), "G1": _sb(4352, bf), "D0": _sb(4608, bf), "D1": _sb(4608, bf), "AB": _sb(4096, bf),
     "Z0": _sb(REP * 256, bf), "Z1": _sb(REP * 256, bf), "Z2": _sb(REP * 256, bf),
-    "ELi": _sb(V, i32), "ELf": _sb(V, f32), "ELu": _sb(V, u16), "Et": _sb(256, f32),
+    "ELi": _sb(V, i32), "ELf": _sb(V, f32), "ELu": _sb(V, u16), "Et": _sb(256, f32), "oE": _sb(V, f32),
     "cin": _sb(768, i32), "cpi": _sb(1792, i32), "cpb": _sb(2304, bf), "thi": _sb(128, i32), "thf": _sb(128, f32),
-    "PS": _sb(304, f32), "PP": _sb(272, f32), "PK": _sb(816, f32), "SF": _sb(272, f32), "SK": _sb(816, f32),
-    "d0f": _sb(272, f32), "d0k": _sb(816, f32), "prm": _sb(54, u16), "prR": _sb(864, f32),
-    "pr": _sb(512, bf), "lv": _sb(256, bf), "JP": _sb(256, bf), "BY": _sb(144, bf), "NQR": _sb(16, bf),
-    "FW": _sb(1280, bf), "F2": _sb(256, bf), "EQ": _sb(256, bf), "KG": _sb(384, bf), "CR": _sb(384, f32), "E2": _sb(384, bf),
-    "XG": _sb(256, bf), "GS": _sb(256, bf), "DS": _sb(256, f32), "DR": _sb(256, bf), "MK": _sb(256, f32), "HG": _sb(256, f32),
+    "PS": _sb(304, f32), "PP0": _sb(272, f32), "PP1": _sb(272, f32), "PK": _sb(544, f32), "SF": _sb(272, f32), "SK": _sb(544, f32), "SJ": _sb(272, f32),
+    "d0f": _sb(272, f32), "d0k": _sb(544, f32), "dJ": _sb(272, f32), "prm": _sb(54, u16), "prR": _sb(864, f32),
+    "pr": _sb(512, bf), "lv": _sb(256, bf), "JP": _sb(256, bf), "BY": _sb(144, bf),
+    "FW": _sb(1280, bf), "EQ": _sb(256, bf), "F2": _sb(256, bf), "KG": _sb(256, bf), "CR": _sb(256, f32), "E2": _sb(384, bf),
+    "XG": _sb(256, bf), "DS": _sb(256, bf), "ZR": _sb(256, f32), "MA": _sb(256, bf), "MK": _sb(512, f32), "HG": _sb(256, f16),
     "AR": _sb(256, bf),
     "sz": _sb(RO * 256, bf), "se": _sb(RO * 256, bf), "so": _sb(RO * 16, u16),
     "lz": _sb(RO * 256, bf), "le": _sb(RO * 256, bf), "lo": _sb(RO * 16, u16),
-    "si": _sb(RO * 192, i32), "sf": _sb(RO * 256, f32), "sb": _sb(RO * 64, bf), "su": _sb(RO * 128, u16),
-    "col": _sb(32, f32), "coli": _sb(8, i32), "n143": _sb(144, f32), "one": _sb(144, f32), "nd16": _sb(128, f32),
-    "OH": _sb(32, f32), "BA": _sb(9 * 144, bf), "BF": _sb(144, f32), "RP": _sb(256, bf),
-    "ID": _sb(7 * 128, bf), "IF": _sb(128, f32),
-    "rr": _sb(256, bf), "cc": _sb(256, bf), "kc": _sb(256, bf), "NB": _sb(3 * 512, bf), "NR": _sb(512, bf),
-    "TM": _sb(384, bf), "VP": _sb(768, bf), "stt": _sb(256, f32), "cxi": _sb(24, i32), "cx": _sb(24, u16), "c92": _sb(16, bf),
+    "si": _sb(RO * 192, i32), "sf": _sb(RO * 144, f32), "sb": _sb(RO * 64, bf), "sh": _sb(RO * 48, f16), "su": _sb(RO * 128, u16),
+    "col": _sb(32, f32), "coli": _sb(8, i32), "n143": _sb(144, f32), "one": _sb(128, f32), "nd16": _sb(128, f32),
+    "OH": _sb(32, f32), "BA": _sb(11 * 144, bf), "BF": _sb(144, f32), "RP": _sb(256, bf),
+    "ID": _sb(15 * 128, bf), "IF": _sb(128, f32),
+    "rr": _sb(256, bf), "cc": _sb(256, bf), "kc": _sb(256, bf), "NB": _sb(512, bf), "on": _sb(256, bf),
+    "LT": _sb(2048, bf), "VP": _sb(768, bf), "stt": _sb(256, f32), "cxi": _sb(16, i32), "cx": _sb(16, u16),
     "cs": _sb(16, u16), "oK": _sb(256, f32), "oO": _sb(512, f32), "oT": _sb(128, f32), "TL": _sb(48, f32),
 }
 for _b in range(8):
     SCRATCH["P%d" % _b] = ("psum", [128, 512], f32)
-SEMAPHORES = ["v", "s", "p", "c", "sent"] + ["az%d" % t for t in range(RO)] + ["ae%d" % t for t in range(RO)] + ["d%d" % t for t in range(40)]
+SEMAPHORES = ["v", "s", "p", "c", "sent"] + ["az%d" % t for t in range(RO)] + ["ae%d" % t for t in range(RO)] + ["d%d" % t for t in range(48)]
+ORDER = []
 
 
 def rank_program(g, core, T, topo):
@@ -48,52 +60,82 @@ def rank_program(g, core, T, topo):
     if rank is None:
         return
     Q = {"v": g.vector, "s": g.scalar, "p": g.tensor, "c": g, "y": g.sync}
-    ops, lastw, readers = [], {}, {}
-    BANKS = ["b%d" % b for b in range(8)]
-    KL, NC = 16 * CH[-1][0], len(CH)
+    ops, seen_by, closer, named, now = [], {}, {}, {}, ["", -1]
+    ALLP = 2 ** 128 - 1
 
-    def add(q, kind, fn, r, w, busy, lat):
-        r, w, me, dep = r.split(), w.split(), len(ops), {}
-        for k in r:
-            for j in lastw.get(k, []):
-                dep[j] = True
-        for k in w:
-            for j in lastw.get(k, []) + readers.get(k, []):
-                same = ops[j]["q"] == q and ops[j]["kind"] == "op" and (q == "p" or k in BANKS or k[0] == "#")
-                dep[j] = dep.get(j, False) or (not same and k[0] != "#")
+    def B(name, a=None, b=None, step=1, p=None):
+        where, shape, dt = SCRATCH[name]
+        a, b = (0, shape[1]) if a is None else (a, a + 1 if b is None else b)
+        p = p or (0, 128, 1)
+        ap = T[name][p[0]:p[1]:p[2], a:b:step]
+        if where == "psum":
+            return dict(ap=ap, key=(name, 0, 1, ALLP), bank=True, n=len(range(a, b, step)), dt=dt)
+        last = a + (len(range(a, b, step)) - 1) * step + 1
+        mask = ALLP if p == (0, 128, 1) else sum(1 << j for j in range(*p))
+        return dict(ap=ap, key=(name, a * SIZE[dt] // 16 * 16, -(-last * SIZE[dt] // 16) * 16, mask), n=len(range(a, b, step)), dt=dt)
+
+    def H(ap, dt): return dict(ap=ap, key=None, dt=dt, n=int(math.prod(ap.shape)) // 128)
+    def ind(win, off): return dict(ap=win["ap"].indirect(off["ap"]), key=win["key"], off=off["key"], n=16 * off["n"], dt=win["dt"])
+    def ap(x): return x["ap"] if isinstance(x, dict) else x
+
+    def add(q, kind, fn, r, w, busy, lat, chain=None):
+        me, dep, rk, wk = len(ops), {}, [], []
+        for x in r:
+            if isinstance(x, dict) and x["key"]:
+                (wk if x.get("bank") else rk).append((x["key"], x.get("bank")))
+        for x in w:
+            (rk if x.get("acc") else wk).append((x["key"], x.get("bank")))
+        rk += [(x["off"], None) for x in list(r) + list(w) if isinstance(x, dict) and "off" in x]
+        if chain:
+            wk.append(((chain, 0, 1, ALLP), "order"))
+        for keys, write in ((rk, False), (wk, True)):
+            for (name, lo, hi, pm), bank in keys:
+                for lo2, hi2, pm2, j, wr in seen_by.get(name, []):
+                    if j != me and lo < hi2 and lo2 < hi and pm & pm2 and (write or wr):
+                        free = bank == "order" or (bank and ops[j]["q"] == q)
+                        dep[j] = dep.get(j, False) or not free
+        for keys, write in ((rk, False), (wk, True)):
+            for (name, lo, hi, pm), bank in keys:
+                old = seen_by.get(name, [])
+                if write:
+                    old = [x for x in old if not (lo <= x[0] and x[1] <= hi and x[2] & ~pm == 0)]
+                seen_by[name] = old + [(lo, hi, pm, me, write)]
         ops.append(dict(q=q, kind=kind, fn=fn, dep=dep, busy=busy, lat=lat))
-        for k in r:
-            readers.setdefault(k, []).append(me)
-        for k in w:
-            lastw[k] = [me]
-            readers[k] = []
+        named.setdefault((q,) + tuple(now), []).append(me)
         return me
 
-    def op(q, fn, r, w, busy): add(q, "op", fn, r, w, busy, busy)
+    def at(name, t=None): now[:] = [name, now[1] if t is None else t]
 
-    def dma(q, pairs, r, w, behind=0):
-        size = behind + sum(int(math.prod(o.shape)) * (2 if "16" in str(o.dtype) else 4) for o, i in pairs)
-        add(q, "dma", pairs, r, w + " #" + q, 60.0 * len(pairs), 2000.0 + size / 150.0)
+    def op(q, fn, r, w, busy, chain=None): add(q, "op", fn, r, w, busy, busy, chain)
 
-    def emit():
+    def dma(q, pairs, behind=0, after=()):
+        size = behind + sum(128 * o["n"] * SIZE[o["dt"]] if o["key"] is None else 128 * i["n"] * SIZE[i["dt"]] if i["key"] is None
+                            else int(math.prod(o["ap"].shape)) * SIZE[o["dt"]] for o, i in pairs)
+        add(q, "dma", pairs, [i for o, i in pairs] + list(after), [o for o, i in pairs if o["key"]], 60.0 * len(pairs), DMA + size / RATE,
+            None if closer.get("steps") else "#" + q)
+
+    def plan():
         n = len(ops)
+        for q, names in CYCLE.items():
+            row = [i for t in range(RO) for x in names.split() for i in named.get((q, x.rstrip("'"), t - x.count("'")), [])]
+            for j, i in zip(row, row[1:]):
+                ops[i]["dep"].setdefault(j, False)
         gap = lambda j, wait: ops[j]["lat"] + HOP if wait else ops[j]["busy"]
-        rank_, succ = [0.0] * n, [[] for _ in range(n)]
+        succ = [[] for _ in range(n)]
         for i in range(n):
             for j, wait in ops[i]["dep"].items():
                 succ[j].append((i, wait))
-        for j in range(n - 1, -1, -1):
-            rank_[j] = max([ops[j]["lat"]] + [gap(j, wait) + rank_[i] for i, wait in succ[j]])
 
         def place(order, links):
             at0, lanes = [0.0] * n, {q: [] for q in Q}
             for i in order:
                 at = max([0.0] + links(i, at0))
-                lane_, pos, busy = lanes[ops[i]["q"]], 0, ops[i]["busy"]
-                for a, b in lane_:
-                    if at + busy <= a:
-                        break
-                    at = max(at, b)
+                lane_, busy = lanes[ops[i]["q"]], ops[i]["busy"]
+                pos = len(lane_)
+                while pos > 0 and lane_[pos - 1][1] > at:
+                    pos -= 1
+                while pos < len(lane_) and at + busy > lane_[pos][0]:
+                    at = max(at, lane_[pos][1])
                     pos += 1
                 lane_.insert(pos, (at, at + busy))
                 at0[i] = at
@@ -101,19 +143,37 @@ def rank_program(g, core, T, topo):
 
         def ahead(i, at0): return [at0[j] + gap(j, wait) for j, wait in ops[i]["dep"].items()]
 
-        def behind(j, at0):
-            return [ops[j]["lat"] - ops[j]["busy"]] + [at0[i] + ops[i]["busy"] + gap(j, wait) - ops[j]["busy"] for i, wait in succ[j]]
+        key = list(range(n))
+        for j in range(closer["steps"] - 1, -1, -1):
+            key[j] = min([n] + [key[i] for i, wait in succ[j]])
+        order, done = [], [False] * n
 
-        order, best = list(range(n)), None
-        for _ in range(ROUNDS):
-            fw = place(order, ahead)
-            span = max(fw[i] + ops[i]["lat"] for i in range(n))
-            if best is None or span < best:
-                best, start = span, fw
-            bw = place(sorted(range(n), key=lambda i: (-fw[i] - ops[i]["busy"], -i)), behind)
-            order = sorted(range(n), key=lambda i: (-bw[i] - ops[i]["busy"], i))
+        def visit(i):
+            todo = [i]
+            while todo:
+                k = todo[-1]
+                ahead_ = [j for j in ops[k]["dep"] if not done[j]]
+                if ahead_:
+                    todo.append(min(ahead_))
+                    assert len(todo) <= n
+                else:
+                    todo.pop()
+                    if not done[k]:
+                        done[k] = True
+                        order.append(k)
+
+        for i in sorted(range(n), key=lambda i: (key[i], i)):
+            visit(i)
+        start = place(order, ahead)
+        rank_ = {i: k for k, i in enumerate(order)}
+        return sorted(range(n), key=lambda i: (start[i], rank_[i]))
+
+    def emit():
+        if not ORDER:
+            ORDER.extend(plan())
+        closer.update({ops[i].get("acc"): i for i in ORDER})
         cnt, seen, final, tok, nd = {q: 0 for q in Q}, {q: {} for q in Q}, {}, {}, 0
-        for i in sorted(range(n), key=lambda i: (start[i], i)):
+        for i in ORDER:
             o = ops[i]
             q, want = o["q"], {}
             for j, wait in o["dep"].items():
@@ -129,7 +189,7 @@ def rank_program(g, core, T, topo):
                 tok[i] = (q, cnt[q])
             elif o["kind"] == "dma":
                 for a, b in o["fn"]:
-                    Q[q].dma_start(a, b).then_inc(T.sem["d%d" % nd], 16)
+                    Q[q].dma_start(a["ap"], b["ap"]).then_inc(T.sem["d%d" % nd], 16)
                 tok[i] = ("d%d" % nd, 16 * len(o["fn"]))
                 nd += 1
             else:
@@ -140,197 +200,196 @@ def rank_program(g, core, T, topo):
             g.wait_ge(T.sem[s], m)
 
     v, sc, pe = g.vector, g.scalar, g.tensor
-    GATHERS = ("G0_", "G1_", "D0_", "D1_", "se", "GS", "DS", "HG", "PP", "FW", "sz", "KG", "EQ", "E2", "XG")
 
-    def cost(o, a, w, per):
-        if w in ("M", "K Kd", "X Xb"):
-            return 50.0 + a.shape[1] * SCAT * CYC
-        if w.startswith(GATHERS):
-            return 60.0 + o.shape[1] * GATH * CYC
+    def cost(o, a, per=None):
+        if "off" in o:
+            return 50.0 + o["n"] * SCAT * CYC
+        if "off" in a:
+            return 60.0 + o["n"] * GATH * CYC
         if per is None:
-            per = 0.5 if "16" in str(o.dtype) and "16" in str(a.dtype) else 1.0
-        return max(64.0, o.shape[1] * per) * CYC
+            per = 0.5 if SIZE[o["dt"]] == 2 and SIZE[a["dt"]] == 2 else 1.0
+        return max(64.0, o["n"] * per) * CYC
 
-    def tt(o, a, b, x, r, w):
-        op("v", lambda: v.tensor_tensor(o, a, b, x), r, w, cost(o, b, w, 1.0 if w[:2] in BANKS and w[2] == " " else 2.0))
+    def tt(o, a, b, x, chain=None, also=()):
+        op("v", lambda: v.tensor_tensor(ap(o), ap(a), ap(b), x), [a, b] + list(also), [o], cost(o, a, 1.0 if a.get("bank") or b.get("bank") else 2.0), chain)
 
-    def ts(o, a, s1, x, r, w): op("v", lambda: v.tensor_scalar(o, a, s1, None, x), r, w, cost(o, a, w, None))
-    def t2(o, a, s1, s2, x, y, r, w): op("v", lambda: v.tensor_scalar(o, a, s1, s2, x, y), r, w, cost(o, a, w, None))
-    def cp(o, a, r, w): op("v", lambda: v.tensor_copy(o, a), r, w, cost(o, a, w, None))
-    def ms(o, x, w): op("v", lambda: v.memset(o, x), "", w, cost(o, o, "", None))
-    def scan(o, a, b, r, w): op("v", lambda: v.tensor_tensor_scan(o, a, b, 0.0, A.add, A.min), r, w, cost(o, a, w, 1.0))
+    def ts(o, a, s1, x, chain=None): op("v", lambda: v.tensor_scalar(ap(o), ap(a), ap(s1), None, x), [a, s1], [o], cost(o, a), chain)
+    def t2(o, a, s1, s2, x, y): op("v", lambda: v.tensor_scalar(ap(o), ap(a), ap(s1), ap(s2), x, y), [a, s1, s2], [o], cost(o, a))
+    def cp(o, a): op("v", lambda: v.tensor_copy(ap(o), ap(a)), [a], [o], cost(o, a))
+    def ms(o, x): op("v", lambda: v.memset(ap(o), x), [], [o], cost(o, o))
+    def scan(o, a, b, x, y, also=()):
+        op("v", lambda: v.tensor_tensor_scan(ap(o), ap(a), ap(b), 0.0, x, y), [a, b] + list(also), [o], cost(o, a, 1.0))
 
-    def act(o, a, f, r, w, bias=0.0, scale=1.0):
-        op("s", lambda: sc.activation(o, a, f, bias=bias, scale=scale), r, w, cost(o, a, w, 1.0))
+    def act(o, a, f, bias=0.0, scale=1.0, chain=None, also=()):
+        op("s", lambda: sc.activation(ap(o), ap(a), f, bias=ap(bias), scale=ap(scale)), [a, bias, scale] + list(also), [o], cost(o, a, 1.0), chain)
 
-    def lin(o, a, r, w, bias=0.0, scale=1.0): act(o, a, F.Identity, r, w, bias, scale)
+    def lin(o, a, bias=0.0, scale=1.0, chain=None, also=()): act(o, a, F.Identity, bias, scale, chain, also)
 
-    def iota(o, pat, base, cm, w, flag=True):
-        busy = 130.0 + 2 * o.shape[1] * CYC
-        if flag:
-            op("c", lambda: g.iota(o, pat, base, cm, allow_small_or_imprecise_dtypes=True), "", w, busy)
+    def iota(o, pat, base, cm=0):
+        if o["dt"] == i32:
+            op("c", lambda: g.iota(ap(o), pat, base, cm), [], [o], 160.0 + 2 * o["n"] * CYC)
         else:
-            op("c", lambda: g.iota(o, pat, base, cm), "", w, busy)
+            op("c", lambda: g.iota(ap(o), pat, base, cm, allow_small_or_imprecise_dtypes=True), [], [o], 160.0 + 2 * o["n"] * CYC)
 
-    def mm(lst, r, w, start=True, stop=True):
-        def fn():
-            ins = None
-            for j, (o, l, x) in enumerate(lst):
-                ins = pe.matmul(o, l, x, start and j == 0, stop and j == len(lst) - 1)
-            return ins
-        op("p", fn, r, w, sum(max(min(64, l.shape[1]), x.shape[1]) * (1 if "16" in str(x.dtype) else 4) * PEC for o, l, x in lst))
+    def mm(lst, start=True, stop=True, part=8, acc=None, chain=None, also=()):
+        for a in range(0, len(lst), part):
+            def fn(a=a, me=len(ops)):
+                ins, end = None, min(a + part, len(lst))
+                for j in range(a, end):
+                    o, l, x = lst[j]
+                    last = (closer[acc] == me and j == end - 1) if acc else (stop and j == len(lst) - 1)
+                    ins = pe.matmul(ap(o), ap(l), ap(x), start and not acc and j == 0, last)
+                return ins
+            sub = lst[a:a + part]
+            op("p", fn, [x for o, l, r in sub for x in (l, r)] + list(also), [dict(sub[0][0], acc=acc)],
+               sum(max(min(64, l["n"]), x["n"]) * (1 if SIZE[x["dt"]] == 2 else 4) * PEC for o, l, x in sub), chain)
+            ops[-1]["acc"] = acc
 
-    def r2l(o, B, off, X, a, b):
-        return [(o, B[:, off + 15 - r:off + 143 - r], X[:, a + r:b:16]) for r in range(16)]
+    def r2l(o, wt, off, X, a, b):
+        return [(o, B(wt, off + 15 - r, off + 143 - r), B(X, a + r, b, 16)) for r in range(16)]
 
-    P = [T["P%d" % b] for b in range(8)]
-    Gb, Db, Zb = [T.G0, T.G1], [T.D0, T.D1], [T.Z0, T.Z1, T.Z2]
-    def cl(j): return T.col[:, j:j + 1]
-    def oh(q, big=0): return T.OH[:, 16 * big + q:16 * big + q + 1]
-    def st(a, n=16): return T.stt[:, a:a + n]
-    QF, G15, GF, WX, WY, WN, WU, WE, WH, H16, SC0, SC1, TW6, TW3, NQ, G23, N8, N16, JA, JB = range(20)
-    bABS, bREL, bDEL, bX, bY, bN, bU, bE, bH = [144 * j for j in range(9)]
-    I1, I46, ILV, IM, IP, I16, I256 = [T.ID[:, 128 * j:128 * j + 128] for j in range(7)]
-    SDUM, SADD, SZ1, SZ2, SV, STT = 0, 16, 64, 80, 96, 144
-    lane = T.cpb[:, 2048:2304]
+    def P(j, a, b, step=1): return B("P%d" % j, a, b, step)
+    def cl(j): return B("col", j)
+    def oh(q, big=0): return B("OH", 16 * big + q)
+    def st(a, n=16): return B("stt", a, a + n)
+    def blk(X, t): return B(X, 256 * t, 256 * t + 256)
+    QF, G15, GF, WX, WY, WN, WU, WH, H16, SC0, SC1, TW6, TW3, NQ, G23, JA, JB, WE, Q8, QB, DUM = list(range(18)) + [18, 21, 24]
+    bABS, bREL, bDEL, bX, bY, bN, bU, bH, bONE, bE, bO = [144 * j for j in range(11)]
+    IDS = (1.0, -float(2 ** 27), -1.0, 1.0 / 64, 8192.0, -16.0, 16.0, 0.5, -0.25, 1.0 / 16, -1.0 / 64, -2048.0, 256.0, 4608.0, -9216.0)
+    (I1, ILV, IM1, I64TH, I8K, IM16, I16, IHALF, IQRT, I16TH, IM64TH, IM2K, I256, I46,
+     IM92) = [B("ID", 128 * j, 128 * j + 128) for j in range(len(IDS))]
+    SADD, SLIM, SV, STT, SFB = 0, 32, 64, 112, 160
+    lane, one16 = B("cpb", 2048, 2304), B("on", 0, 16)
 
-    dma("y", [(T.cin[:, 0:256], T.own[0:8, :]), (T.cin[:, 256:512], T.own[8:16, :])], "", "cin")
-    dma("s", [(T.ELi[:, 0:256], T.ends[:, 0:256])], "", "ELi0")
-    dma("s", [(Zb[0][:, 0:256], T.st[:, 0:256])], "", "Z0")
-    dma("y", [(T.Mw[:, 0:W], T.msg[:, :])], "", "M", 2 ** 19)
-    dma("s", [(T.cin[:, 512:768], T.enc[:, :])] + [(T.thi[0:48, 16 * q:16 * q + 16], T.th[q, :]) for q in range(8)], "", "thi cin2")
-    iota(T.coli[:, 0:1], [[0, 1]], 0, 1, "coli", False)
-    iota(lane, [[1, 256]], 0, 0, "cpl")
-    iota(T.n143[:, :], [[1, 144]], 0, 0, "n143")
-    iota(T.one[:, :], [[0, 144]], 1, 0, "one")
-    op("c", lambda: g.affine_select(T.IF[:, :], T.one[:, 0:128], [[-1, 128]], A.is_equal, 0.0, 0, 1), "one", "IF", 440.0)
+    dma("y", [(B("cin", 0, 256), H(T.own[0:8, :], i32))])
+    dma("s", [(B("cin", 256, 512), H(T.own[8:16, :], i32))], 2 ** 17)
+    dma("y", [(B("ELi", 0, 256), H(T.ends[:, 0:256], i32)), (blk("Z0", 0), H(T.st[:, 0:256], bf))], 2 ** 18)
+    dma("y", [(B("Mw", 0, W), H(T.msg[:, :], bf))], 2 ** 19)
+    iota(B("coli", 0), [[0, 1]], 0, 1)
+    iota(lane, [[1, 256]], 0)
+    iota(B("n143"), [[1, 144]], 0)
+    iota(B("one"), [[0, 128]], 1)
+    op("c", lambda: g.affine_select(T.IF[:, :], T.one[:, :], [[-1, 128]], A.is_equal, 0.0, 0, 1), [B("one")], [B("IF")], 480.0)
+    iota(B("NB", 0, 256), [[0, 16], [-16, 16]], 0)
+    iota(B("NB", 256, 512), [[0, 16], [-16, 16]], -8)
+    iota(B("kc"), [[256, 16], [16, 16]], 0)
     for b in range(3):
-        iota(T.prR[:, 288 * b:288 * b + 272], [[1, 16], [16, 17]], -16, 0, "prR%d" % b)
-        iota(T.prR[:, 288 * b + 272:288 * b + 288], [[0, 16]], 0, 0, "prQ%d" % b)
-    for b in range(3):
-        iota(T.prR[:, 288 * b:288 * b + 272:17], [[1, 16]], 256 + 16 * b, 0, "prR%d" % b)
-    PRR = "prR0 prR1 prR2 prQ0 prQ1 prQ2"
-    iota(T.NB[:, 0:512], [[0, 32], [-16, 16]], 0, 0, "NB0")
-    iota(T.kc[:, :], [[256, 16], [16, 16]], 0, 0, "kc")
-    iota(st(STT, 48), [[0, 3], [16, 16]], -4096, 0, "st4")
-    iota(T.nd16[:, :], [[1, 8], [0, 16]], 0, 0, "nd16")
-    iota(T.rr[:, :], [[0, 16], [1, 16]], 0, 0, "rr")
-    iota(T.cc[:, :], [[1, 16], [0, 16]], 0, 0, "cc")
-    iota(st(SDUM), [[16, 16]], 4352, 0, "st0")
-    iota(st(SADD), [[0, 16]], 0, 0, "st1a")
-    iota(st(SADD + 16), [[32, 16]], 7680, 0, "st1b")
-    iota(st(SADD + 32), [[16, 16]], 3840, 0, "st1c")
-    iota(st(SZ1), [[16, 16]], 4096, 0, "st2a")
-    iota(st(SZ2), [[16, 16]], 4352 - 8192, 0, "st2b")
-    iota(st(SV, 48), [[16, 48]], 0, 0, "st3")
-    iota(T.cxi[:, 0:16], [[1, 16]], 0, 0, "cxi", False)
-    iota(T.cxi[:, 16:24], [[2, 8]], 0, 0, "cxj", False)
-    for b in (1, 2):
-        iota(T.NB[:, 512 * b:512 * b + 512], [[0, 32], [-16, 16]], -256 * b, 0, "NB%d" % b)
+        iota(B("prR", 288 * b, 288 * b + 272), [[1, 16], [-16, 17]], 256)
+        iota(B("prR", 288 * b + 272, 288 * b + 288), [[0, 16]], 0)
+        if b:
+            iota(B("prR", 288 * b, 288 * b + 272, 17), [[1, 16]], 256 + 16 * b)
+    iota(st(STT, 48), [[0, 3], [16, 16]], -4096)
+    iota(B("dJ"), [[-16, 16], [256, 17]], -4096)
+    iota(B("nd16"), [[1, 8], [0, 16]], 0)
+    iota(B("rr"), [[0, 16], [1, 16]], 0)
+    iota(B("cc"), [[1, 16], [0, 16]], 0)
+    iota(st(SADD + 16), [[32, 16]], 0)
+    iota(st(SLIM, 32), [[-256, 2], [16, 16]], 4352)
+    iota(st(SV, 48), [[512, 3], [16, 16]], 0, 0)
+    iota(st(SFB), [[-8192, 16]], -8192)
+    iota(B("cxi"), [[1, 16]], 0)
+    iota(B("on"), [[0, 256]], 1)
 
-    ms(T.Xw[:, :], 0.0, "X Xb")
-    ts(T.coli[:, 1:2], T.coli[:, 0:1], 15, A.bitwise_and, "coli", "coli1")
-    ts(T.coli[:, 2:3], T.coli[:, 0:1], 4, A.arith_shift_right, "coli", "coli2")
-    cp(cl(QF), T.coli[:, 1:2], "coli1", "qf")
-    t2(cl(G15), T.coli[:, 2:3], 16.0, 15.0, A.mult, A.add, "coli2", "g15")
-    lin(T.cpb[:, 1792:2048], lane, "cpl qf", "cph", cl(QF), 0.0)
-    ts(T.cpi[:, 0:256], T.cin[:, 0:256], 15, A.bitwise_and, "cin", "cpi0")
-    t2(T.cpi[:, 256:512], T.cin[:, 0:256], 4, 15, A.arith_shift_right, A.bitwise_and, "cin", "cpi1")
-    ts(T.cpi[:, 512:1024], T.cin[:, 0:512], 8, A.arith_shift_right, "cin", "cpi2")
-    ts(T.cpi[:, 1024:1280], T.cin[:, 256:512], 255, A.bitwise_and, "cin", "cpi3")
-    cp(T.cpb[:, 0:1280], T.cpi[:, 0:1280], "cpi0 cpi1 cpi2 cpi3", "cpb")
-    rows = [(0, 0), (1, 256), (6, 512), (3, 768), (2, 1024), (4, 1792), (5, 2048)]
-    dma("s", [(T.Xw[q::16, 0:W], T.cpb[:, a:a + 256]) for q, a in rows[5:]], "cph cpl", "Xb")
-    dma("y", [(T.Xw[q::16, 0:W], T.cpb[:, a:a + 256]) for q, a in rows[:5]], "cpb", "X", 2 ** 19)
-    dma("y", [(T.Kw[:, 0:W], T.msg[:, :])], "X Xb", "K")
-    dma("y", [(T.ELi[:, 256:V], T.ends[:, 256:V])], "", "ELi1", 2 ** 20)
-    for b in (1, 2):
-        dma("y", [(Zb[b][:, 256 * j:256 * j + 256], T.st[:, 256 * b:256 * b + 256]) for j in range(REP)], "", "Z%d Zr%d" % (b, b), 2 ** 21)
-    cp(T.ELu[:, 0:256], T.ELi[:, 0:256], "ELi0", "ELu0")
-    ts(T.BF[:, :], T.n143[:, :], cl(G15), A.is_equal, "n143 g15", "BF")
-    mm(r2l(P[7][:, 0:54], T.BF, 0, T.prR, 0, 864), "BF " + PRR, "b7")
-    ts(T.OH[:, 0:16], T.n143[:, 0:16], cl(QF), A.is_equal, "n143 qf", "oh")
-    t2(T.OH[:, 16:32], T.n143[:, 0:16], cl(QF), 256.0, A.is_equal, A.mult, "n143 qf", "oi")
-    ts(cl(NQ), cl(QF), -1.0, A.mult, "qf", "nq")
-    cp(cl(GF), T.coli[:, 2:3], "coli2", "gf")
-    t2(cl(WX), oh(1), 16.0, oh(0), A.mult, A.add, "oh", "wx")
-    tt(cl(WY), oh(2), oh(3, 1), A.add, "oh oi", "wy")
-    tt(cl(WN), oh(5), oh(4, 1), A.add, "oh oi", "wn")
-    tt(cl(WX), cl(WX), oh(6, 1), A.add, "wx oi", "wx")
-    tt(cl(WH), oh(1), oh(6, 1), A.add, "oh oi", "wh")
-    t2(cl(WE), oh(4), oh(5), 4608.0, A.add, A.mult, "oh", "we")
-    tt(cl(WU), cl(WX), cl(WY), A.add, "wx wy", "wu")
-    ts(cl(H16), oh(4), 16.0, A.mult, "oh", "h16")
-    ts(cl(TW6), oh(6), 2.0, A.mult, "oh", "tw6")
-    ts(cl(TW3), oh(3), 2.0, A.mult, "oh", "tw3")
-    ts(cl(SC0), cl(WX), 0.0, A.is_equal, "wx", "sc0")
-    ts(cl(SC1), cl(WY), 0.0, A.is_equal, "wy", "sc1")
-    for j, x in enumerate((1.0, 4608.0, -float(2 ** 27), -32.0, 32.0, 16.0, 256.0)):
-        lin(T.ID[:, 128 * j:128 * j + 128], T.IF[:, :], "IF", "ID%d" % j, 0.0, x)
-    ts(T.coli[:, 3:4], T.coli[:, 0:1], 7, A.bitwise_and, "coli", "coli3")
-    ts(cl(G23), cl(G15), 8.0, A.add, "g15", "g23")
-    ts(cl(N8), T.coli[:, 3:4], -1.0, A.mult, "coli3", "n8")
-    t2(T.BY[:, :], T.n143[:, :], cl(G23), cl(WY), A.is_equal, A.mult, "n143 g23 wy", "BY")
-    ts(cl(N16), cl(N8), -8.0, A.add, "n8", "n16")
-    t2(cl(JA), cl(G15), -15.0, cl(N8), A.add, A.subtract, "g15 n8", "ja")
-    t2(cl(JB), cl(G15), -15.0, cl(N16), A.add, A.subtract, "g15 n16", "jb")
-    lin(T.BA[:, bY:bY + 144], T.BF[:, :], "BF wx", "BX", 0.0, cl(WX))
-    ts(T.JP[:, 0:128], T.n143[:, 0:128], cl(JA), A.is_equal, "n143 ja", "JA")
-    ts(T.JP[:, 128:256], T.n143[:, 0:128], cl(JB), A.is_equal, "n143 jb", "JB")
-    tt(T.BA[:, bX:bX + 144], T.BA[:, bY:bY + 144], T.BY[:, :], A.add, "BX BY", "BA%d" % bX)
-    lin(T.NR[:, 0:256], lane, "cpl n8", "NR", cl(N8), 0.0)
-    lin(T.NR[:, 256:512], lane, "cpl n16", "NS", cl(N16), 0.0)
-    lin(T.NQR[:, :], lane[:, 0:16], "cpl nq", "NQR", cl(NQ), 0.0)
-    for off, x, r in ((bREL, 16384.0, ""), (bDEL, -8192.0, ""), (bABS, 8192.0, ""),
-                      (bN, cl(WN), "wn"), (bU, cl(WU), "wu"), (bE, cl(WE), "we"), (bH, cl(WH), "wh")):
-        lin(T.BA[:, off:off + 144], T.BF[:, :], "BF " + r, "BA%d" % off, 0.0, x)
+    ms(B("Xw"), 0.0)
+    ts(B("coli", 4), B("coli", 0), 15, A.bitwise_and)
+    ts(B("coli", 5), B("coli", 0), 4, A.arith_shift_right)
+    ts(B("coli", 6), B("coli", 0), 7, A.bitwise_and)
+    cp(cl(QF), B("coli", 4))
+    t2(cl(G15), B("coli", 5), 16.0, 15.0, A.mult, A.add)
+    lin(B("cpb", 1792, 2048), lane, cl(QF), 0.0)
+    def piece(X, q): return B(X, 0, W, 1, (q, 128, 16))
+    dma("s", [(piece("Xw", q), B("cpb", a, a + 256)) for q, a in ((4, 1792), (5, 2048))], 2 ** 20)
+    ts(B("cpi", 0, 256), B("cin", 0, 256), 15, A.bitwise_and, "#v")
+    t2(B("cpi", 256, 512), B("cin", 0, 256), 4, 15, A.arith_shift_right, A.bitwise_and)
+    ts(B("cpi", 512, 768), B("cin", 0, 256), 8, A.arith_shift_right, "#v")
+    cp(B("cpb", 768, 1024), B("cin", 256, 512))
+    cp(B("cpb", 0, 768), B("cpi", 0, 768))
+    tt(B("cpb", 1024, 1280), B("cin", 256, 512), B("cpb", 768, 1024), A.subtract, "#v")
+    dma("y", [(piece("Xw", q), B("cpb", a, a + 256)) for q, a in ((0, 0), (1, 256), (6, 512))], 2 ** 19)
+    dma("s", [(piece("Xw", q), B("cpb", a, a + 256)) for q, a in ((3, 768), (2, 1024))], 2 ** 19)
     for j in range(1, REP):
-        cp(Zb[0][:, 256 * j:256 * j + 256], Zb[0][:, 0:256], "Z0", "Zr0")
-    ms(T.FW[:, :], -1.0, "FW")
-    ms(T.d0f[:, :], 0.0, "d0f")
-    for j, x in enumerate((0.0, -512.0, -256.0)):
-        ms(T.d0k[:, 272 * j:272 * j + 272], x, "d0k%d" % j)
-    ms(T.d0f[:, 0:272:17], BIG, "d0f")
-    ms(T.d0k[:, 0:816:17], BIG, "d0k0 d0k1 d0k2")
-    ms(T.c92[:, :], -9216.0, "c92")
-    ms(T.d0k[:, 1:816:17], BIG, "d0k0 d0k1 d0k2")
-    for j, X in enumerate((T.G0, T.G1)):
-        ms(X[:, W + 256:W + 512], 0.0, "Gz%d" % j)
-    for j, X in enumerate((T.D0, T.D1)):
-        ms(X[:, W:W + 256], 0.0, "Dz%d" % j)
-    ms(T.TM[:, 256:384], 0.0, "TMb")
-    for X, w in ((T.G0, "Gd0"), (T.G1, "Gd1"), (T.Kw, "Kd")):
-        lin(X[:, W:W + 256], lane, "cpl oh h16", w, cl(H16), oh(5))
-    ts(st(STT, 48), st(STT, 48), -float(2 ** 27), A.add, "st4", "st4")
-    ts(T.prm[:, :], P[7][:, 0:54], 1.0 / 16, A.mult, "", "b7 prm")
-
-    def mid_setup():
-        cp(T.thf[0:48, :], T.thi[0:48, :], "thi M", "thf")
-        mm([(P[6][:, 0:48], T.thf[0:48, :], T.IF[0:48, 0:48])], "IF thf", "b6")
-        ts(T.cpi[:, 1280:1536], T.cin[:, 512:768], 8, A.arith_shift_right, "cin2 M", "cpk0")
-        ts(T.cpi[:, 1536:1792], T.cin[:, 512:768], 255, A.bitwise_and, "cin2 M", "cpk1")
-        cp(T.cpb[:, 1280:1792], T.cpi[:, 1280:1792], "cpk0 cpk1", "cpk")
-        dma("y", [(T.Kw[4::16, 0:W], T.cpb[:, 1280:1536]), (T.Kw[5::16, 0:W], T.cpb[:, 1536:1792])], "cpk", "K")
-        ts(T.TL[:, :], P[6][:, 0:48], 8192.0, A.mult, "", "b6 TL")
-        tt(T.PS[:, 256:304], T.TL[:, :], st(STT, 48), A.add, "TL st4", "TT0 TT1 TT2")
-
-    def late_setup():
-        t2(T.RP[:, 0:128], T.nd16[:, :], cl(GF), cl(WN), A.is_equal, A.mult, "nd16 gf wn", "RP0")
-        t2(T.RP[:, 128:256], T.nd16[:, :], cl(GF), oh(0), A.is_equal, A.mult, "nd16 gf oh", "RP1")
-        ts(st(SV, 48), st(SV, 48), cl(QF), A.add, "st3 qf", "st3")
-        t2(T.TM[:, 0:256], T.rr[:, :], cl(QF), 8192.0, A.is_le, A.mult, "rr qf", "TM")
-        ts(st(SDUM), st(SDUM), cl(QF), A.add, "st0 qf", "st0")
-        cp(T.cx[:, :], T.cxi[:, :], "cxi cxj", "cx")
-        ts(T.VP[:, 512:768], T.cc[:, :], oh(1), A.mult, "cc oh", "VP2")
-        ts(T.VP[:, 0:256], T.rr[:, :], oh(0), A.mult, "rr oh", "VP")
-        ts(T.VP[:, 256:512], lane, oh(2), A.mult, "cpl oh", "VP1")
-        tt(T.VP[:, 0:256], T.VP[:, 0:256], T.VP[:, 512:768], A.add, "VP VP2", "VP")
-
-    def late_lists():
-        cp(T.ELu[:, 256:V], T.ELi[:, 256:V], "ELi1", "ELu1 ELu2")
-
-    def late_out():
-        cp(T.ELf[:, :], T.ELi[:, :], "ELi0 ELi1", "ELf")
+        lin(blk("Z0", j), blk("Z0", 0))
+    dma("y", [(B("thi", 16 * q, 16 * q + 16, 1, (0, 48, 1)), dict(H(T.th[q, :], i32), n=6)) for q in range(8)]
+        + [(B("cin", 512, 768), H(T.enc[:, :], i32))], 0, [B("Xw")])
+    dma("y", [(B("Kw", 0, W), H(T.msg[:, :], bf))], 2 ** 17)
+    dma("y", [(B("ELi", 256, V), H(T.ends[:, 256:V], i32))], 2 ** 20)
+    for b in (1, 2):
+        dma("y", [(blk("Z%d" % b, j), H(T.st[:, 256 * b:256 * b + 256], bf)) for j in range(REP)], 2 ** 21)
+    cp(B("ELu", 0, 256), B("ELi", 0, 256))
+    ts(B("BF"), B("n143"), cl(G15), A.is_equal)
+    mm(r2l(P(7, 0, 54), "BF", 0, "prR", 0, 864))
+    ts(B("OH", 0, 16), B("n143", 0, 16), cl(QF), A.is_equal)
+    t2(B("OH", 16, 32), B("n143", 0, 16), cl(QF), 256.0, A.is_equal, A.mult)
+    ts(cl(NQ), cl(QF), -1.0, A.mult)
+    cp(cl(GF), B("coli", 5))
+    t2(cl(WX), oh(1), 16.0, oh(0), A.mult, A.add)
+    tt(cl(WY), oh(2), oh(3), A.add)
+    tt(cl(WN), oh(5), oh(4, 1), A.add)
+    tt(cl(WX), cl(WX), oh(6, 1), A.add)
+    tt(cl(WH), oh(1), oh(6, 1), A.add)
+    tt(cl(WU), cl(WX), cl(WY), A.add)
+    ts(cl(H16), oh(4), 16.0, A.mult)
+    ts(cl(TW6), oh(6), 2.0, A.mult)
+    ts(cl(TW3), oh(3), 512.0, A.mult)
+    ts(cl(SC0), cl(WX), 0.0, A.is_equal)
+    ts(cl(SC1), cl(WY), 0.0, A.is_equal)
+    ts(cl(DUM), cl(QF), 4096.0, A.add)
+    ts(cl(DUM + 1), cl(QF), 4112.0, A.add)
+    cp(B("col", 31), B("coli", 6))
+    ts(B("col", Q8, Q8 + 3), B("kc", 0, 48, 16), B("col", 31), A.add)
+    ts(B("col", QB, QB + 3), B("kc", 0, 48, 16), cl(QF), A.add)
+    for j, x in enumerate(IDS):
+        lin(B("ID", 128 * j, 128 * j + 128), B("IF"), 0.0, x)
+    ts(cl(G23), cl(G15), 8.0, A.add)
+    t2(B("BY"), B("n143"), cl(G23), cl(WY), A.is_equal, A.mult)
+    t2(cl(JA), cl(G15), -15.0, B("col", 31), A.add, A.add)
+    ts(cl(JB), cl(JA), 8.0, A.add)
+    lin(B("BA", bY, bY + 144), B("BF"), 0.0, cl(WX))
+    ts(B("JP", 0, 128), B("n143", 0, 128), cl(JA), A.is_equal)
+    ts(B("JP", 128, 256), B("n143", 0, 128), cl(JB), A.is_equal)
+    tt(B("BA", bX, bX + 144), B("BA", bY, bY + 144), B("BY"), A.add)
+    for off, x in ((bREL, 16384.0), (bDEL, -8192.0), (bABS, 8192.0), (bONE, 1.0), (bN, cl(WN)), (bU, cl(WU)), (bH, cl(WH)), (bO, cl(WY))):
+        lin(B("BA", off, off + 144), B("BF"), 0.0, x)
+    ms(B("FW"), -1.0)
+    ms(B("d0f"), 0.0)
+    ms(B("d0k", 0, 272), 0.0)
+    ms(B("d0k", 272, 544), 512.0)
+    ms(B("d0f", 0, 272, 17), BIG)
+    ms(B("d0k", 0, 544, 17), BIG)
+    ms(B("d0k", 1, 544, 17), BIG)
+    ms(st(SADD), -float(2 ** 26))
+    ms(B("PS", KL, 256), BIG)
+    for X in ("D0", "D1"):
+        ms(B(X, W, W + 256), 0.0)
+    ms(B("Kw", W, W + 256), 0.0)
+    for X in ("G0", "G1"):
+        lin(B(X, W, W + 256), lane, cl(H16), oh(5))
+    ts(st(STT, 48), st(STT, 48), -float(2 ** 27), A.add)
+    ts(B("prm"), P(7, 0, 54), 1.0 / 16, A.mult)
+    th48 = (0, 48, 1)
+    cp(B("thf", 0, 128, 1, th48), B("thi", 0, 128, 1, th48))
+    mm([(P(6, 0, 48), B("thf", 0, 128, 1, th48), B("IF", 0, 48, 1, th48))])
+    ts(B("cpi", 1280, 1536), B("cin", 512, 768), 8, A.arith_shift_right)
+    ts(B("cpi", 1536, 1792), B("cin", 512, 768), 255, A.bitwise_and)
+    cp(B("cpb", 1280, 1792), B("cpi", 1280, 1792))
+    dma("y", [(piece("Kw", 4), B("cpb", 1280, 1536)), (piece("Kw", 5), B("cpb", 1536, 1792))])
+    ts(B("TL"), P(6, 0, 48), 8192.0, A.mult)
+    tt(B("PS", 256, 304), B("TL"), st(STT, 48), A.add)
+    t2(B("RP", 0, 128), B("nd16"), cl(GF), cl(WN), A.is_equal, A.mult)
+    t2(B("RP", 128, 256), B("nd16"), cl(GF), oh(0), A.is_equal, A.mult)
+    t2(st(SV, 48), st(SV, 48), cl(QF), cl(QF), A.add, A.add)
+    for r in range(16):
+        def fn(r=r): return g.affine_select(T.LT[:, 128 * r:128 * r + 128], T.BA[:, bABS + 15 - r:bABS + 143 - r], [[1, 128]], A.is_gt, 0.0, 0, -1)
+        op("c", fn, [B("BA", bABS, bABS + 144)], [B("LT", 128 * r, 128 * r + 128)], 170.0 + 256 * CYC)
+    t2(cl(WE), oh(4), oh(5), 4608.0, A.add, A.mult)
+    lin(B("BA", bE, bE + 144), B("BF"), 0.0, cl(WE))
+    cp(B("cx"), B("cxi"))
+    ts(B("VP", 512, 768), B("cc"), oh(1), A.mult)
+    ts(B("VP", 0, 256), B("rr"), oh(0), A.mult)
+    ts(B("VP", 256, 512), lane, oh(2), A.mult)
+    tt(B("VP", 0, 256), B("VP", 0, 256), B("VP", 512, 768), A.add)
+    cp(B("ELu", 256, V), B("ELi", 256, V))
+    ts(B("ELf"), B("ELi"), -2048.0, A.add)
 
     peers = [c for c in T.cores if c != core]
     mask = topo.mask(core, peers[0])
@@ -338,348 +397,314 @@ def rank_program(g, core, T, topo):
         mask &= topo.mask(core, c)
     ne = bin(mask).count("1")
     nsent = [0]
+    closer["steps"] = len(ops)
 
-    def send(t, dst, src, sem, r):
+    def send(t, dst, src, sem, parts):
         to = T.cores[(rank + 1 + t % (N - 1)) % N]
         rid, pid, _ = topo.addr(to)
 
         def fn():
-            g.remote_dma(dst, src, T.sem[sem], T.sem.sent, pid, rid, mask)
-            return sem, (2 * ne if sem[1] == "z" else ne)
-        lastw.setdefault("l" + sem[1:], []).append(add("c", "far", fn, r, "", 300.0, FAR + dst.shape[1] * 4.0))
+            g.remote_dma(ap(dst), ap(src), T.sem[sem], T.sem.sent, pid, rid, mask)
+            return sem, parts * ne
+        add("c", "far", fn, [src], [dst], 300.0, FAR + dst["n"] * 5.0, "#c")
         nsent[0] += ne
 
-    def si(t, j, n=1): return T.si[:, 192 * t + 16 * j:192 * t + 16 * (j + n)]
-    def sf(t, j): return T.sf[:, 256 * t + 16 * j:256 * t + 16 * j + 16]
-    def sb(t, j): return T.sb[:, 64 * t + 16 * j:64 * t + 16 * j + 16]
-    def su(t, j): return T.su[:, 128 * t + 16 * j:128 * t + 16 * j + 16]
-    def blk(X, t): return X[:, 256 * t:256 * t + 256]
-    def allg(p): return " ".join("G%d_%d" % (p, j) for j in range(len(OC)))
-    def alld(p): return " ".join("D%d_%d" % (p, j) for j in range(NC))
+    def si(t, j, n=1): return B("si", 192 * t + 16 * j, 192 * t + 16 * (j + n))
+    def sf(t, j, n=1): return B("sf", 144 * t + 16 * j, 144 * t + 16 * (j + n))
+    def sb(t, j): return B("sb", 64 * t + 16 * j, 64 * t + 16 * j + 16)
+    def sh(t, j): return B("sh", 48 * t + 16 * j, 48 * t + 16 * j + 16)
+    def su(t, j, n=1): return B("su", 128 * t + 16 * j, 128 * t + 16 * (j + n))
+    def lo(t): return B("lo", 16 * t, 16 * t + 16)
+    iK, iLF, iF, iRS, iRM, iJ, iLS, iLM, iLJ = range(9)
+    fY, fC, fU1, fU2, fOZ, fSEL, fA, fB, fE = range(9)
+    bNF, bLT, bROW = range(3)
+    hN = 0
+    uF, uE, uU, uC, uZ, uSEL, uH = range(7)
 
-    def scat_m(t): cp(T.Mw[:, :].indirect(T.lo[:, 16 * t:16 * t + 16]), blk(T.lz, t), "lz%d" % t, "M")
-    def scat_k(t): cp(T.Kw[:, :].indirect(T.lo[:, 16 * t:16 * t + 16]), blk(T.le, t), "lz%d le%d" % (t, t), "K Kd")
+    def scat(t, X, src):
+        o = ind(B(X), lo(t))
+        at("put" + X[0], t)
+        op("v", lambda: v.tensor_copy(ap(o), ap(src)), [src, blk("lz", t)], [o], cost(o, src))
 
-    def own_gather(t, j):
-        b, p, (k0, k1) = t % 3, t % 2, OC[j]
-        lin(Gb[p][:, 256 * k0:256 * k1], T.Xw[:, 0:W].indirect(T.ELu[:, 256 * b + 16 * k0:256 * b + 16 * k1]),
-            "X Xb ELu%d" % b, "G%d_%d #og" % (p, j))
+    def window(t):
+        b, p = t % 3, t % 2
+        G, D, Z = "G%d" % p, "D%d" % p, "Z%d" % b
+        def names(k0, k1): return B("ELu", 256 * b + 16 * k0, 256 * b + 16 * k1)
+        def key(a, z): return [(P(0, a, min(z, KL)), a, min(z, KL))] * (a < KL) + [(P(1, max(a, KL), z), max(a, KL), z)] * (z > KL)
+        at("", t)
+        mm([(P(2, 0, 512), I1, B("NB"))], True, False)
+        for o, a, z in key(0, 256):
+            mm([(o, I1, B("kc", a, z))], True, False)
+        for j, (k0, k1) in enumerate(OC):
+            at("own%d" % k0)
+            lin(B(G, 256 * k0, 256 * k1), ind(B("Xw", 0, W), names(k0, k1)))
+            mm([(P(2, 256 * (r // 8) + 16 * k0, 256 * (r // 8) + 16 * k1), B("BA", bX + 15 - r % 8, bX + 143 - r % 8),
+                 B(G, 256 * k0 + r, 256 * k1, 16)) for r in range(16)], False, j == len(OC) - 1)
+        if t:
+            scat(t - 1, "Mw", blk("lz", t - 1))
 
-    def own_mm(t, j):
-        b, p, (k0, k1) = t % 3, t % 2, OC[j]
-        if j < 0:
-            mm([(P[1][:, :], I1, T.NB[:, 512 * b:512 * b + 512]), (P[1][:, :], I1, T.NR[:, :])], "ID0 NR NS NB%d" % b, "b1", True, False)
-            return
-        lst = [(P[1][:, 256 * (r // 8) + 16 * k0:256 * (r // 8) + 16 * k1], T.BA[:, bX + 15 - r % 8:bX + 143 - r % 8],
-                Gb[p][:, 256 * k0 + r:256 * k1:16]) for r in range(16)]
-        mm(lst, "G%d_%d BA%d" % (p, j, bX), "b1", False, j == len(OC) - 1)
+        def live():
+            ts(B("pr"), P(2, 0, 512), B("col", Q8 + b), A.is_equal)
+            mm([(P(3, 0, 256), B("JP", 0, 128), B("pr", 0, 256)), (P(3, 0, 256), B("JP", 128, 256), B("pr", 256, 512))])
 
-    def diff(t, j):
-        b, p, (k0, k1) = t % 3, t % 2, CH[j]
-        tt(Db[p][:, 256 * k0:256 * k1], T.Mw[:, 0:W].indirect(T.ELu[:, 256 * b + 16 * k0:256 * b + 16 * k1]),
-           Zb[b][:, 0:256 * (k1 - k0)], A.subtract, "M Z%d Zr%d ELu%d" % (b, b, b), "D%d_%d #df" % (p, j))
+        def sign():
+            act(B("lv"), P(3, 0, 256), F.Sign)
+            for o, a, z in key(0, 256):
+                mm([(o, ILV, B("lv", a, z))], acc=(t, a < KL))
 
-    def fold(t, j):
-        p, (k0, k1) = t % 2, CH[j]
-        o, a, r, w = T.AB[:, 256 * k0:256 * k1], Db[p][:, 256 * k0:256 * k1], "D%d_%d" % (p, j), "AB%d" % j
-        if j < RELU:
-            ts(o, a, 0.0, A.max, r, w)
-        else:
-            act(o, a, F.Abs, r, w)
+        def least():
+            lin(B("PS", 0, KL), P(0, 0, KL))
+            lin(B("PP%d" % p), ind(B("PS"), B("prm", 18 * b, 18 * b + 17)))
+            scan(B("SF"), B("d0f"), B("PP%d" % p), A.add, A.min)
 
-    def dist_a(t, j):
-        p, (k0, k1) = t % 2, CH[j]
-        lst = [(P[0][:, 0:KL], I1, T.kc[:, 0:KL])] if j == 0 else []
-        if j < RELU:
-            lst += r2l(P[0][:, 16 * k0:16 * k1], T.BA, bDEL, Db[p], 256 * k0, 256 * k1)
-        if lst:
-            mm(lst, "D%d_%d ID0 kc BA%d" % (p, j, bDEL), "b0", j == 0, False)
+        def stream(what, k0, k1):
+            o, a = B("AB", 256 * k0, 256 * k1), B(D, 256 * k0, 256 * k1)
+            at(what + "%d" % k0 * (k1 > 0), t)
+            if what == "diff":
+                tt(a, ind(B("Mw", 0, W), names(k0, k1)), B(Z, 0, 256 * (k1 - k0)), A.subtract)
+            elif what in ("relu", "abs"):
+                if what == "relu":
+                    at("diff%d" % k0)
+                    for ko, a0, z0 in key(16 * k0, 16 * k1):
+                        mm(r2l(ko, "BA", bDEL, D, 16 * a0, 16 * z0), acc=(t, a0 < KL))
+                    at("relu%d" % k0)
+                    ts(o, a, 0.0, A.max)
+                else:
+                    act(o, a, F.Abs)
+                for ko, a0, z0 in key(16 * k0, 16 * k1):
+                    mm(r2l(ko, "BA", bREL if what == "relu" else bABS, "AB", 16 * a0, 16 * z0), acc=(t, a0 < KL))
+            else:
+                {"live": live, "sign": sign, "least": least}[what]()
 
-    def dist_b(t, j):
-        k0, k1 = CH[j]
-        off = bREL if j < RELU else bABS
-        bank = 4 if j == NC - 1 else 0
-        mm(r2l(P[bank][:, 16 * k0:16 * k1], T.BA, off, T.AB, 256 * k0, 256 * k1), "AB%d BA%d" % (j, off), "b%d" % bank, False, bank == 4)
-
-    def live(t):
-        ts(T.pr[:, :], P[1][:, :], 0.0, A.is_equal, "", "b1 pr")
-        mm([(P[2][:, 0:256], T.JP[:, 0:128], T.pr[:, 0:256]), (P[2][:, 0:256], T.JP[:, 128:256], T.pr[:, 256:512])], "pr JA JB", "b2")
-
-    def live_s(t): act(T.lv[:, :], P[2][:, 0:256], F.Sign, "", "b2 lv")
-
-    def live_mm(t):
-        mm([(P[0][:, 0:KL], ILV, T.lv[:, 0:KL])], "lv ID2", "b0", False, True)
-        mm([(P[4][:, KL:256], I1, T.kc[:, KL:256]), (P[4][:, KL:256], ILV, T.lv[:, KL:256])], "lv kc ID0 ID2", "b4", True, False)
-
-    def rows_of(t, part):
-        if part == 0:
-            tt(si(t, 2, 3), T.SK[:, 16:816:17], st(SADD, 48), A.add, "SK st1a st1b st1c", "raw%d" % t)
-            tt(sf(t, 6), sf(t, 1), st(SZ2), A.add, "fl%d st2b" % t, "b_%d" % t)
-        elif part == 1:
-            ts(si(t, 5, 2), si(t, 2, 2), 4095, A.bitwise_and, "raw%d" % t, "low%d" % t)
-            tt(sf(t, 5), si(t, 4), st(SZ1), A.min, "raw%d st2a" % t, "a%d" % t)
-            ts(su(t, 4), si(t, 6), cl(QF), A.add, "low%d qf" % t, "om%d" % t)
-            tt(sf(t, 6), sf(t, 6), si(t, 5), A.max, "b_%d low%d" % (t, t), "b_%d" % t)
-        else:
-            tt(sf(t, 5), sf(t, 5), sf(t, 6), A.max, "a%d b_%d" % (t, t), "a%d" % t)
-            ts(su(t, 5), sf(t, 5), cl(QF), A.add, "a%d qf" % t, "oz%d" % t)
-
-    def rows_late(t):
-        b = t % 3
-        tt(sf(t, 7), si(t, 5), sf(t, 1), A.subtract, "low%d fl%d" % (t, t), "c%d" % t)
-        t2(sf(t, 8), si(t, 4), float(2 ** 20), float(2 ** 22), A.is_lt, A.mult, "raw%d" % t, "d%d" % t)
-        t2(sf(t, 2), si(t, 1), 4096.0, 524288.0, A.is_ge, A.mult, "lf%d" % t, "fm%d" % t)
-        tt(sf(t, 7), sf(t, 7), si(t, 4), A.max, "c%d raw%d" % (t, t), "c%d" % t)
-        tt(sf(t, 8), sf(t, 8), si(t, 1), A.add, "d%d lf%d" % (t, t), "d%d" % t)
-        tt(T.PS[:, 256 + 16 * b:272 + 16 * b], T.PS[:, 256 + 16 * b:272 + 16 * b], sf(t, 2), A.add, "TT%d fm%d" % (b, t), "TT%d" % b)
-        tt(sb(t, 1), sf(t, 7), sf(t, 8), A.min, "c%d d%d" % (t, t), "row%d" % t)
-
-    def em_out(t):
-        p = t % 2
-        lin(blk(T.se, t), Gb[p][:, 0:W].indirect(su(t, 4)), allg(p) + " om%d" % t, "se%d" % t)
-        send(t, blk(T.le, t), blk(T.se, t), "ae%d" % t, "se%d" % t)
-
-    def stale_gather(t):
-        p = t % 2
-        lin(T.GS[:, :], Gb[p][:, :].indirect(su(t, 5)), allg(p) + " Gd%d Gz%d oz%d" % (p, p, t), "GS")
-        lin(T.DS[:, :], Db[p][:, :].indirect(su(t, 5)), alld(p) + " Dz%d Dn%d oz%d" % (p, p, t), "DS", -0.25, 0.5)
-
-    def hop_mm(t):
-        mm(r2l(P[6][:, 256:272], T.BA, bH, T.GS, 0, 256), "GS BA%d" % bH, "b6")
-        mm([(P[6][:, 0:256], T.RP[:, 128:256], T.GS[:, :])], "GS RP1", "b6")
-
-    def state_v(t):
-        t2(T.DR[:, :], T.DS[:, :], 12582912.0, 12582912.0, A.add, A.subtract, "DS", "DR")
-
-    def state_mm(t):
-        b = t % 3
-        mm([(P[7][:, 0:256], I1, Zb[b][:, 0:256]), (P[7][:, 0:256], I1, T.DR[:, :]), (P[7][:, 0:256], I1, blk(T.sz, t))],
-           "Z%d DR sz%d ID0" % (b, t), "b7")
-
-    def state_s(t):
-        b = t % 3
-        lin(Zb[b][:, 0:256], P[7][:, 0:256], "", "b7 Z%d" % b)
-        if t + 3 < RO:
-            dma("y", [(Zb[b][:, 256 * j:256 * j + 256], Zb[b][:, 0:256]) for j in range(1, REP)], "Z%d" % b, "Zr%d" % b)
-        else:
-            dma("y", [(blk(T.yz, b), Zb[b][:, 0:256])], "Z%d" % b, "")
-
-    def hint_a(t):
-        t2(si(t, 7), si(t, 5), 4, 240, A.arith_shift_right, A.bitwise_and, "low%d" % t, "s16_%d" % t)
-        ts(T.MK[:, :], P[6][:, 0:256], cl(QF), A.is_equal, "qf", "b6 MK")
-        tt(sf(t, 9), P[6][:, 256:272], si(t, 7), A.add, "s16_%d" % t, "b6 hc%d" % t)
-
-    def hint_b(t):
-        cp(su(t, 6), sf(t, 9), "hc%d" % t, "hu%d" % t)
-        tt(T.HG[:, :], T.ELf[:, :].indirect(su(t, 6)), T.MK[:, :], A.mult, "ELf MK hu%d" % t, "HG")
-
-    def hint_mm(t): mm(r2l(P[6][:, 272:288], T.BF, 0, T.HG, 0, 256), "HG BF", "b6")
-
-    def row_mm(t):
-        mm([(P[7][:, 256:512], IM, T.kc[:, :])] + [(P[7][:, 256 + 16 * k:272 + 16 * k], IP, sb(t, 1)) for k in range(16)],
-           "kc ID3 ID4 row%d" % t, "b7")
-
-    def row_s(t):
-        act(T.AR[:, :], P[7][:, 256:512], F.Abs, "", "b7 AR", scale=1.0 / 32)
-        act(P[5][:, 256:512], P[7][:, 256:512], F.Abs, "", "b7 b5")
-
-    def name_v(t):
-        tt(sf(t, 10), P[6][:, 272:288], sf(t, 1), A.add, "fl%d" % t, "b6 nm%d" % t)
-        tt(sf(t, 10), sf(t, 10), sf(t, 4), A.min, "nm%d C%d" % (t, t), "nm%d" % t)
-        cp(sb(t, 2), sf(t, 10), "nm%d" % t, "nh%d" % t)
-        tt(sb(t, 3), sf(t, 10), sb(t, 2), A.subtract, "nm%d nh%d" % (t, t), "nl%d" % t)
-
-    def bounds_mm(t):
-        lst = [(P[5][:, 0:256], IM, T.AR[:, :])]
-        for k in range(16):
-            lst += [(P[5][:, 16 * k:16 * k + 16], I1, sb(t, j)) for j in (2, 3)]
-        mm(lst, "AR ID0 ID3 nh%d nl%d" % (t, t), "b5")
-
-    def list_a(t): tt(T.Et[:, :], P[5][:, 256:512], blk(T.ELf, t % 3), A.min, "ELf", "b5 Et")
-
-    def list_b(t):
-        b = t % 3
-        tt(blk(T.ELf, b), P[5][:, 0:256], T.Et[:, :], A.max, "Et", "b5 ELf")
-        if t + 3 < RO:
-            cp(blk(T.ELu, b), blk(T.ELf, b), "ELf", "ELu%d" % b)
-        else:
-            dma("y", [(blk(T.ye, b), blk(T.ELf, b))], "ELf", "")
+        for what, k0, k1 in STREAM:
+            stream(what, k0, k1)
+        at("late")
+        cp(sf(t, fY), P(1, KL, KL + 16))
+        for k in range(KL // 16 + 1, 16):
+            tt(sf(t, fY), P(1, 16 * k, 16 * k + 16), sf(t, fY), A.min)
+        at("min")
+        tt(si(t, iK), B("SF", 16, 272, 17), sf(t, fY), A.min)
+        at("keys")
+        for j, bias in enumerate((0.0, float(2 ** 27 - 2 ** 25))):
+            act(B("PK", 272 * j, 272 * j + 272), B("PP%d" % p), F.Abs, bias)
+        for k in range(KL // 16, 16):
+            for j, bias in enumerate((0.0, float(2 ** 27 - 2 ** 25))):
+                o = B("PK", 272 * j + 16 - k, 272 * j + 272, 17)
+                act(dict(o, key=("PK%d_%d" % (j, k), 0, 1, ALLP)), P(1, 16 * k, 16 * k + 16), F.Abs, bias, 1.0, None, [o])
 
     def choose(t):
-        b, p, s, u, w = t % 3, t % 2, t % 2, t - 1, t - 2
-        Fw = T.FW[:, 512:768]
-        lin(T.PS[:, 0:KL], P[0][:, 0:KL], "", "b0 PS")
-        lin(T.PS[:, KL:256], P[4][:, KL:256], "", "b4 PS2")
-        lin(T.PP[:, :], T.PS[:, :].indirect(T.prm[:, 18 * b:18 * b + 17]), "PS PS2 TT0 TT1 TT2 prm", "PP")
-        if w >= 0:
-            bounds_mm(w)
-        scan(T.SF[:, :], T.d0f[:, :], T.PP[:, :], "PP d0f", "SF")
-        act(T.PK[:, 0:272], T.PP[:, :], F.Abs, "PP", "PK0")
-        act(T.PK[:, 272:544], T.PP[:, :], F.Abs, "PP", "PK1", bias=float(2 ** 27 - 2 ** 25))
-        cp(si(t, 0), T.SF[:, 16:272:17], "SF", "f%d" % t)
-        ts(si(t, 1), si(t, 0), 8191, A.bitwise_and, "f%d" % t, "lf%d" % t)
-        ts(su(t, 0), si(t, 1), cl(QF), A.add, "lf%d qf" % t, "of%d" % t)
-        lin(Fw, Gb[p][:, 0:W + 256].indirect(su(t, 0)), allg(p) + " Gd%d of%d" % (p, t), "FW")
-        act(blk(T.sz, t), Db[p][:, 0:W + 256].indirect(su(t, 0)), F.Abs, alld(p) + " Dz%d of%d" % (p, t), "sz%d" % t)
-        send(t, blk(T.lz, t), blk(T.sz, t), "az%d" % t, "sz%d" % t)
-        lin(T.F2[:, :], Fw, "FW", "F2")
-        t2(sf(t, 0), si(t, 1), 4096.0, 256.0, A.is_ge, A.mult, "lf%d" % t, "nf%d" % t)
-        t2(sf(t, 1), si(t, 1), 4096.0, 8192.0, A.is_lt, A.mult, "lf%d" % t, "fl%d" % t)
-        if w >= 0:
-            list_b(w)
-        if u >= 0:
-            hint_a(u)
-            state_v(u)
-        if t == 0:
-            late_lists()
-        mm(r2l(P[3][:, 0:16], T.BA, bN, T.FW, 512, 768), "FW BA%d" % bN, "b3")
-        mm([(P[2][:, 0:16], I1, T.NB[:, 512 * b:512 * b + 16]), (P[2][:, 0:16], I1, T.NQR[:, :])]
-           + r2l(P[2][:, 0:16], T.BA, bU, T.FW, 512, 768), "FW ID0 NQR NB%d BA%d" % (b, bU), "b2")
-        ef = T.su[:, 128 * t + 32:128 * t + 56]
-        cp(ef[:, 0:16], P[3][:, 0:16], "", "b3 ef%d" % t)
-        cp(ef[:, 16:24], P[3][:, 1:16:2], "", "b3 eg%d" % t)
-        lin(T.KG[:, :], T.Kw[:, 0:W + 256].indirect(ef), "K Kd ef%d eg%d" % (t, t), "KG")
-        tt(sf(t, 3), P[3][:, 0:16], sf(t, 0), A.add, "nf%d" % t, "b3 es%d" % t)
-        act(T.PK[:, 544:816], T.PP[:, :], F.Relu, "PP", "PK2", scale=-1.0)
-        mm([(P[3][:, 0:384], I1, T.TM[:, :])], "TM TMb ID0", "b3", True, False)
-        if u >= 0:
-            rows_late(u)
-        cp(su(t, 1), P[2][:, 0:16], "", "b2 u%d" % t)
-        tt(sb(t, 0), P[2][:, 0:16], st(SV + 16 * b), A.is_lt, "st3", "b2 lt%d" % t)
-        tt(T.EQ[:, :], T.FW[:, 512 - 256 * b:1280 - 256 * b].indirect(su(t, 1)), T.F2[:, :], A.is_equal, "FW F2 u%d" % t, "EQ")
-        mm([(P[3][:, 0:384], T.RP[:, 0:128], T.KG[:, :])], "KG RP0", "b3", False, True)
-        mm(r2l(P[2][:, 0:16], T.BA, bN, T.KG, 0, 256), "KG BA%d" % bN, "b2")
-        lin(T.CR[:, :], P[3][:, 0:384], "", "b3 CR")
-        mm([(P[4][:, 0:16], I1, T.c92[:, :]), (P[4][:, 0:16], I46, sb(t, 0))] + r2l(P[4][:, 0:16], T.BA, bE, T.EQ, 0, 256),
-           "EQ c92 ID0 ID1 lt%d BA%d" % (t, bE), "b4")
-        if u >= 0:
-            hint_b(u)
-        else:
-            late_out()
-        cp(sf(t, 4), P[2][:, 0:16], "", "b2 C%d" % t)
-        cp(su(t, 7), P[2][:, 0:16], "", "b2 cu%d" % t)
-        tt(T.E2[:, :], sf(t, 4).indirect(T.cx[:, :]), T.CR[:, :], A.is_equal, "C%d cx CR" % t, "E2")
-        bias = 0.0 if b == 0 else (oh((6, 3)[s]) if b == 1 else cl((TW6, TW3)[s]))
-        lin(T.XG[:, :], T.Xw[:, :].indirect(su(t, 7)), "X Xb cu%d sc0 sc1 oh tw6 tw3" % t, "XG", bias, cl((SC0, SC1)[s]))
-        act(sf(t, 12), P[4][:, 0:16], F.Relu, "", "b4 y%d" % t)
-        mm(r2l(P[2][:, 0:16], T.BA, bABS, T.E2, 0, 256) + r2l(P[2][:, 1:16:2], T.BA, bABS, T.E2, 256, 384), "E2 BA%d" % bABS, "b2")
-        tt(sf(t, 3), sf(t, 12), sf(t, 3), A.add, "es%d y%d" % (t, t), "es%d" % t)
-        cp(T.so[:, 16 * t:16 * t + 16], sf(t, 3), "es%d" % t, "so%d" % t)
-        send(t, T.lo[:, 16 * t:16 * t + 16], T.so[:, 16 * t:16 * t + 16], "az%d" % t, "so%d" % t)
-        scan(T.SK[:, :], T.d0k[:, :], T.PK[:, :], "PK0 PK1 PK2 d0k0 d0k1 d0k2", "SK")
-        lin(Db[p][:, W + 256:W + 512], Zb[b][:, 0:256], "Z%d of%d" % (b, t), "Dn%d" % p, 0.0, -2.0)
-        if u >= 0:
-            state_mm(u)
-            state_s(u)
-            row_mm(u)
-            hint_mm(u)
-        tt(sf(t, 11), P[2][:, 0:16], st(SDUM), A.min, "st0", "b2 cd%d" % t)
-        rows_of(t, 0)
-        tt(sf(t, 11), sf(t, 11), sf(t, 4), A.max, "cd%d C%d" % (t, t), "cd%d" % t)
-        rows_of(t, 1)
-        em_out(t)
-        if u >= 0:
-            row_s(u)
-        cp(T.cs[:, :], sf(t, 11), "cd%d" % t, "cs")
-        rows_of(t, 2)
-        stale_gather(t)
+        b, p, s = t % 3, t % 2, t % 2
+        G, D, Z = "G%d" % p, "D%d" % p, "Z%d" % b
+        at("row", t)
+        ts(si(t, iLF), si(t, iK), 8191, A.bitwise_and)
+        ts(su(t, uF), si(t, iLF), cl(QF), A.add)
+        at("chosen")
+        lin(B("FW", 512, 768), ind(B(G), su(t, uF)))
+        act(blk("sz", t), ind(B(D, 0, W + 256), su(t, uF)), F.Abs)
+        lin(B("F2"), B("FW", 512, 768))
+        at("")
+        for k in range(KL // 16, 16):
+            cp(B("PP%d" % p, 16 - k, 272, 17), P(1, 16 * k, 16 * k + 16))
+        send(t, blk("lz", t), blk("sz", t), "az%d" % t, 2)
+        t2(sb(t, bNF), si(t, iLF), 4096.0, 524288.0, A.is_ge, A.mult)
+        t2(si(t, iF), si(t, iLF), 4096.0, 524288.0, A.is_lt, A.mult)
+        at("open")
+        mm([(P(3, 0, 16), I1, B("NB", 0, 16))], True, False)
+        mm([(P(2, 0, 16), IM2K, one16)] + [(P(2, 8 * j, 8 * j + 8), I64TH, B("sb", 64 * t + 16 * bNF + j, 64 * t + 16 * bNF + 16, 2)) for j in range(2)],
+           True, False)
+        at("name")
+        mm(r2l(P(4, 0, 16), "BA", bN, "FW", 512, 768), part=16)
+        for j in range(2):
+            cp(B("su", 128 * t + 16 * uE + 8 * j, 128 * t + 16 * uE + 8 * j + 8), P(4, j, 16, 2))
+        cp(sf(t, fE), P(4, 0, 16))
+        at("enclosed")
+        lin(B("KG"), ind(B("Kw", 0, W + 256), su(t, uE)))
+        at("other")
+        mm(r2l(P(3, 0, 16), "BA", bU, "FW", 512, 768), False, True, 16)
+        ts(su(t, uU), P(3, 0, 16), B("col", QB + b), A.subtract)
+        tt(sb(t, bLT), P(3, 0, 16), st(SV + 16 * b), A.is_lt)
+        at("same")
+        tt(B("EQ"), ind(B("FW", 512 - 256 * b, 1280 - 256 * b), su(t, uU)), B("F2"), A.is_equal)
+        at("smaller")
+        mm([(P(3, 0, 16), IM92, one16), (P(3, 0, 16), B("IF"), sf(t, fE)), (P(3, 0, 16), I46, sb(t, bLT))], True, False)
+        at("same")
+        mm(r2l(P(3, 0, 16), "BA", bE, "EQ", 0, 256), False, True, 16)
+        at("drop")
+        tt(sf(t, fY), P(3, 0, 16), sf(t, fE), A.max)
+        cp(B("so", 16 * t, 16 * t + 16), sf(t, fY))
+        send(t, lo(t), B("so", 16 * t, 16 * t + 16), "az%d" % t, 2)
+        at("twice")
+        mm([(P(0, 0, 256), B("RP", 0, 128), B("KG"))])
+        lin(B("CR"), P(0, 0, 256), -2048.0)
+        at("enclosed")
+        mm(r2l(P(2, 0, 16), "BA", bN, "KG", 0, 256), False, True, 16)
+        cp(sf(t, fC), P(2, 0, 16))
+        for j in range(2):
+            t2(halves(su(t, uC), "su", 128 * t + 16 * uC)[j], P(2, 8 * j, 8 * j + 8), 2048.0, 4096.0, A.add, A.min)
+        at("twice")
+        tt(B("E2", 256, 384), ind(sf(t, fC), B("cx", 0, 8)), B("CR", 128, 256), A.is_equal)
+        tt(B("E2", 0, 256), ind(sf(t, fC), B("cx")), B("CR"), A.is_equal)
+        at("merge")
+        bias = 0.0 if b == 0 else (oh((6, 3)[s], s) if b == 1 else cl((TW6, TW3)[s]))
+        lin(B("XG"), ind(B("Xw"), su(t, uC)), bias, cl((SC0, SC1)[s]), None, halves(su(t, uC), "su", 128 * t + 16 * uC))
+        at("both")
+        mm([(P(2, 0, 16), B("IF"), sf(t, fC))], True, False)
+        mm(r2l(P(2, 8, 16), "BA", bABS, "E2", 256, 384), False, False, 16)
+        mm([(P(2, 0, 16), B("LT", 128 * r, 128 * r + 128), B("E2", r, 256, 16)) for r in range(16)], False, True, 16)
 
-    def claims(t, hi, lo):
+    def halves(x, name, a):
+        return [dict(B(name, a + j, a + 16, 2), key=("%s%d_%d" % (name, a, j), 0, 1, ALLP)) for j in range(2)]
+
+    def claims(t, hi=7, low=-1):
         s = t % 2
-        for c in range(hi, lo, -1):
-            tt(T.Xw[:, :].indirect(T.cs[:, 2 * c:2 * c + 2]), T.XG[:, 32 * c:32 * c + 32],
-               T.VP[:, 256 * s + 32 * c:256 * s + 32 * c + 32], A.add, "cs XG VP VP1", "X Xb")
+        half = halves(B("cs"), "cs", 0)
+        at("claim" if hi == 7 else "", t)
+        for j in range(2 * (hi == 7)):
+            t2(half[j], P(2, 8 * j, 8 * j + 8), 2048.0, cl(DUM + j), A.add, A.min)
+        for c in range(hi, low, -1):
+            tt(ind(B("Xw"), B("cs", 2 * c, 2 * c + 2)), B("XG", 32 * c, 32 * c + 32), B("VP", 256 * s + 32 * c, 256 * s + 32 * c + 32), A.add, None, half)
+
+    def rows_of(t):
+        b, p = t % 3, t % 2
+        G, D, Z = "G%d" % p, "D%d" % p, "Z%d" % b
+        at("keys", t)
+        at("")
+        tt(B("dJ", 0, 272, 17), st(SFB), si(t, iLF), A.subtract)
+        at("first")
+        scan(B("SJ"), B("PP%d" % p), B("dJ"), A.max, A.min)
+        at("others")
+        scan(B("SK"), B("d0k"), B("PK"), A.add, A.min, [dict(key=("PK%d_%d" % (j, k), 0, 1, ALLP)) for j in range(2) for k in range(KL // 16, 16)])
+        at("")
+        tt(si(t, iRS, 2), B("SK", 16, 544, 17), st(SADD, 32), A.add)
+        ts(si(t, iJ), B("SJ", 16, 272, 17), -1.0, A.mult)
+        ts(si(t, iLS, 3), si(t, iRS, 3), 4095, A.bitwise_and)
+        tt(sf(t, fU1, 2), si(t, iF, 2), st(SLIM, 32), A.min)
+        tt(sf(t, fOZ), sf(t, fU1), sf(t, fU2), A.max)
+        tt(sf(t, fA), si(t, iLM), sb(t, bNF), A.max)
+        tt(sf(t, fOZ), sf(t, fOZ), si(t, iLS), A.max)
+        tt(sf(t, fB), si(t, iLJ), sb(t, bNF), A.max)
+        tt(sf(t, fSEL), sf(t, fA), sf(t, fOZ), A.min)
+        tt(sb(t, bROW), sf(t, fB), sf(t, fOZ), A.min)
+        ts(su(t, uZ, 2), sf(t, fOZ, 2), cl(QF), A.add)
+        thr = B("PS", 256 + 16 * b, 272 + 16 * b)
+        tt(thr, thr, sb(t, bNF), A.add)
+        at("send")
+        lin(blk("se", t), ind(B(G), su(t, uSEL)))
+        send(t, blk("le", t), blk("se", t), "ae%d" % t, 1)
+        at("minus")
+        lin(B(D, W + 256, W + 512), blk(Z, 0), 0.0, -2.0)
+        at("stale")
+        lin(B("DS"), ind(B(D), su(t, uZ)))
+
+    def state(t):
+        b = t % 3
+        z = blk("Z%d" % b, 0)
+        lst = [(P(7, 0, 256), I1, z), (P(7, 0, 256), IHALF, B("DS")), (P(7, 0, 256), I1, blk("sz", t))]
+        at("round", t)
+        if ROUND_S:
+            mm(lst, part=1)
+            lin(B("ZR"), P(7, 0, 256), MAGIC, 1.0 - 2.0 ** -11)
+            at("state")
+            lin(z, B("ZR"), -MAGIC)
+        else:
+            mm(lst + [(P(7, 0, 256), IQRT, B("on"))], part=1)
+            t2(z, P(7, 0, 256), MAGIC, MAGIC, A.add, A.subtract)
+        at("")
+        if t + 3 < RO:
+            dma("y", [(blk("Z%d" % b, j), z) for j in range(1, REP)])
+        else:
+            dma("y", [(H(T.yz[:, 256 * b:256 * b + 256], bf), z)])
+
+    def hint(t):
+        at("mask", t)
+        mm([(P(6, 0, 256), B("RP", 128, 256), blk("se", t))])
+        if MASK_S:
+            act(B("MA"), P(6, 0, 256), F.Abs, cl(NQ))
+            act(blk("MK", t % 2), B("MA"), F.Relu, 1.0, -1.0)
+        else:
+            ts(blk("MK", t % 2), P(6, 0, 256), cl(QF), A.is_equal)
+        at("")
+        hop = P(4, 288, 304)
+        mm([(hop, I16TH, sb(t, bROW)), (hop, I16TH, B("NB", 0, 16))] + r2l(hop, "BA", bH, "se", 256 * t, 256 * t + 256), part=6)
+        cp(su(t, uH), hop)
+        mm([(P(6, 256, 512), IM16, B("kc"))] + [(P(6, 256 + 16 * k, 272 + 16 * k), I16, sb(t, bROW)) for k in range(16)], part=6)
+        at("cutoff")
+        act(B("AR"), P(6, 256, 512), F.Abs, 0.0, 2.0)
+        mm([(P(5, 256, 512), I1, B("AR")), (P(5, 256, 512), IM2K, B("on"))], part=1)
+
+    def name(t):
+        at("hint", t)
+        tt(B("HG"), ind(B("ELf"), su(t, uH)), blk("MK", t % 2), A.mult)
+        mm([(P(4, 272, 288), I8K, one16), (P(4, 272, 288), IM64TH, sb(t, bNF))], True, False)
+        mm(r2l(P(4, 272, 288), "BA", bONE, "HG", 0, 256), False, True, 4)
+        at("")
+        for j in range(2):
+            tt(halves(sh(t, hN), "sh", 48 * t)[j], P(4, 272 + j, 288, 2), B("sf", 144 * t + 16 * fC + 8 * j, 144 * t + 16 * fC + 8 * j + 8), A.min)
+
+    def cut(t):
+        at("cut", t)
+        tt(B("Et"), P(5, 256, 512), blk("ELf", t % 3), A.min)
+
+    def put(t):
+        b = t % 3
+        el = blk("ELf", b)
+        at("bounds", t)
+        mm([(P(5, 0, 256), IM1, B("AR"))], True, False)
+        mm([(P(5, 16 * k, 16 * k + 16), I1, sh(t, hN)) for k in range(16)], False, True, 4, also=halves(sh(t, hN), "sh", 48 * t))
+        at("put")
+        tt(el, P(5, 0, 256), B("Et"), A.max)
+        at("offsets")
+        if t + 3 < RO:
+            ts(blk("ELu", b), el, 2048.0, A.add)
+        else:
+            lin(blk("oE", b), el, 2048.0)
+            dma("y", [(H(T.ye[:, 256 * b:256 * b + 256], f32), blk("oE", b))])
+
+    def table_out(X, wt, off, bank, buf, y):
+        mm([(P(bank, 0, 256), B(wt, off + 15 - j, off + 143 - j), blk(X, j)) for j in range(16)], part=4)
+        lin(buf, P(bank, 0, 256))
+        dma("y", [(H(y, f32), buf)])
 
     for t in range(RO):
-        u, w = t - 1, t - 2
-        own_mm(t, -1)
-        own_gather(t, 0)
-        if u >= 0:
-            hop_mm(u)
-            scat_m(u)
-        own_mm(t, 0)
-        diff(t, 0)
-        own_gather(t, 1)
-        fold(t, 0)
-        own_mm(t, 1)
-        dist_a(t, 0)
-        dist_b(t, 0)
-        if t == 0:
-            mid_setup()
-        diff(t, 1)
-        own_gather(t, 2)
-        own_mm(t, 2)
-        own_gather(t, 3)
-        if RELU > 1:
-            fold(t, 1)
-            dist_a(t, 1)
-            dist_b(t, 1)
-        own_mm(t, 3)
-        if RELU < 2:
-            fold(t, 1)
-            dist_b(t, 1)
-        diff(t, 2)
-        for j in range(2, NC - 1):
-            fold(t, j)
-            if j == NC - 2:
-                live(t)
-            diff(t, j + 1)
-            if j < RELU:
-                dist_a(t, j)
-            dist_b(t, j)
-        live_s(t)
-        fold(t, NC - 1)
-        live_mm(t)
-        dist_b(t, NC - 1)
-        if t == 0:
-            late_setup()
-        if w >= 0:
-            name_v(w)
-            list_a(w)
-        if u >= 0:
-            scat_k(u)
+        window(t)
+        if t == RO - 1:
+            s = t % 2
+            at("")
+            table_out("Xw", "BA", (bO, bY)[s], 4, blk("oO", 0), T.yo[8 - 8 * s:16 - 8 * s, :])
+        if t:
+            scat(t - 1, "Kw", blk("le", t - 1))
+            cut(t - 1)
         choose(t)
-        if t < RO - 1:
-            claims(t, 7, -1)
+        if t:
+            name(t - 1)
+        claims(t)
+        rows_of(t)
+        if t:
+            put(t - 1)
+        hint(t)
+        state(t)
 
     t = RO - 1
-    rows_late(t)
-    scat_m(t)
-    dma("y", [(T.ym[:, 0:W // 2], T.Mw[:, 0:W // 2])], "M", "")
-    name_v(t - 1)
-    bounds_mm(t - 1)
-    hop_mm(t)
-    list_a(t - 1)
-    claims(t, 7, 3)
-    hint_a(t)
-    list_b(t - 1)
-    row_mm(t)
-    hint_b(t)
-    row_s(t)
-    hint_mm(t)
-    claims(t, 3, -1)
-    dma("s", [(T.cpb[:, a:a + 256], T.Xw[q::16, 0:W]) for q, a in rows[:5]], "X Xb", "cpb")
-    scat_k(t)
-    dma("s", [(T.cpb[:, 1280:1536], T.Kw[4::16, 0:W]), (T.cpb[:, 1536:1792], T.Kw[5::16, 0:W])], "K", "cpk")
-    dma("s", [(T.ym[:, W // 2:W], T.Mw[:, W // 2:W])], "M", "")
-    state_v(t)
-    tt(T.TL[:, :], T.PS[:, 256:304], st(STT, 48), A.subtract, "TT0 TT1 TT2 st4", "TL")
-    list_a(t)
-    ts(T.TL[:, :], T.TL[:, :], 1.0 / 8192, A.mult, "TL", "TL")
-    name_v(t)
-    state_mm(t)
-    bounds_mm(t)
-    state_s(t)
-    mm([(P[2][0:48, 0:128], T.TL[:, :], T.IF[:, :])], "IF TL", "b2")
-    list_b(t)
-    lin(T.oT[0:48, :], P[2][0:48, 0:128], "", "b2 oT")
-    dma("s", [(T.yt[q, :], T.oT[0:48, 16 * q:16 * q + 16]) for q in range(8)], "oT", "")
-    mm([(P[1][:, 0:256], I, T.cpb[:, a:a + 256]) for I, a in ((I1, 0), (I16, 256), (I256, 512))], "cpb ID0 ID5 ID6", "b1")
-    mm([(P[1][:, 256:512], I, T.cpb[:, a:a + 256]) for I, a in ((I256, 768), (I1, 1024))], "cpb", "b1")
-    mm([(P[0][:, 0:256], I, T.cpb[:, a:a + 256]) for I, a in ((I256, 1280), (I1, 1536))], "cpk", "b0")
-    cp(T.oO[:, :], P[1][:, :], "", "b1 oO")
-    lin(T.oK[:, :], P[0][:, 0:256], "", "b0 oK")
-    dma("y", [(T.yo[0:8, :], T.oO[:, 0:256]), (T.yo[8:16, :], T.oO[:, 256:512])], "oO", "")
-    dma("s", [(T.yk[:, :], T.oK[:, :])], "oK", "")
+    at("")
+    parts = (((0, I1), (1, I16), (6, I256)), ((2, I1), (3, I1)))[s]
+    dma("s", [(blk("cpb", j), piece("Xw", q)) for j, (q, I) in enumerate(parts)])
+    scat(t, "Mw", blk("lz", t))
+    at("")
+    dma("y", [(H(T.ym[:, 0:W // 2], bf), B("Mw", 0, W // 2))])
+    dma("s", [(H(T.ym[:, W // 2:W], bf), B("Mw", W // 2, W))], 2 ** 19)
+    name(t)
+    scat(t, "Kw", blk("le", t))
+    cut(t)
+    put(t)
+    at("")
+    table_out("Kw", "BA", bN, 0, B("oK"), T.yk[:, :])
+    mm([(P(1, 0, 256), I, blk("cpb", j)) for j, (q, I) in enumerate(parts)])
+    cp(blk("oO", 1), P(1, 0, 256))
+    dma("y", [(H(T.yo[8 * s:8 + 8 * s, :], f32), blk("oO", 1))])
+    tt(B("TL"), B("PS", 256, 304), st(STT, 48), A.subtract)
+    ts(B("TL"), B("TL"), 1.0 / 8192, A.mult)
+    mm([(dict(P(3, 0, 128), ap=T.P3[0:48, 0:128]), B("TL"), B("IF"))])
+    lin(B("oT", 0, 128, 1, th48), dict(P(3, 0, 128), ap=T.P3[0:48, 0:128]))
+    dma("y", [(dict(H(T.yt[q, :], f32), n=6), B("oT", 16 * q, 16 * q + 16, 1, th48)) for q in range(8)])
     emit()
     g.wait_ge(T.sem.sent, nsent[0])

import math
from concourse.mybir import AluOpType as A, ActivationFunctionType as F

W, V, PB, RO, N = 4096, 768, 256, 8, 4
STREAM = [("diff", 0, 5), ("diff", 5, 10), ("relu", 0, 5), ("diff", 10, 14), ("abs", 5, 10), ("live", 0, 0), ("diff", 14, 16), ("abs", 10, 14),
          ("sign", 0, 0), ("abs", 14, 16), ("least", 0, 0)]
OC = [(0, 4), (4, 8), (8, 12), (12, 16)]
KL = 16 * 14
REP = 5
ROUND_S, MASK_S = True, True
BIG = float(2 ** 29)
MAGIC = 12582912.0
CYC, PEC, GATH, SCAT, HOP, FAR, DMA, RATE = 0.83, 0.42, 1.56, 3.8, 175.0, 2300.0, 2000.0, 300.0
CYCLE = {
    "v": "putM' diff0 diff5 relu0 diff10 live diff14 put'' putK' late least min row others first name other same hint' "
         "enclosed twice drop cut' offsets'' claim",
    "s": "own0 own4 own8 own12 abs5 abs10 sign abs14 least keys chosen minus enclosed twice send merge stale mask round cutoff state",
    "p": "own0 own4 diff0 own8 relu0 own12 live abs5 abs10 sign abs14 cutoff' open name other smaller twice enclosed same both hint' bounds'",
}
LAST = 2
SIZE = {"bfloat16": 2, "float16": 2, "uint16": 2, "float32": 4, "int32": 4}


def _sb(n, d):
    return ("sbuf", [128, n], d)


bf, f16, f32, i32, u16 = "bfloat16", "float16", "float32", "int32", "uint16"
TW = 8960
SCRATCH = {
    "Mw": _sb(TW, bf), "Kw": _sb(TW, bf), "Xw": _sb(4128, bf),
    "G0": _sb(4352, bf), "G1": _sb(4352, bf), "D0": _sb(4608, bf), "D1": _sb(4608, bf), "AB": _sb(4096, bf),
    "Z0": _sb(REP * 256, bf), "Z1": _sb(REP * 256, bf), "Z2": _sb(REP * 256, bf),
    "ELi": _sb(V, i32), "ELf": _sb(V, f32), "ELu": _sb(V, u16), "Et": _sb(256, f32), "oE": _sb(V, f32),
    "cin": _sb(768, i32), "cpi": _sb(1792, i32), "cpb": _sb(2304, bf), "thi": _sb(128, i32), "thf": _sb(128, f32),
    "PS": _sb(304, f32), "PP0": _sb(272, f32), "PP1": _sb(272, f32), "PK": _sb(544, f32), "SF": _sb(272, f32), "SK": _sb(544, f32), "SJ": _sb(272, f32),
    "d0f": _sb(272, f32), "d0k": _sb(544, f32), "dJ": _sb(272, f32), "prm": _sb(54, u16), "prR": _sb(864, f32),
    "pr": _sb(512, bf), "lv": _sb(256, bf), "JP": _sb(256, bf), "BY": _sb(144, bf),
    "FW": _sb(1280, bf), "EQ": _sb(256, bf), "F2": _sb(256, bf), "KG": _sb(256, bf), "CR": _sb(256, f32), "E2": _sb(384, bf),
    "XG": _sb(256, bf), "DS": _sb(256, bf), "ZR": _sb(256, f32), "MA": _sb(256, bf), "MK": _sb(512, f32), "HG": _sb(256, f16),
    "AR": _sb(256, bf),
    "sz": _sb(RO * 256, bf), "se": _sb(RO * 256, bf), "so": _sb(RO * 16, u16),
    "lz": _sb(RO * 256, bf), "le": _sb(RO * 256, bf), "lo": _sb(RO * 16, u16),
    "si": _sb(RO * 192, i32), "sf": _sb(RO * 144, f32), "sb": _sb(RO * 64, bf), "sh": _sb(RO * 48, f16), "su": _sb(RO * 128, u16),
    "col": _sb(32, f32), "coli": _sb(8, i32), "n143": _sb(144, f32), "one": _sb(128, f32), "nd16": _sb(128, f32),
    "OH": _sb(32, f32), "BA": _sb(11 * 144, bf), "BF": _sb(144, f32), "RP": _sb(256, bf),
    "ID": _sb(15 * 128, bf), "IF": _sb(128, f32),
    "rr": _sb(256, bf), "cc": _sb(256, bf), "kc": _sb(256, bf), "NB": _sb(512, bf), "on": _sb(256, bf),
    "LT": _sb(2048, bf), "VP": _sb(768, bf), "stt": _sb(256, f32), "cxi": _sb(16, i32), "cx": _sb(16, u16),
    "cs": _sb(16, u16), "oK": _sb(256, f32), "oO": _sb(512, f32), "oT": _sb(128, f32), "TL": _sb(48, f32),
}
for _b in range(8):
    SCRATCH["P%d" % _b] = ("psum", [128, 512], f32)
SEMAPHORES = ["v", "s", "p", "c", "sent"] + ["az%d" % t for t in range(RO)] + ["ae%d" % t for t in range(RO)] + ["d%d" % t for t in range(48)]
ORDER = []


def rank_program(g, core, T, topo):
    rank = T.rank_of(core)
    if rank is None:
        return
    Q = {"v": g.vector, "s": g.scalar, "p": g.tensor, "c": g, "y": g.sync}
    ops, seen_by, closer, named, now = [], {}, {}, {}, ["", -1]
    ALLP = 2 ** 128 - 1

    def B(name, a=None, b=None, step=1, p=None):
        where, shape, dt = SCRATCH[name]
        a, b = (0, shape[1]) if a is None else (a, a + 1 if b is None else b)
        p = p or (0, 128, 1)
        ap = T[name][p[0]:p[1]:p[2], a:b:step]
        if where == "psum":
            return dict(ap=ap, key=(name, 0, 1, ALLP), bank=True, n=len(range(a, b, step)), dt=dt)
        last = a + (len(range(a, b, step)) - 1) * step + 1
        mask = ALLP if p == (0, 128, 1) else sum(1 << j for j in range(*p))
        return dict(ap=ap, key=(name, a * SIZE[dt] // 16 * 16, -(-last * SIZE[dt] // 16) * 16, mask), n=len(range(a, b, step)), dt=dt)

    def H(ap, dt): return dict(ap=ap, key=None, dt=dt, n=int(math.prod(ap.shape)) // 128)
    def ind(win, off): return dict(ap=win["ap"].indirect(off["ap"]), key=win["key"], off=off["key"], n=16 * off["n"], dt=win["dt"])
    def ap(x): return x["ap"] if isinstance(x, dict) else x

    def add(q, kind, fn, r, w, busy, lat, chain=None):
        me, dep, rk, wk = len(ops), {}, [], []
        for x in r:
            if isinstance(x, dict) and x["key"]:
                (wk if x.get("bank") else rk).append((x["key"], x.get("bank")))
        for x in w:
            (rk if x.get("acc") else wk).append((x["key"], x.get("bank")))
        rk += [(x["off"], None) for x in list(r) + list(w) if isinstance(x, dict) and "off" in x]
        if chain:
            wk.append(((chain, 0, 1, ALLP), "order"))
        for keys, write in ((rk, False), (wk, True)):
            for (name, lo, hi, pm), bank in keys:
                for lo2, hi2, pm2, j, wr in seen_by.get(name, []):
                    if j != me and lo < hi2 and lo2 < hi and pm & pm2 and (write or wr):
                        free = bank == "order" or (bank and ops[j]["q"] == q)
                        dep[j] = dep.get(j, False) or not free
        for keys, write in ((rk, False), (wk, True)):
            for (name, lo, hi, pm), bank in keys:
                old = seen_by.get(name, [])
                if write:
                    old = [x for x in old if not (lo <= x[0] and x[1] <= hi and x[2] & ~pm == 0)]
                seen_by[name] = old + [(lo, hi, pm, me, write)]
        ops.append(dict(q=q, kind=kind, fn=fn, dep=dep, busy=busy, lat=lat))
        named.setdefault((q,) + tuple(now), []).append(me)
        return me

    def at(name, t=None): now[:] = [name, now[1] if t is None else t]

    def op(q, fn, r, w, busy, chain=None): add(q, "op", fn, r, w, busy, busy, chain)

    def dma(q, pairs, behind=0, after=()):
        size = behind + sum(128 * o["n"] * SIZE[o["dt"]] if o["key"] is None else 128 * i["n"] * SIZE[i["dt"]] if i["key"] is None
                            else int(math.prod(o["ap"].shape)) * SIZE[o["dt"]] for o, i in pairs)
        add(q, "dma", pairs, [i for o, i in pairs] + list(after), [o for o, i in pairs if o["key"]], 60.0 * len(pairs), DMA + size / RATE,
            None if closer.get("steps") else "#" + q)

    def plan():
        n = len(ops)
        for q, names in CYCLE.items():
            row = [i for t in range(RO) for x in names.split() for i in named.get((q, x.rstrip("'"), t - x.count("'")), [])]
            for j, i in zip(row, row[1:]):
                ops[i]["dep"].setdefault(j, False)
        gap = lambda j, wait: ops[j]["lat"] + HOP if wait else ops[j]["busy"]
        succ = [[] for _ in range(n)]
        for i in range(n):
            for j, wait in ops[i]["dep"].items():
                succ[j].append((i, wait))

        def place(order, links):
            at0, lanes = [0.0] * n, {q: [] for q in Q}
            for i in order:
                at = max([0.0] + links(i, at0))
                lane_, busy = lanes[ops[i]["q"]], ops[i]["busy"]
                pos = len(lane_)
                while pos > 0 and lane_[pos - 1][1] > at:
                    pos -= 1
                while pos < len(lane_) and at + busy > lane_[pos][0]:
                    at = max(at, lane_[pos][1])
                    pos += 1
                lane_.insert(pos, (at, at + busy))
                at0[i] = at
            return at0

        def ahead(i, at0): return [at0[j] + gap(j, wait) for j, wait in ops[i]["dep"].items()]

        key = list(range(n))
        for j in range(closer["steps"] - 1, -1, -1):
            key[j] = min([n] + [key[i] for i, wait in succ[j]])
        order, done = [], [False] * n

        def visit(i):
            todo = [i]
            while todo:
                k = todo[-1]
                ahead_ = [j for j in ops[k]["dep"] if not done[j]]
                if ahead_:
                    todo.append(min(ahead_))
                    assert len(todo) <= n
                else:
                    todo.pop()
                    if not done[k]:
                        done[k] = True
                        order.append(k)

        for i in sorted(range(n), key=lambda i: (key[i], i)):
            visit(i)
        start = place(order, ahead)
        rank_ = {i: k for k, i in enumerate(order)}
        return sorted(range(n), key=lambda i: (start[i], rank_[i]))

    def emit():
        if not ORDER:
            ORDER.extend(plan())
        closer.update({ops[i].get("acc"): i for i in ORDER})
        cnt, seen, final, tok, nd = {q: 0 for q in Q}, {q: {} for q in Q}, {}, {}, 0
        for i in ORDER:
            o = ops[i]
            q, want = o["q"], {}
            for j, wait in o["dep"].items():
                if wait:
                    want[tok[j][0]] = max(want.get(tok[j][0], 0), tok[j][1])
            for s, m in want.items():
                if seen[q].get(s, 0) < m:
                    Q[q].wait_ge(T.sem[s], m)
                    seen[q][s] = m
            if o["kind"] == "op":
                cnt[q] += 1
                o["fn"]().then_inc(T.sem[q], 1)
                tok[i] = (q, cnt[q])
            elif o["kind"] == "dma":
                for a, b in o["fn"]:
                    Q[q].dma_start(a["ap"], b["ap"]).then_inc(T.sem["d%d" % nd], 16)
                tok[i] = ("d%d" % nd, 16 * len(o["fn"]))
                nd += 1
            else:
                tok[i] = o["fn"]()
                continue
            final[tok[i][0]] = tok[i][1]
        for s, m in final.items():
            g.wait_ge(T.sem[s], m)

    v, sc, pe = g.vector, g.scalar, g.tensor

    def cost(o, a, per=None):
        if "off" in o:
            return 50.0 + o["n"] * SCAT * CYC
        if "off" in a:
            return 60.0 + o["n"] * GATH * CYC
        if per is None:
            per = 0.5 if SIZE[o["dt"]] == 2 and SIZE[a["dt"]] == 2 else 1.0
        return max(64.0, o["n"] * per) * CYC

    def tt(o, a, b, x, chain=None, also=()):
        op("v", lambda: v.tensor_tensor(ap(o), ap(a), ap(b), x), [a, b] + list(also), [o], cost(o, a, 1.0 if a.get("bank") or b.get("bank") else 2.0), chain)

    def ts(o, a, s1, x, chain=None): op("v", lambda: v.tensor_scalar(ap(o), ap(a), ap(s1), None, x), [a, s1], [o], cost(o, a), chain)
    def t2(o, a, s1, s2, x, y): op("v", lambda: v.tensor_scalar(ap(o), ap(a), ap(s1), ap(s2), x, y), [a, s1, s2], [o], cost(o, a))
    def cp(o, a): op("v", lambda: v.tensor_copy(ap(o), ap(a)), [a], [o], cost(o, a))
    def ms(o, x): op("v", lambda: v.memset(ap(o), x), [], [o], cost(o, o))
    def scan(o, a, b, x, y, also=()):
        op("v", lambda: v.tensor_tensor_scan(ap(o), ap(a), ap(b), 0.0, x, y), [a, b] + list(also), [o], cost(o, a, 1.0))

    def act(o, a, f, bias=0.0, scale=1.0, chain=None, also=()):
        op("s", lambda: sc.activation(ap(o), ap(a), f, bias=ap(bias), scale=ap(scale)), [a, bias, scale] + list(also), [o], cost(o, a, 1.0), chain)

    def lin(o, a, bias=0.0, scale=1.0, chain=None, also=()): act(o, a, F.Identity, bias, scale, chain, also)

    def iota(o, pat, base, cm=0):
        if o["dt"] == i32:
            op("c", lambda: g.iota(ap(o), pat, base, cm), [], [o], 160.0 + 2 * o["n"] * CYC)
        else:
            op("c", lambda: g.iota(ap(o), pat, base, cm, allow_small_or_imprecise_dtypes=True), [], [o], 160.0 + 2 * o["n"] * CYC)

    def mm(lst, start=True, stop=True, part=8, acc=None, chain=None, also=()):
        for a in range(0, len(lst), part):
            def fn(a=a, me=len(ops)):
                ins, end = None, min(a + part, len(lst))
                for j in range(a, end):
                    o, l, x = lst[j]
                    last = (closer[acc] == me and j == end - 1) if acc else (stop and j == len(lst) - 1)
                    ins = pe.matmul(ap(o), ap(l), ap(x), start and not acc and j == 0, last)
                return ins
            sub = lst[a:a + part]
            op("p", fn, [x for o, l, r in sub for x in (l, r)] + list(also), [dict(sub[0][0], acc=acc)],
               sum(max(min(64, l["n"]), x["n"]) * (1 if SIZE[x["dt"]] == 2 else 4) * PEC for o, l, x in sub), chain)
            ops[-1]["acc"] = acc

    def r2l(o, wt, off, X, a, b):
        return [(o, B(wt, off + 15 - r, off + 143 - r), B(X, a + r, b, 16)) for r in range(16)]

    def P(j, a, b, step=1): return B("P%d" % j, a, b, step)
    def cl(j): return B("col", j)
    def oh(q, big=0): return B("OH", 16 * big + q)
    def st(a, n=16): return B("stt", a, a + n)
    def blk(X, t): return B(X, 256 * t, 256 * t + 256)
    QF, G15, GF, WX, WY, WN, WU, WH, H16, SC0, SC1, TW6, TW3, NQ, G23, JA, JB, WE, Q8, QB, DUM = list(range(18)) + [18, 21, 24]
    bABS, bREL, bDEL, bX, bY, bN, bU, bH, bONE, bE, bO = [144 * j for j in range(11)]
    IDS = (1.0, -float(2 ** 27), -1.0, 1.0 / 64, 8192.0, -16.0, 16.0, 0.5, -0.25, 1.0 / 16, -1.0 / 64, -2048.0, 256.0, 4608.0, -9216.0)
    (I1, ILV, IM1, I64TH, I8K, IM16, I16, IHALF, IQRT, I16TH, IM64TH, IM2K, I256, I46,
     IM92) = [B("ID", 128 * j, 128 * j + 128) for j in range(len(IDS))]
    SADD, SLIM, SV, STT, SFB = 0, 32, 64, 112, 160
    lane, one16 = B("cpb", 2048, 2304), B("on", 0, 16)

    dma("y", [(B("cin", 0, 256), H(T.own[0:8, :], i32))])
    dma("s", [(B("cin", 256, 512), H(T.own[8:16, :], i32))], 2 ** 17)
    dma("y", [(B("ELi", 0, 256), H(T.ends[:, 0:256], i32)), (blk("Z0", 0), H(T.st[:, 0:256], bf))], 2 ** 18)
    dma("y", [(B("Mw", 0, W), H(T.msg[:, :], bf))], 2 ** 19)
    iota(B("coli", 0), [[0, 1]], 0, 1)
    iota(lane, [[1, 256]], 0)
    iota(B("n143"), [[1, 144]], 0)
    iota(B("one"), [[0, 128]], 1)
    op("c", lambda: g.affine_select(T.IF[:, :], T.one[:, :], [[-1, 128]], A.is_equal, 0.0, 0, 1), [B("one")], [B("IF")], 480.0)
    iota(B("NB", 0, 256), [[0, 16], [-16, 16]], 0)
    iota(B("NB", 256, 512), [[0, 16], [-16, 16]], -8)
    iota(B("kc"), [[256, 16], [16, 16]], 0)
    for b in range(3):
        iota(B("prR", 288 * b, 288 * b + 272), [[1, 16], [-16, 17]], 256)
        iota(B("prR", 288 * b + 272, 288 * b + 288), [[0, 16]], 0)
        if b:
            iota(B("prR", 288 * b, 288 * b + 272, 17), [[1, 16]], 256 + 16 * b)
    iota(st(STT, 48), [[0, 3], [16, 16]], -4096)
    iota(B("dJ"), [[-16, 16], [256, 17]], -4096)
    iota(B("nd16"), [[1, 8], [0, 16]], 0)
    iota(B("rr"), [[0, 16], [1, 16]], 0)
    iota(B("cc"), [[1, 16], [0, 16]], 0)
    iota(st(SADD + 16), [[32, 16]], 0)
    iota(st(SLIM, 32), [[-256, 2], [16, 16]], 4352)
    iota(st(SV, 48), [[512, 3], [16, 16]], 0, 0)
    iota(st(SFB), [[-8192, 16]], -8192)
    iota(B("cxi"), [[1, 16]], 0)
    iota(B("on"), [[0, 256]], 1)

    ms(B("Xw"), 0.0)
    ts(B("coli", 4), B("coli", 0), 15, A.bitwise_and)
    ts(B("coli", 5), B("coli", 0), 4, A.arith_shift_right)
    ts(B("coli", 6), B("coli", 0), 7, A.bitwise_and)
    cp(cl(QF), B("coli", 4))
    t2(cl(G15), B("coli", 5), 16.0, 15.0, A.mult, A.add)
    lin(B("cpb", 1792, 2048), lane, cl(QF), 0.0)
    def piece(X, q): return B(X, 0, W, 1, (q, 128, 16))
    dma("s", [(piece("Xw", q), B("cpb", a, a + 256)) for q, a in ((4, 1792), (5, 2048))], 2 ** 20)
    ts(B("cpi", 0, 256), B("cin", 0, 256), 15, A.bitwise_and, "#v")
    t2(B("cpi", 256, 512), B("cin", 0, 256), 4, 15, A.arith_shift_right, A.bitwise_and)
    ts(B("cpi", 512, 768), B("cin", 0, 256), 8, A.arith_shift_right, "#v")
    cp(B("cpb", 768, 1024), B("cin", 256, 512))
    cp(B("cpb", 0, 768), B("cpi", 0, 768))
    tt(B("cpb", 1024, 1280), B("cin", 256, 512), B("cpb", 768, 1024), A.subtract, "#v")
    dma("y", [(piece("Xw", q), B("cpb", a, a + 256)) for q, a in ((0, 0), (1, 256), (6, 512))], 2 ** 19)
    dma("s", [(piece("Xw", q), B("cpb", a, a + 256)) for q, a in ((3, 768), (2, 1024))], 2 ** 19)
    for j in range(1, REP):
        lin(blk("Z0", j), blk("Z0", 0))
    dma("y", [(B("thi", 16 * q, 16 * q + 16, 1, (0, 48, 1)), dict(H(T.th[q, :], i32), n=6)) for q in range(8)]
        + [(B("cin", 512, 768), H(T.enc[:, :], i32))], 0, [B("Xw")])
    dma("y", [(B("Kw", 0, W), H(T.msg[:, :], bf))], 2 ** 17)
    dma("y", [(B("ELi", 256, V), H(T.ends[:, 256:V], i32))], 2 ** 20)
    for b in (1, 2):
        dma("y", [(blk("Z%d" % b, j), H(T.st[:, 256 * b:256 * b + 256], bf)) for j in range(REP)], 2 ** 21)
    cp(B("ELu", 0, 256), B("ELi", 0, 256))
    ts(B("BF"), B("n143"), cl(G15), A.is_equal)
    mm(r2l(P(7, 0, 54), "BF", 0, "prR", 0, 864))
    ts(B("OH", 0, 16), B("n143", 0, 16), cl(QF), A.is_equal)
    t2(B("OH", 16, 32), B("n143", 0, 16), cl(QF), 256.0, A.is_equal, A.mult)
    ts(cl(NQ), cl(QF), -1.0, A.mult)
    cp(cl(GF), B("coli", 5))
    t2(cl(WX), oh(1), 16.0, oh(0), A.mult, A.add)
    tt(cl(WY), oh(2), oh(3), A.add)
    tt(cl(WN), oh(5), oh(4, 1), A.add)
    tt(cl(WX), cl(WX), oh(6, 1), A.add)
    tt(cl(WH), oh(1), oh(6, 1), A.add)
    tt(cl(WU), cl(WX), cl(WY), A.add)
    ts(cl(H16), oh(4), 16.0, A.mult)
    ts(cl(TW6), oh(6), 2.0, A.mult)
    ts(cl(TW3), oh(3), 512.0, A.mult)
    ts(cl(SC0), cl(WX), 0.0, A.is_equal)
    ts(cl(SC1), cl(WY), 0.0, A.is_equal)
    ts(cl(DUM), cl(QF), 4096.0, A.add)
    ts(cl(DUM + 1), cl(QF), 4112.0, A.add)
    cp(B("col", 31), B("coli", 6))
    ts(B("col", Q8, Q8 + 3), B("kc", 0, 48, 16), B("col", 31), A.add)
    ts(B("col", QB, QB + 3), B("kc", 0, 48, 16), cl(QF), A.add)
    for j, x in enumerate(IDS):
        lin(B("ID", 128 * j, 128 * j + 128), B("IF"), 0.0, x)
    ts(cl(G23), cl(G15), 8.0, A.add)
    t2(B("BY"), B("n143"), cl(G23), cl(WY), A.is_equal, A.mult)
    t2(cl(JA), cl(G15), -15.0, B("col", 31), A.add, A.add)
    ts(cl(JB), cl(JA), 8.0, A.add)
    lin(B("BA", bY, bY + 144), B("BF"), 0.0, cl(WX))
    ts(B("JP", 0, 128), B("n143", 0, 128), cl(JA), A.is_equal)
    ts(B("JP", 128, 256), B("n143", 0, 128), cl(JB), A.is_equal)
    tt(B("BA", bX, bX + 144), B("BA", bY, bY + 144), B("BY"), A.add)
    for off, x in ((bREL, 16384.0), (bDEL, -8192.0), (bABS, 8192.0), (bONE, 1.0), (bN, cl(WN)), (bU, cl(WU)), (bH, cl(WH)), (bO, cl(WY))):
        lin(B("BA", off, off + 144), B("BF"), 0.0, x)
    ms(B("FW"), -1.0)
    ms(B("d0f"), 0.0)
    ms(B("d0k", 0, 272), 0.0)
    ms(B("d0k", 272, 544), 512.0)
    ms(B("d0f", 0, 272, 17), BIG)
    ms(B("d0k", 0, 544, 17), BIG)
    ms(B("d0k", 1, 544, 17), BIG)
    ms(st(SADD), -float(2 ** 26))
    ms(B("PS", KL, 256), BIG)
    for X in ("D0", "D1"):
        ms(B(X, W, W + 256), 0.0)
    ms(B("Kw", W, W + 256), 0.0)
    for X in ("G0", "G1"):
        lin(B(X, W, W + 256), lane, cl(H16), oh(5))
    ts(st(STT, 48), st(STT, 48), -float(2 ** 27), A.add)
    ts(B("prm"), P(7, 0, 54), 1.0 / 16, A.mult)
    th48 = (0, 48, 1)
    cp(B("thf", 0, 128, 1, th48), B("thi", 0, 128, 1, th48))
    mm([(P(6, 0, 48), B("thf", 0, 128, 1, th48), B("IF", 0, 48, 1, th48))])
    ts(B("cpi", 1280, 1536), B("cin", 512, 768), 8, A.arith_shift_right)
    ts(B("cpi", 1536, 1792), B("cin", 512, 768), 255, A.bitwise_and)
    cp(B("cpb", 1280, 1792), B("cpi", 1280, 1792))
    dma("y", [(piece("Kw", 4), B("cpb", 1280, 1536)), (piece("Kw", 5), B("cpb", 1536, 1792))])
    ts(B("TL"), P(6, 0, 48), 8192.0, A.mult)
    tt(B("PS", 256, 304), B("TL"), st(STT, 48), A.add)
    t2(B("RP", 0, 128), B("nd16"), cl(GF), cl(WN), A.is_equal, A.mult)
    t2(B("RP", 128, 256), B("nd16"), cl(GF), oh(0), A.is_equal, A.mult)
    t2(st(SV, 48), st(SV, 48), cl(QF), cl(QF), A.add, A.add)
    for r in range(16):
        def fn(r=r): return g.affine_select(T.LT[:, 128 * r:128 * r + 128], T.BA[:, bABS + 15 - r:bABS + 143 - r], [[1, 128]], A.is_gt, 0.0, 0, -1)
        op("c", fn, [B("BA", bABS, bABS + 144)], [B("LT", 128 * r, 128 * r + 128)], 170.0 + 256 * CYC)
    t2(cl(WE), oh(4), oh(5), 4608.0, A.add, A.mult)
    lin(B("BA", bE, bE + 144), B("BF"), 0.0, cl(WE))
    cp(B("cx"), B("cxi"))
    ts(B("VP", 512, 768), B("cc"), oh(1), A.mult)
    ts(B("VP", 0, 256), B("rr"), oh(0), A.mult)
    ts(B("VP", 256, 512), lane, oh(2), A.mult)
    tt(B("VP", 0, 256), B("VP", 0, 256), B("VP", 512, 768), A.add)
    cp(B("ELu", 256, V), B("ELi", 256, V))
    ts(B("ELf"), B("ELi"), -2048.0, A.add)

    peers = [c for c in T.cores if c != core]
    mask = topo.mask(core, peers[0])
    for c in peers:
        mask &= topo.mask(core, c)
    ne = bin(mask).count("1")
    nsent = [0]
    closer["steps"] = len(ops)

    def send(t, dst, src, sem, parts):
        to = T.cores[(rank + 1 + t % (N - 1)) % N]
        rid, pid, _ = topo.addr(to)

        def fn():
            g.remote_dma(ap(dst), ap(src), T.sem[sem], T.sem.sent, pid, rid, mask)
            return sem, parts * ne
        add("c", "far", fn, [src], [dst], 300.0, FAR + dst["n"] * 5.0, "#c")
        nsent[0] += ne

    def si(t, j, n=1): return B("si", 192 * t + 16 * j, 192 * t + 16 * (j + n))
    def sf(t, j, n=1): return B("sf", 144 * t + 16 * j, 144 * t + 16 * (j + n))
    def sb(t, j): return B("sb", 64 * t + 16 * j, 64 * t + 16 * j + 16)
    def sh(t, j): return B("sh", 48 * t + 16 * j, 48 * t + 16 * j + 16)
    def su(t, j, n=1): return B("su", 128 * t + 16 * j, 128 * t + 16 * (j + n))
    def lo(t): return B("lo", 16 * t, 16 * t + 16)
    iK, iLF, iF, iRS, iRM, iJ, iLS, iLM, iLJ = range(9)
    fY, fC, fU1, fU2, fOZ, fSEL, fA, fB, fE = range(9)
    bNF, bLT, bROW = range(3)
    hN = 0
    uF, uE, uU, uC, uZ, uSEL, uH = range(7)

    def scat(t, X, src):
        o = ind(B(X), lo(t))
        at("put" + X[0], t)
        op("v", lambda: v.tensor_copy(ap(o), ap(src)), [src, blk("lz", t)], [o], cost(o, src))

    def window(t):
        b, p = t % 3, t % 2
        G, D, Z = "G%d" % p, "D%d" % p, "Z%d" % b
        def names(k0, k1): return B("ELu", 256 * b + 16 * k0, 256 * b + 16 * k1)
        def key(a, z): return [(P(0, a, min(z, KL)), a, min(z, KL))] * (a < KL) + [(P(1, max(a, KL), z), max(a, KL), z)] * (z > KL)
        at("", t)
        mm([(P(2, 0, 512), I1, B("NB"))], True, False)
        for o, a, z in key(0, 256):
            mm([(o, I1, B("kc", a, z))], True, False)
        for j, (k0, k1) in enumerate(OC):
            at("own%d" % k0)
            lin(B(G, 256 * k0, 256 * k1), ind(B("Xw", 0, W), names(k0, k1)))
            mm([(P(2, 256 * (r // 8) + 16 * k0, 256 * (r // 8) + 16 * k1), B("BA", bX + 15 - r % 8, bX + 143 - r % 8),
                 B(G, 256 * k0 + r, 256 * k1, 16)) for r in range(16)], False, j == len(OC) - 1)
        if t:
            scat(t - 1, "Mw", blk("lz", t - 1))

        def live():
            ts(B("pr"), P(2, 0, 512), B("col", Q8 + b), A.is_equal)
            mm([(P(3, 0, 256), B("JP", 0, 128), B("pr", 0, 256)), (P(3, 0, 256), B("JP", 128, 256), B("pr", 256, 512))])

        def sign():
            act(B("lv"), P(3, 0, 256), F.Sign)
            for o, a, z in key(0, 256):
                mm([(o, ILV, B("lv", a, z))], acc=(t, a < KL))

        def least():
            lin(B("PS", 0, KL), P(0, 0, KL))
            lin(B("PP%d" % p), ind(B("PS"), B("prm", 18 * b, 18 * b + 17)))
            scan(B("SF"), B("d0f"), B("PP%d" % p), A.add, A.min)

        def stream(what, k0, k1):
            o, a = B("AB", 256 * k0, 256 * k1), B(D, 256 * k0, 256 * k1)
            at(what + "%d" % k0 * (k1 > 0), t)
            if what == "diff":
                tt(a, ind(B("Mw", 0, W), names(k0, k1)), B(Z, 0, 256 * (k1 - k0)), A.subtract)
            elif what in ("relu", "abs"):
                if what == "relu":
                    at("diff%d" % k0)
                    for ko, a0, z0 in key(16 * k0, 16 * k1):
                        mm(r2l(ko, "BA", bDEL, D, 16 * a0, 16 * z0), acc=(t, a0 < KL))
                    at("relu%d" % k0)
                    ts(o, a, 0.0, A.max)
                else:
                    act(o, a, F.Abs)
                for ko, a0, z0 in key(16 * k0, 16 * k1):
                    mm(r2l(ko, "BA", bREL if what == "relu" else bABS, "AB", 16 * a0, 16 * z0), acc=(t, a0 < KL))
            else:
                {"live": live, "sign": sign, "least": least}[what]()

        for what, k0, k1 in STREAM:
            stream(what, k0, k1)
        at("late")
        cp(sf(t, fY), P(1, KL, KL + 16))
        for k in range(KL // 16 + 1, 16):
            tt(sf(t, fY), P(1, 16 * k, 16 * k + 16), sf(t, fY), A.min)
        at("min")
        tt(si(t, iK), B("SF", 16, 272, 17), sf(t, fY), A.min)
        at("keys")
        for j, bias in enumerate((0.0, float(2 ** 27 - 2 ** 25))):
            act(B("PK", 272 * j, 272 * j + 272), B("PP%d" % p), F.Abs, bias)
        for k in range(KL // 16, 16):
            for j, bias in enumerate((0.0, float(2 ** 27 - 2 ** 25))):
                o = B("PK", 272 * j + 16 - k, 272 * j + 272, 17)
                act(dict(o, key=("PK%d_%d" % (j, k), 0, 1, ALLP)), P(1, 16 * k, 16 * k + 16), F.Abs, bias, 1.0, None, [o])

    def choose(t):
        b, p, s = t % 3, t % 2, t % 2
        G, D, Z = "G%d" % p, "D%d" % p, "Z%d" % b
        at("row", t)
        ts(si(t, iLF), si(t, iK), 8191, A.bitwise_and)
        ts(su(t, uF), si(t, iLF), cl(QF), A.add)
        at("chosen")
        lin(B("FW", 512, 768), ind(B(G), su(t, uF)))
        act(blk("sz", t), ind(B(D, 0, W + 256), su(t, uF)), F.Abs)
        lin(B("F2"), B("FW", 512, 768))
        at("")
        for k in range(KL // 16, 16):
            cp(B("PP%d" % p, 16 - k, 272, 17), P(1, 16 * k, 16 * k + 16))
        send(t, blk("lz", t), blk("sz", t), "az%d" % t, 2)
        t2(sb(t, bNF), si(t, iLF), 4096.0, 524288.0, A.is_ge, A.mult)
        t2(si(t, iF), si(t, iLF), 4096.0, 524288.0, A.is_lt, A.mult)
        at("open")
        mm([(P(3, 0, 16), I1, B("NB", 0, 16))], True, False)
        mm([(P(2, 0, 16), IM2K, one16)] + [(P(2, 8 * j, 8 * j + 8), I64TH, B("sb", 64 * t + 16 * bNF + j, 64 * t + 16 * bNF + 16, 2)) for j in range(2)],
           True, False)
        at("name")
        mm(r2l(P(4, 0, 16), "BA", bN, "FW", 512, 768), part=16)
        for j in range(2):
            cp(B("su", 128 * t + 16 * uE + 8 * j, 128 * t + 16 * uE + 8 * j + 8), P(4, j, 16, 2))
        cp(sf(t, fE), P(4, 0, 16))
        at("enclosed")
        lin(B("KG"), ind(B("Kw", 0, W + 256), su(t, uE)))
        at("other")
        mm(r2l(P(3, 0, 16), "BA", bU, "FW", 512, 768), False, True, 16)
        ts(su(t, uU), P(3, 0, 16), B("col", QB + b), A.subtract)
        tt(sb(t, bLT), P(3, 0, 16), st(SV + 16 * b), A.is_lt)
        at("same")
        tt(B("EQ"), ind(B("FW", 512 - 256 * b, 1280 - 256 * b), su(t, uU)), B("F2"), A.is_equal)
        at("smaller")
        mm([(P(3, 0, 16), IM92, one16), (P(3, 0, 16), B("IF"), sf(t, fE)), (P(3, 0, 16), I46, sb(t, bLT))], True, False)
        at("same")
        mm(r2l(P(3, 0, 16), "BA", bE, "EQ", 0, 256), False, True, 16)
        at("drop")
        tt(sf(t, fY), P(3, 0, 16), sf(t, fE), A.max)
        cp(B("so", 16 * t, 16 * t + 16), sf(t, fY))
        send(t, lo(t), B("so", 16 * t, 16 * t + 16), "az%d" % t, 2)
        at("twice")
        mm([(P(0, 0, 256), B("RP", 0, 128), B("KG"))])
        lin(B("CR"), P(0, 0, 256), -2048.0)
        at("enclosed")
        mm(r2l(P(2, 0, 16), "BA", bN, "KG", 0, 256), False, True, 16)
        cp(sf(t, fC), P(2, 0, 16))
        for j in range(2):
            t2(halves(su(t, uC), "su", 128 * t + 16 * uC)[j], P(2, 8 * j, 8 * j + 8), 2048.0, 4096.0, A.add, A.min)
        at("twice")
        tt(B("E2", 256, 384), ind(sf(t, fC), B("cx", 0, 8)), B("CR", 128, 256), A.is_equal)
        tt(B("E2", 0, 256), ind(sf(t, fC), B("cx")), B("CR"), A.is_equal)
        at("merge")
        bias = 0.0 if b == 0 else (oh((6, 3)[s], s) if b == 1 else cl((TW6, TW3)[s]))
        lin(B("XG"), ind(B("Xw"), su(t, uC)), bias, cl((SC0, SC1)[s]), None, halves(su(t, uC), "su", 128 * t + 16 * uC))
        at("both")
        mm([(P(2, 0, 16), B("IF"), sf(t, fC))], True, False)
        mm(r2l(P(2, 8, 16), "BA", bABS, "E2", 256, 384), False, False, 16)
        mm([(P(2, 0, 16), B("LT", 128 * r, 128 * r + 128), B("E2", r, 256, 16)) for r in range(16)], False, True, 16)

    def halves(x, name, a):
        return [dict(B(name, a + j, a + 16, 2), key=("%s%d_%d" % (name, a, j), 0, 1, ALLP)) for j in range(2)]

    def claims(t, hi=7, low=-1):
        s = t % 2
        half = halves(B("cs"), "cs", 0)
        at("claim" if hi == 7 else "", t)
        for j in range(2 * (hi == 7)):
            t2(half[j], P(2, 8 * j, 8 * j + 8), 2048.0, cl(DUM + j), A.add, A.min)
        for c in range(hi, low, -1):
            tt(ind(B("Xw"), B("cs", 2 * c, 2 * c + 2)), B("XG", 32 * c, 32 * c + 32), B("VP", 256 * s + 32 * c, 256 * s + 32 * c + 32), A.add, None, half)

    def rows_of(t):
        b, p = t % 3, t % 2
        G, D, Z = "G%d" % p, "D%d" % p, "Z%d" % b
        at("keys", t)
        at("")
        tt(B("dJ", 0, 272, 17), st(SFB), si(t, iLF), A.subtract)
        at("first")
        scan(B("SJ"), B("PP%d" % p), B("dJ"), A.max, A.min)
        at("others")
        scan(B("SK"), B("d0k"), B("PK"), A.add, A.min, [dict(key=("PK%d_%d" % (j, k), 0, 1, ALLP)) for j in range(2) for k in range(KL // 16, 16)])
        at("")
        tt(si(t, iRS, 2), B("SK", 16, 544, 17), st(SADD, 32), A.add)
        ts(si(t, iJ), B("SJ", 16, 272, 17), -1.0, A.mult)
        ts(si(t, iLS, 3), si(t, iRS, 3), 4095, A.bitwise_and)
        tt(sf(t, fU1, 2), si(t, iF, 2), st(SLIM, 32), A.min)
        tt(sf(t, fOZ), sf(t, fU1), sf(t, fU2), A.max)
        tt(sf(t, fA), si(t, iLM), sb(t, bNF), A.max)
        tt(sf(t, fOZ), sf(t, fOZ), si(t, iLS), A.max)
        tt(sf(t, fB), si(t, iLJ), sb(t, bNF), A.max)
        tt(sf(t, fSEL), sf(t, fA), sf(t, fOZ), A.min)
        tt(sb(t, bROW), sf(t, fB), sf(t, fOZ), A.min)
        ts(su(t, uZ, 2), sf(t, fOZ, 2), cl(QF), A.add)
        thr = B("PS", 256 + 16 * b, 272 + 16 * b)
        tt(thr, thr, sb(t, bNF), A.add)
        at("send")
        lin(blk("se", t), ind(B(G), su(t, uSEL)))
        send(t, blk("le", t), blk("se", t), "ae%d" % t, 1)
        at("minus")
        lin(B(D, W + 256, W + 512), blk(Z, 0), 0.0, -2.0)
        at("stale")
        lin(B("DS"), ind(B(D), su(t, uZ)))

    def state(t):
        b = t % 3
        z = blk("Z%d" % b, 0)
        lst = [(P(7, 0, 256), I1, z), (P(7, 0, 256), IHALF, B("DS")), (P(7, 0, 256), I1, blk("sz", t))]
        at("round", t)
        if ROUND_S:
            mm(lst, part=1)
            lin(B("ZR"), P(7, 0, 256), MAGIC, 1.0 - 2.0 ** -11)
            at("state")
            lin(z, B("ZR"), -MAGIC)
        else:
            mm(lst + [(P(7, 0, 256), IQRT, B("on"))], part=1)
            t2(z, P(7, 0, 256), MAGIC, MAGIC, A.add, A.subtract)
        at("")
        if t + 3 < RO:
            dma("y", [(blk("Z%d" % b, j), z) for j in range(1, REP)])
        else:
            dma("y", [(H(T.yz[:, 256 * b:256 * b + 256], bf), z)])

    def hint(t):
        at("mask", t)
        mm([(P(6, 0, 256), B("RP", 128, 256), blk("se", t))])
        if MASK_S:
            act(B("MA"), P(6, 0, 256), F.Abs, cl(NQ))
            act(blk("MK", t % 2), B("MA"), F.Relu, 1.0, -1.0)
        else:
            ts(blk("MK", t % 2), P(6, 0, 256), cl(QF), A.is_equal)
        at("")
        hop = P(4, 288, 304)
        mm([(hop, I16TH, sb(t, bROW)), (hop, I16TH, B("NB", 0, 16))] + r2l(hop, "BA", bH, "se", 256 * t, 256 * t + 256), part=6)
        cp(su(t, uH), hop)
        mm([(P(6, 256, 512), IM16, B("kc"))] + [(P(6, 256 + 16 * k, 272 + 16 * k), I16, sb(t, bROW)) for k in range(16)], part=6)
        at("cutoff")
        act(B("AR"), P(6, 256, 512), F.Abs, 0.0, 2.0)
        mm([(P(5, 256, 512), I1, B("AR")), (P(5, 256, 512), IM2K, B("on"))], part=1)

    def name(t):
        at("hint", t)
        tt(B("HG"), ind(B("ELf"), su(t, uH)), blk("MK", t % 2), A.mult)
        mm([(P(4, 272, 288), I8K, one16), (P(4, 272, 288), IM64TH, sb(t, bNF))], True, False)
        mm(r2l(P(4, 272, 288), "BA", bONE, "HG", 0, 256), False, True, 4)
        at("")
        for j in range(2):
            tt(halves(sh(t, hN), "sh", 48 * t)[j], P(4, 272 + j, 288, 2), B("sf", 144 * t + 16 * fC + 8 * j, 144 * t + 16 * fC + 8 * j + 8), A.min)

    def cut(t):
        at("cut", t)
        tt(B("Et"), P(5, 256, 512), blk("ELf", t % 3), A.min)

    def put(t):
        b = t % 3
        el = blk("ELf", b)
        at("bounds", t)
        mm([(P(5, 0, 256), IM1, B("AR"))], True, False)
        mm([(P(5, 16 * k, 16 * k + 16), I1, sh(t, hN)) for k in range(16)], False, True, 4, also=halves(sh(t, hN), "sh", 48 * t))
        at("put")
        tt(el, P(5, 0, 256), B("Et"), A.max)
        at("offsets")
        if t + 3 < RO:
            ts(blk("ELu", b), el, 2048.0, A.add)
        else:
            lin(blk("oE", b), el, 2048.0)
            dma("y", [(H(T.ye[:, 256 * b:256 * b + 256], f32), blk("oE", b))])

    def table_out(X, wt, off, bank, buf, y):
        mm([(P(bank, 0, 256), B(wt, off + 15 - j, off + 143 - j), blk(X, j)) for j in range(16)], part=4)
        lin(buf, P(bank, 0, 256))
        dma("y", [(H(y, f32), buf)])

    for t in range(RO):
        window(t)
        if t == RO - 1:
            s = t % 2
            at("")
            table_out("Xw", "BA", (bO, bY)[s], 4, blk("oO", 0), T.yo[8 - 8 * s:16 - 8 * s, :])
        if t:
            scat(t - 1, "Kw", blk("le", t - 1))
            cut(t - 1)
        choose(t)
        if t:
            name(t - 1)
        claims(t)
        rows_of(t)
        if t:
            put(t - 1)
        hint(t)
        state(t)

    t = RO - 1
    at("")
    parts = (((0, I1), (1, I16), (6, I256)), ((2, I1), (3, I1)))[s]
    dma("s", [(blk("cpb", j), piece("Xw", q)) for j, (q, I) in enumerate(parts)])
    scat(t, "Mw", blk("lz", t))
    at("")
    dma("y", [(H(T.ym[:, 0:W // 2], bf), B("Mw", 0, W // 2))])
    dma("s", [(H(T.ym[:, W // 2:W], bf), B("Mw", W // 2, W))], 2 ** 19)
    name(t)
    scat(t, "Kw", blk("le", t))
    cut(t)
    put(t)
    at("")
    table_out("Kw", "BA", bN, 0, B("oK"), T.yk[:, :])
    mm([(P(1, 0, 256), I, blk("cpb", j)) for j, (q, I) in enumerate(parts)])
    cp(blk("oO", 1), P(1, 0, 256))
    dma("y", [(H(T.yo[8 * s:8 + 8 * s, :], f32), blk("oO", 1))])
    tt(B("TL"), B("PS", 256, 304), st(STT, 48), A.subtract)
    ts(B("TL"), B("TL"), 1.0 / 8192, A.mult)
    mm([(dict(P(3, 0, 128), ap=T.P3[0:48, 0:128]), B("TL"), B("IF"))])
    lin(B("oT", 0, 128, 1, th48), dict(P(3, 0, 128), ap=T.P3[0:48, 0:128]))
    dma("y", [(dict(H(T.yt[q, :], f32), n=6), B("oT", 16 * q, 16 * q + 16, 1, th48)) for q in range(8)])
    emit()
    g.wait_ge(T.sem.sent, nsent[0])
